import numpy as np, ml_dtypes
CORES = [2,3,42,43,82,83,122,123]
N = 8
BF = ml_dtypes.bfloat16
def gentries(a):
    return np.ascontiguousarray(a.reshape(8, 16, -1).transpose(0, 2, 1)).reshape(8, -1)
def gtable(e):
    e = np.asarray(e); return np.ascontiguousarray(e.reshape(8, -1, 16).transpose(0, 2, 1)).reshape(128, -1).astype(np.int32)
V, H, PP, RO, S = 2048, 8192, 512, 2, 3
TH = 6
def slot(y, w1, w2):
    u1 = np.sum(y * w1[..., None], axis=-2) & 4095; u2 = np.sum(y * w2[..., None], axis=-2) & 4095
    return (((u1 * u2) >> 5) + u2) & (H - 1)
def keys(y):
    return np.ascontiguousarray((y & 255).astype(np.uint8).T).view("S16").reshape(-1)
def index(y):
    k = keys(y); o = np.argsort(k); return k[o], o
def find(ix, q):
    ks, o = ix; kq = keys(q); pos = np.minimum(np.searchsorted(ks, kq), len(ks) - 1)
    return np.where(ks[pos] == kq, o[pos], -1)
def weights(rng):
    return rng.integers(0, 16, (N, 8, 16)), rng.integers(0, 16, (N, 8, 16))
def themes(rng):
    return rng.integers(-6, 7, (8, TH, 16)) * (rng.random((8, TH, 16)) < 0.6)
def choose(rng, w1, w2, cand, bare=False):
    c = np.concatenate([cand[:, np.all((cand >= 0) & (cand <= 127), axis=0)], rng.integers(0, 128, (16, 2 * H))], axis=1)
    h = slot(c, w1, w2)
    if bare: c, h = c[:, h > 0], h[h > 0]
    i = np.sort(np.unique(h, return_index=True)[1])[:V]
    return c[:, rng.permutation(i)]
def song(rng, w1, w2, D, top=None, first=None, alpha=None, off=None, bare=()):
    if top is None: top = np.full((8, 16, 1), 128)
    if first is None: first = np.zeros((8, 16, 0), np.int64)
    if off is None: off = np.zeros((8, 16, 1), np.int64)
    al = np.full(TH, 3.0) if alpha is None else np.asarray(alpha, float)
    y = np.zeros((N, 8, 16, V), np.int64)
    for g in range(8):
        p = np.append(0.7 * rng.dirichlet(al), 0.3); E = np.ascontiguousarray(D[g].T); M = off.shape[2]
        for k in range(N):
            r = k * S % N; img = np.zeros((16, 0), np.int64)
            if k > 0:
                s = rng.choice(TH + 1, V, p=p); m = np.flatnonzero(s < TH)
                img = y[(r - S) % N, g][:, m] + E[:, s[m]] + off[g][:, rng.integers(0, M, len(m))]
            if k == N - 1:
                s = rng.choice(TH + 1, V, p=p); m = np.flatnonzero(s < TH)
                img = np.concatenate([img, y[0, g][:, m] - E[:, s[m]] + off[g][:, rng.integers(0, M, len(m))]], axis=1)
                img = img[:, rng.permutation(img.shape[1])]
            y[r, g] = choose(rng, w1[r, g], w2[r, g], np.concatenate([first[g], img, rng.integers(0, top[g], (16, V))], axis=1), g in bare)
    return y, [[index(y[r, g]) for g in range(8)] for r in range(N)]
def hits(y, ix, r, g, d):
    b = find(ix[r][g], y[(r - S) % N, g] + d[:, None]); a = np.flatnonzero(b >= 0)
    return a, b[a]
def main(y, ix, D, g):
    return int(np.argmax([sum(len(hits(y, ix, r, g, D[g, k])[0]) for r in range(N)) for k in range(TH)]))
def pick(rng, y, ix, r, g, d, n):
    a, b = hits(y, ix, r, g, d)
    if len(a) == 0: return rng.integers(0, V, (2, n))
    i = rng.integers(0, len(a), n); return np.stack([a[i], b[i]])
def pairs(rng, y, ix, D):
    pr = np.zeros((N, 8, 2, PP), np.int64); n = PP // 16
    for r in range(N):
        for g in range(8):
            o = rng.permutation(TH)
            tail = np.concatenate([pick(rng, y, ix, r, g, D[g, k], n) for k in o[2:]] + [rng.integers(0, V, (2, 4 * n))], axis=1)
            pr[r, g] = np.concatenate([pick(rng, y, ix, r, g, D[g, o[0]], 4 * n), pick(rng, y, ix, r, g, D[g, o[1]], 4 * n), tail[:, rng.permutation(8 * n)]], axis=1)
    return pr
def race(rng, w1, w2, y, ix, g):
    E = rng.integers(-2, 3, (N, 16))
    for k in range(N):
        r = k * S % N; img = np.zeros((16, 0), np.int64)
        if k > 0:
            img = y[(r - S) % N, g][:, rng.permutation(V)] + E[r][:, None]; img = img[:, np.all((img >= 0) & (img <= 127), axis=0)]
            img = img[:, np.sort(np.unique(slot(img, w1[r, g], w2[r, g]), return_index=True)[1])[:V // 4 + int(r == N - 1)]]
        y[r, g] = choose(rng, w1[r, g], w2[r, g], img); ix[r][g] = index(y[r, g])
    return E
def pack(y, w1, w2, pr):
    return {"x": np.ascontiguousarray(y.reshape(N, 128, V)).astype(np.int32), "w1": w1.reshape(N, 128, 1).astype(np.int32), "w2": w2.reshape(N, 128, 1).astype(np.int32),
            "pa": np.stack([gtable(a[:, 0]) for a in pr]), "pb": np.stack([gtable(a[:, 1]) for a in pr])}
def setup_inputs(rng):
    w1, w2 = weights(rng); D = themes(rng); y, ix = song(rng, w1, w2, D); pr = pairs(rng, y, ix, D)
    g, h = rng.permutation(8)[:2]; m = main(y, ix, D, g)
    for r in range(N): pr[r, g] = pick(rng, y, ix, r, g, D[g, m], PP)
    q = int(rng.integers(0, N)); pr[q, h] = pick(rng, y, ix, q, h, D[h, main(y, ix, D, h)], PP)
    return pack(y, w1, w2, pr)
def setup_inputs_ties(rng):
    w1, w2 = weights(rng); D = themes(rng); y, ix = song(rng, w1, w2, D); E = race(rng, w1, w2, y, ix, 6); pr = pairs(rng, y, ix, D)
    one = np.repeat(np.array([[V - 1], [0]]), PP, axis=1)
    for g in range(8):
        m = main(y, ix, D, g)
        for r in range(N):
            if g % 4 == 0 or (g % 4 == 3 and r == 0): pr[r, g] = one
            elif g % 4 != 2: pr[r, g] = pick(rng, y, ix, r, g, D[g, m], PP)
    pr[0, 6] = rng.integers(0, V, (2, PP))
    for r in range(1, N): pr[r, 6] = pick(rng, y, ix, r, 6, E[r], PP)
    return pack(y, w1, w2, pr)
def setup_inputs_near(rng):
    w1, w2 = weights(rng); D = themes(rng); off = np.zeros((8, 16, 10), np.int64); c = np.arange(8) % 4
    for g in range(8):
        i, j, z = 2 * g, 2 * g + 1, min(2 * g, 12)
        w1[:, g, z:z + 4] = 0; w2[:, g, z:z + 4] = 0
        off[g, i, 4] = 1; off[g, j, 5] = -1; off[g, i, 6] = 1; off[g, j, 6] = -1; off[g, j, 7] = 2
        off[g, z:z + 4, 8] = np.array([1, -3, 3, -1]); off[g, z:z + 4, 9] = np.array([-1, 3, -3, 1])
    D[:, 0] = -(1 + c)[:, None]; D[4, 0] = 1
    first = np.tile(np.stack([c, 1 + c, 127 + 0 * c], axis=1)[:, None, :], (1, 16, 1))
    y, ix = song(rng, w1, w2, D, first=first, alpha=[9, 3, 3, 3, 3, 3], off=off, bare=(2, 6)); pr = pairs(rng, y, ix, D)
    for g in range(8):
        for r in range(N):
            if g % 2 == 0 or r == 0: pr[r, g, :, :PP // 2] = pick(rng, y, ix, r, g, D[g, 0], PP // 2)
    return pack(y, w1, w2, pr)
def setup_inputs_same(rng):
    w1, w2 = weights(rng); D = themes(rng); D[::2, 0] = 0; D[1, 0] = 0; D[:, 2] = -D[:, 1]
    w1[:, 1] = w1[0, 1].copy(); w2[:, 1] = w2[0, 1].copy()
    first = [rng.integers(0, 128, (16, 64)) for g in range(8)]; first[1] = choose(rng, w1[0, 1], w2[0, 1], first[1])[:, :7 * V // 8]
    y, ix = song(rng, w1, w2, D, first=first, alpha=[6, 3, 3, 3, 3, 3]); pr = pairs(rng, y, ix, D)
    for g in (0, 1, 2, 4, 6):
        for r in range(0, N, 2): pr[r, g, :, :PP // 4] = pick(rng, y, ix, r, g, D[g, 0], PP // 4)
    return pack(y, w1, w2, pr)
def setup_inputs_late(rng):
    w1, w2 = weights(rng); D = themes(rng); y, ix = song(rng, w1, w2, D); pr = np.zeros((N, 8, 2, PP), np.int64)
    for g in range(8):
        m = main(y, ix, D, g); dead = np.zeros((N, V), bool)
        for r in range(N):
            a, b = hits(y, ix, r, g, D[g, m]); dead[(r - S) % N, a] = True; dead[r, b] = True
        for r in range(N):
            c = (r - S) % N; fa = np.flatnonzero(~dead[c]); fb = np.flatnonzero(~dead[r])
            if len(fa) == 0: fa = np.array([0])
            if len(fb) == 0: fb = np.array([0])
            q = pick(rng, y, ix, r, g, D[g, m], PP - 1)
            if g % 2 == 1:
                z = rng.random(PP - 1) < 0.5; late = np.arange(PP - 1) > 0
                q = np.stack([np.where(z & late, rng.choice(fa, PP - 1), q[0]), np.where(~z & late, rng.choice(fb, PP - 1), q[1])])
            ca, cb = hits(y, ix, r, g, D[g, (m + 1 + (r + g) % (TH - 1)) % TH]); ok = ~dead[c, ca] & ~dead[r, cb]; ca, cb = ca[ok], cb[ok]
            if len(ca) == 0: ca, cb = fa[:1], fb[:1]
            j = int(rng.integers(0, len(ca)))
            pr[r, g] = np.concatenate([q, np.array([[ca[j]], [cb[j]]])], axis=1)
    return pack(y, w1, w2, pr)
def setup_inputs_spread(rng):
    ws = np.array([0, 1, 2, 7, 15]); w1 = rng.choice(ws, (N, 8, 16)); w2 = rng.choice(ws, (N, 8, 16))
    top = 2 ** rng.integers(1, 8, (8, 16, 1)); top[:, ::5] = 128
    D = rng.integers(-1, 2, (8, TH, 16)) * 2 ** rng.integers(0, 6, (8, TH, 16)) * (rng.random((8, TH, 16)) < 0.5)
    D = np.where(top.reshape(8, 1, 16) < 128, np.abs(D), D)
    e = int(rng.integers(0, 8)); top[e, 1] = 1; D[e, :, 1] = 0; D[e, 0] = 0; D[e, 0, 1] = 127; D[e, 1, 1] = -127
    y, ix = song(rng, w1, w2, D, top=top); pr = pairs(rng, y, ix, D)
    for r in range(N): pr[r, e, :, :PP // 2] = pick(rng, y, ix, r, e, D[e, 0], PP // 2)
    return pack(y, w1, w2, pr)
def check_inputs(d):
    bad = []
    for k, hi in (("x", 127), ("w1", 15), ("w2", 15), ("pa", V - 1), ("pb", V - 1)):
        if np.min(d[k]) < 0 or np.max(d[k]) > hi: bad.append("range of " + k)
    h = np.sort(slot(d["x"].astype(np.int64).reshape(N, 8, 16, V), d["w1"].astype(np.int64).reshape(N, 8, 16), d["w2"].astype(np.int64).reshape(N, 8, 16)), axis=-1)
    if np.any(h[..., 1:] == h[..., :-1]): bad.append("two notes of a rank and group have one slot number")
    return bad
def reference(x, w1, w2, pa, pb):
    y = x.astype(np.int64).reshape(N, 8, 16, V)
    la = np.stack([gentries(a) for a in pa]).astype(np.int64); lb = np.stack([gentries(a) for a in pb]).astype(np.int64)
    ix = [[index(y[r, g]) for g in range(8)] for r in range(N)]
    cov = np.zeros((N, 8, V), np.int64); win = np.zeros((8, 2 * RO), np.int64)
    for t in range(RO):
        new = cov + 0
        for g in range(8):
            best, top, won = -1, -1, []
            for d in range(N):
                c = (d - S) % N
                free = np.flatnonzero((cov[c, g][la[d, g]] == 0) & (cov[d, g][lb[d, g]] == 0))
                if len(free) == 0: continue
                k = int(free[0]); D = y[d, g][:, lb[d, g, k]] - y[c, g][:, la[d, g, k]]
                fit = []
                for r in range(N):
                    e = (r - S) % N; b = find(ix[r][g], y[e, g] + D[:, None])
                    p = np.flatnonzero((b >= 0) & (cov[e, g] == 0) & (cov[r, g][np.maximum(b, 0)] == 0))
                    fit.append((p, b[p]))
                n = sum(len(p) for p, b in fit)
                if n > top: best, top, won = d, n, fit
            win[g, t] = best; win[g, RO + t] = top
            for r in range(len(won)):
                p, b = won[r]; new[(r - S) % N, g, p] = t + 1; new[r, g, b] = t + 1
        cov = new
    return {"yc": cov.astype(np.float32), "yw": np.stack([win] * N).astype(np.float32)}

@@ -1,0 +1,722 @@
+from concourse.bass import DstId, RemoteDMATransfer
+from concourse.mybir import AluOpType, AxisListType, ActivationFunctionType
+
+N, SH, NV, NP = 8, 3, 2048, 512
+TW = 12288
+BIG = float(2 ** 26)
+VFILL = 4096
+S1, S2 = 36, 24
+QOFF = 137
+SQ7 = 2
+
+
+def _sb(n, dt):
+    return ("sbuf", [128, n], dt)
+
+
+B16, F32, I32, U16, F16 = "bfloat16", "float32", "int32", "uint16", "float16"
+SCRATCH = {
+    "tab": _sb(TW, B16), "xi": _sb(NV, I32), "xb": _sb(NV, B16), "xp": _sb(NV, B16), "xs": _sb(NV, B16),
+    "ga": _sb(8 * NV, B16), "ne": _sb(12 * 512, B16), "xpk": _sb(1536, F32), "dbc": _sb(1024, B16),
+    "nn": _sb(2048, B16), "u1": _sb(1024, F32), "mm": _sb(1024, I32), "kk": _sb(1024, I32), "hh": _sb(1024, F32),
+    "lst": _sb(1024, U16), "in1": _sb(NV, B16), "xsd": _sb(1024, B16), "ner": _sb(1024, B16), "fit": _sb(1024, B16),
+    "ew": _sb(36, I32), "pbi": _sb(32, I32), "es": _sb(2, F32), "el": _sb(4, U16), "wf": _sb(4, F32),
+    "pcol": _sb(1, I32), "ci": _sb(12, I32), "cf": _sb(12, F32), "ct": _sb(28, F32), "i3": _sb(1, I32),
+    "nrow": _sb(352, B16), "rv1": _sb(128, B16), "rv2": _sb(128, B16), "krow": _sb(512, F32),
+    "zone": _sb(144, B16), "zw": _sb(6 * 144, B16), "zp": _sb(256, B16), "zq": _sb(256, B16),
+    "ya": _sb(144, B16), "y1": _sb(144, B16), "ys": _sb(144, B16), "yr": _sb(144, B16), "ysel": _sb(288, B16),
+    "xm": _sb(512, B16), "idh": _sb(128, F16), "idq": _sb(128, B16), "nw": _sb(256, B16), "b8": _sb(128, F16),
+    "b1k": _sb(128, B16), "ones": _sb(128, B16), "onef": _sb(128, F32), "crow": _sb(512, B16), "oh": _sb(24, F32),
+    "s12": _sb(256, I32), "u12": _sb(256, I32), "m1": _sb(128, I32), "k1": _sb(128, I32), "h1": _sb(128, F32),
+    "own": _sb(128, U16), "rl": _sb(128, U16), "l0": _sb(4, U16), "lb": _sb(2, U16), "ao": _sb(256, F16),
+    "ah": _sb(256, F16), "aso": _sb(256, F32), "asi": _sb(256, F32), "la1": _sb(8 * S1, F32), "la2": _sb(8 * S2, F32),
+    "cl1": _sb(64, F16), "cl2": _sb(64, F16), "cnt": _sb(4, F32), "base": _sb(16, F16),
+    "w_1": _sb(56, F32), "w_2": _sb(56, F32), "wo": _sb(32, F32), "km": _sb(8, I32), "wl": _sb(4, U16),
+    "mf1": _sb(128, B16), "mf2": _sb(128, B16), "mr1": _sb(128, B16), "mr2": _sb(128, B16),
+    "fi1": _sb(128, B16), "fi2": _sb(128, B16), "ri1": _sb(128, B16), "ri2": _sb(128, B16), "rj1": _sb(128, B16),
+    "cov": _sb(128, B16), "pt": _sb(128, I32), "pl": _sb(192, U16),
+    "xbk": _sb(512, B16), "dall": _sb(512, B16), "em": _sb(1024, B16), "gm": _sb(1536, B16),
+    "kf": _sb(4, F32), "kl": _sb(2, U16), "c1": _sb(128, F32), "lim": _sb(128, F32), "ta": _sb(128, F32),
+    "tb": _sb(128, F32), "yo": _sb(128, F32), "ywo": _sb(4, F32),
+}
+BANKS = ("p0", "p1", "p2", "p3", "r0", "r1", "m0", "mb")
+for _n in BANKS:
+    SCRATCH[_n] = ("psum", [128, 512], F32)
+SEMAPHORES = ["qv", "qs", "qp", "qg", "sent", "dx0", "dx1", "dx2", "dx3", "dw", "dpb", "dy", "dz",
+              "ael", "aes", "al1", "aah", "axp", "axs", "aas", "ac1", "af1", "ar1", "aj1", "al2", "ac2", "af2", "ar2"]
+
+OP = AluOpType
+ACT = ActivationFunctionType
+AX = AxisListType.X
+
+
+def _count(mask):
+    return bin(mask).count("1")
+
+
+def rank_program(g, core, T, topo):
+    rank = T.rank_of(core)
+    if rank is None:
+        return
+    cores = list(T.cores)
+    pred = (rank - SH) % N
+    Q = {"v": g.vector, "s": g.scalar, "p": g.tensor, "g": g, "y": g.sync}
+    cnt = {}
+    waited = {}
+    lastw, reads = {}, {}
+
+    def need(q, toks):
+        best = {}
+        for s, v in toks:
+            best[s] = max(best.get(s, 0), v)
+        for s, v in best.items():
+            if waited.get((q, s), 0) < v:
+                Q[q].wait_ge(T.sem[s], v)
+                waited[(q, s)] = v
+
+    def deps(q, r, w):
+        toks = []
+        for x in r:
+            if x in lastw:
+                toks.append(lastw[x])
+            if x in BANKS:
+                toks += [t for t in reads.get(x, []) if t[0] != "q" + q]
+        for x in w:
+            if x in lastw:
+                toks.append(lastw[x])
+            toks += reads.get(x, [])
+        if q == "p":
+            toks = [t for t in toks if t[0] != "qp"]
+        need(q, toks)
+
+    def done(tok, r, w):
+        for x in r:
+            reads.setdefault(x, []).append(tok)
+        for x in w:
+            lastw[x] = tok
+            reads[x] = []
+
+    def run(q, r, w, fn):
+        deps(q, r, w)
+        s = "q" + q
+        cnt[s] = cnt.get(s, 0) + 1
+        fn().then_inc(T.sem[s], 1)
+        done((s, cnt[s]), r, w)
+
+    def ts(r, w, out, in0, a, op0, b=None, op1=None):
+        if op1 is None:
+            run("v", r, w, lambda: g.vector.tensor_scalar(out, in0, a, None, op0))
+        else:
+            run("v", r, w, lambda: g.vector.tensor_scalar(out, in0, a, b, op0, op1))
+
+    def tt(r, w, out, in0, in1, op):
+        run("v", r, w, lambda: g.vector.tensor_tensor(out, in0, in1, op))
+
+    def cp(r, w, out, in_):
+        run("v", r, w, lambda: g.vector.tensor_copy(out, in_))
+
+    def fill(w, out, c):
+        run("v", [], w, lambda: g.vector.memset(out, c))
+
+    def red(r, w, out, in_, op):
+        run("v", r, w, lambda: g.vector.tensor_reduce(out, in_, AX, op))
+
+    def act(r, w, out, in_, func=None, bias=0.0, scale=1.0, accum=None):
+        f = ACT.Identity if func is None else func
+        run("s", r, w, lambda: g.scalar.activation(out, in_, f, bias=bias, scale=scale, accum_out=accum))
+
+    def mm(r, bank, out, lhsT, rhs, start, stop):
+        run("p", r, [bank], lambda: g.tensor.matmul(out, lhsT, rhs, start, stop))
+
+    def iota(w, out, pattern, base, mult, small=True):
+        if small:
+            run("g", [], w, lambda: g.iota(out, pattern, base, mult, allow_small_or_imprecise_dtypes=True))
+        else:
+            run("g", [], w, lambda: g.iota(out, pattern, base, mult))
+
+    def dma(q, sem, r, w, out, in_):
+        deps(q, r, w)
+        cnt[sem] = cnt.get(sem, 0) + 16
+        Q[q].dma_start(out, in_).then_inc(T.sem[sem], 16)
+        done((sem, cnt[sem]), r, w)
+
+    def plan(src_rank, dst_ranks):
+        c = cores[src_rank]
+        far = [d for d in dst_ranks if topo.chip(cores[d]) != topo.chip(c)]
+        near = [d for d in dst_ranks if topo.chip(cores[d]) == topo.chip(c)]
+        out, used = [], 0
+        if far:
+            m = topo.mask(c, cores[far[0]])
+            for d in far[1:]:
+                m &= topo.mask(c, cores[d])
+            out.append((m, far))
+            used = m
+        if near:
+            es = [e for e in topo.engines(c, cores[near[0]]) if not used >> e & 1]
+            out.append((sum(1 << e for e in es[0:3:2]), near))
+        return out
+
+    def dst_id(d):
+        rid, pid, _ = topo.addr(cores[d])
+        return DstId(rid=rid, pnc=pid)
+
+    def gather_all(r, sem, src, landing):
+        deps("g", r, [])
+        trs = []
+        for m, ds in plan(rank, [(rank + j) % N for j in range(1, N)]):
+            trs.append(RemoteDMATransfer(dst_ids=[dst_id(d) for d in ds], dma_engine_mask=m, remote_sem=T.sem[sem],
+                                         srcs=[src], dsts=[src for d in ds]))
+            cnt["sent"] = cnt.get("sent", 0) + _count(m)
+        g.remote_dma_fused(trs, local_sem=T.sem.sent)
+        total = 0
+        for s in range(N):
+            if s != rank:
+                total += sum(_count(m) for m, ds in plan(s, [(s + j) % N for j in range(1, N)]) if rank in ds)
+        cnt[sem] = total
+        lastw[landing] = (sem, total)
+
+    def shift(r, items):
+        deps("g", r, [])
+
+        def masks(s):
+            m = None
+            for it in items:
+                k = topo.mask(cores[s], cores[(s + it[1]) % N])
+                m = k if m is None else m & k
+            es = [e for e in topo.engines(cores[s], cores[(s + items[0][1]) % N]) if m >> e & 1]
+            per = len(es) // len(items)
+            return [sum(1 << e for e in es[j * per:(j + 1) * per]) for j in range(len(items))]
+        mine = masks(rank)
+        if len(items) == 1:
+            src, off, land, sem = items[0]
+            rid, pid, _ = topo.addr(cores[(rank + off) % N])
+            g.remote_dma(T[land][:], src, T.sem[sem], T.sem.sent, pid, rid, mine[0])
+        else:
+            g.remote_dma_fused([RemoteDMATransfer(dst_ids=[dst_id((rank + it[1]) % N)], dma_engine_mask=m,
+                                                  remote_sem=T.sem[it[3]], src=it[0], dst=T[it[2]][:])
+                                for it, m in zip(items, mine)], local_sem=T.sem.sent)
+        for j, it in enumerate(items):
+            cnt["sent"] = cnt.get("sent", 0) + _count(mine[j])
+            cnt[it[3]] = _count(masks((rank - it[1]) % N)[j])
+            lastw[it[2]] = (it[3], cnt[it[3]])
+
+    TAB = ["tab%d" % j for j in range(TW // 2048)]
+    XB = ["xb%d" % j for j in range(4)]
+    DBC = ["dbc%d" % d for d in range(8)]
+
+    dma("s", "dw", [], ["ew"], T.ew[:, 0:1], T.w1[:])
+    dma("y", "dw", [], ["ew1"], T.ew[:, 1:2], T.w2[:])
+    dma("s", "dw", [], ["ew2"], T.ew[:, 2:34], T.pa[:])
+    lastw["ew"] = lastw["ew2"]
+    dma("y", "dx0", [], ["xi0"], T.xi[:, 0:512], T.x[:, 0:512])
+    dma("s", "dpb", [], ["pbi"], T.pbi[:], T.pb[:])
+    for j in range(1, 4):
+        dma("y", "dx%d" % j, [], ["xi%d" % j], T.xi[:, 512 * j:512 * j + 512], T.x[:, 512 * j:512 * j + 512])
+
+    iota(["pcol"], T.pcol[:], [[0, 1]], 0, 1, small=False)
+    iota(["nrow"], T.nrow[:], [[1, 352]], -96, 0)
+    iota(["rv1"], T.rv1[:], [[1, 8], [0, 16]], 0, 0)
+    iota(["rv2"], T.rv2[:], [[16, 8], [0, 4], [1, 4]], 0, 0)
+    fill(["tab0"], T.tab[:, 0:2048], BIG)
+    for j in range(VFILL // 2048, TW // 2048):
+        act(["tab0"], [TAB[j]], T.tab[:, 2048 * j:2048 * j + 2048], T.tab[:, 0:2048])
+
+    def cf(j):
+        return T.cf[:, j:j + 1]
+
+    def ct(j):
+        return T.ct[:, j:j + 1]
+
+    def wf(j):
+        return T.wf[:, j:j + 1]
+
+    def cast(j):
+        cp(["xi%d" % j], [XB[j]], T.xb[:, 512 * j:512 * j + 512], T.xi[:, 512 * j:512 * j + 512])
+
+    AND, SHR = OP.bitwise_and, OP.arith_shift_right
+    EQ, MUL, ADD, SUB, GE = OP.is_equal, OP.mult, OP.add, OP.subtract, OP.is_ge
+    bit = [(0x70, AND, None), (15, AND, None), (4, SHR, None), (7, AND, None), (3, SHR, None), (3, AND, None),
+           (2, SHR, 3), (6, SHR, None), (3, SHR, 7), (127, AND, None)]
+    for j, (a, op, b) in enumerate(bit):
+        ts(["pcol"], ["ci%d" % j], T.ci[:, j:j + 1], T.pcol[:], a, op, b, None if b is None else AND)
+    fill(["ones"], T.ones[:], 1.0)
+    cp(["ci%d" % j for j in range(10)], ["cf"], T.cf[:, 0:10], T.ci[:, 0:10])
+    fill(["crow"], T.crow[0:1, :], 4096.0 * QOFF)
+    ts(["nrow", "cf"], ["zone"], T.zone[:], T.nrow[:, 81:225], cf(0), EQ)
+    o1 = S1 * rank
+    cp(["ew"], ["wf0"], T.wf[:, 0:2], T.ew[:, 0:2])
+    cp(["ew"], ["l0"], T.l0[:], T.ew[:, 2:6])
+    shift(["wf0", "l0"], [(T.wf[:, 0:2], -SH, "es", "aes"), (T.l0[:], -SH, "el", "ael")])
+    cp(["ew"], ["la1w"], T.la1[:, o1:o1 + 2], T.ew[:, 0:2])
+    for j in range(2):
+        ts(["zone", "wf0"], ["zw%d" % j], T.zw[:, 144 * j:144 * j + 144], T.zone[:], wf(j), MUL)
+    ts(["wf0"], ["wf2"], T.wf[:, 2:4], T.wf[:, 0:2], -1.0, MUL)
+    for j in range(1, VFILL // 2048):
+        fill([TAB[j]], T.tab[:, 2048 * j:2048 * j + 2048], BIG)
+    cast(0)
+    cp(["pbi"], ["lb"], T.lb[:], T.pbi[:, 0:2])
+    for j in range(2):
+        ts(["rv1", "cf", "wf2"], ["nw%d" % j], T.nw[:, 128 * j:128 * j + 128], T.rv1[:], cf(2), EQ, wf(2 + j), MUL)
+    ts(["nrow", "cf"], ["idh"], T.idh[:], T.nrow[:, 96:224], cf(9), EQ)
+    ts(["nrow", "cf"], ["idq"], T.idq[:], T.nrow[:, 96:224], cf(9), EQ, -4096.0, MUL)
+    cast(1)
+
+    def sums(bank, z0, halves):
+        for h in halves:
+            a, b = (0, NV) if h is None else (1024 * h, 1024 * h + 1024)
+            rd = XB[a // 512:b // 512]
+            for j in range(2):
+                for r in range(16):
+                    o = 144 * (z0 + j) + 15 - r
+                    mm(rd + ["zw%d" % (z0 + j)], bank, T[bank][:, 128 * j + a // 16:128 * j + b // 16], T.zw[:, o:o + 128],
+                       T.xb[:, a + r:b:16], a == 0 and j == 0 and r == 0, b == NV and j == 1 and r == 15)
+
+    sums("m0", 0, [0])
+    ts(["cf"], ["i3"], T.i3[:], cf(1), -1.0, ADD, 1.0 / 3.0, MUL)
+    ts(["cf"], ["ct0"], ct(0), cf(4), 6.0, GE)
+    ts(["cf"], ["ct1"], ct(1), cf(8), 2.0, GE, 2.0, ADD)
+    ts(["i3", "cf"], ["ct2"], ct(2), T.i3[:], 8.0, MUL, cf(2), ADD)
+    ts(["i3", "cf"], ["ct3"], ct(3), T.i3[:], -3.0, MUL, cf(1), ADD)
+    ts(["cf", "ct0"], ["ct4"], ct(4), cf(4), 12.0, GE, ct(0), ADD)
+    ts(["cf", "ct1"], ["ct5"], ct(5), cf(7), 4.0, MUL, ct(1), ADD)
+    cast(2)
+    ts(["ct3"], ["ct6"], ct(6), ct(3), 1.0, GE, 255.0, MUL)
+    ts(["ct3"], ["ct7"], ct(7), ct(3), 2.0, GE, 65280.0, MUL)
+    ts(["cf", "ct4"], ["ct8"], ct(8), cf(3), 16.0, MUL, ct(4), ADD)
+    ts(["cf", "ct5"], ["ct9"], ct(9), cf(3), 16.0, MUL, ct(5), ADD)
+    ts(["ct6", "ct7"], ["ct10"], ct(10), ct(6), ct(7), ADD, 1.0, ADD)
+    cast(3)
+    sums("m0", 0, [1])
+    ts(["cf", "ct10"], ["ct11"], ct(11), cf(1), 12.0, GE, ct(10), MUL)
+    ts(["nrow", "ct8"], ["ya"], T.ya[:], T.nrow[:, 84:228], ct(8), EQ)
+    ts(["nrow", "ct9"], ["y1"], T.y1[:], T.nrow[:, 88:232], ct(9), EQ)
+    ts(["nrow", "ct2", "ct10"], ["zp"], T.zp[:], T.nrow[:, 0:256], ct(2), EQ, ct(10), MUL)
+    ts(["nrow", "ct2", "ct11"], ["zq"], T.zq[:], T.nrow[:, 0:256], ct(2), EQ, ct(11), MUL)
+
+    def slots(out, outname, between=()):
+        rest = list(between) + [lambda: None] * 5
+        ts(["s12a", "s12b"], ["u12"], T.u12[:], T.s12[:], 4095, AND)
+        rest[0]()
+        tt(["u12"], ["m1"], T.m1[:], T.u12[:, 0:128], T.u12[:, 128:256], MUL)
+        rest[1]()
+        ts(["m1"], ["k1"], T.k1[:], T.m1[:], 5, SHR, 8191, AND)
+        rest[2]()
+        tt(["k1", "u12"], ["h1"], T.h1[:], T.k1[:], T.u12[:, 128:256], ADD)
+        rest[3]()
+        cp(["h1"], [outname], out, T.h1[:])
+
+    def put(j):
+        cp(["own", XB[j]], TAB, T.tab[:].indirect(T.own[:, 32 * j:32 * j + 32]), T.xb[:, 512 * j:512 * j + 512])
+
+    cp(["m0"], ["s12a", "s12b"], T.s12[:], T.m0[:, 0:256])
+    slots(T.own[:], "own")
+    put(0)
+    put(1)
+    act(XB + ["lb"], ["la1a"], T.la1[:, o1 + 2:o1 + 18], T.xb[:].indirect(T.lb[:, 0:1]), scale=-1.0)
+    act(XB + ["el"], ["la1b"], T.la1[:, o1 + 18:o1 + 34], T.xb[:].indirect(T.el[:, 0:1]))
+    gather_all(["la1a", "la1b", "la1w"], "al1", T.la1[:, o1:o1 + 19], "la1")
+    for j in (2, 3):
+        act(["zone", "es"], ["zw%d" % j], T.zw[:, 144 * j:144 * j + 144], T.zone[:], scale=T.es[:, j - 2:j - 1])
+    sums("mb", 2, [None])
+    ts(["mb"], ["s12a", "s12b"], T.s12[:], T.mb[:, 0:256], 2048.0, ADD)
+    ts(["s12a", "s12b"], ["u12"], T.u12[:], T.s12[:], 4095, AND)
+    ts(["u12"], ["ao"], T.ao[:], T.u12[:], -2048.0, ADD)
+    shift(["ao"], [(T.ao[:], SH, "ah", "aah")])
+    shift(XB, [(T.xb[:], SH, "xp", "axp")])
+    iota(["krow"], T.krow[0:1, :], [[1, 512]], 0, 0)
+    put(2)
+    put(3)
+
+    def late_sums():
+        for j in (4, 5):
+            c = S1 * pred + j - 4
+            act(["zone", "la1"], ["zw%d" % j], T.zw[:, 144 * j:144 * j + 144], T.zone[:], scale=T.la1[:, c:c + 1])
+
+    def late_sends():
+        sums("r0", 4, [None])
+        act(["r0"], ["aso"], T.aso[:], T.r0[:, 0:256])
+        shift(["aso"], [(T.aso[:], -SH, "asi", "aas")])
+        shift(XB, [(T.xb[:], -SH, "xs", "axs")])
+
+    def lists_front(t):
+        side = ("r0", "r1", "mb", "m0")
+
+        def apart(bank, b, start, stop):
+            o = 128 * (b // 2)
+            for dd in range(4):
+                mm(["ah", "idh"], bank, T[bank][:, 128 * dd:128 * dd + 128], T.idh[:], T.ah[:, o:o + 128],
+                   start and dd == 0, stop and dd == 3)
+
+        def const(b):
+            bank = "p%d" % b
+            mm(["ones", "crow"], bank, T[bank][:], T.ones[0:1, :], T.crow[0:1, :], True, False)
+
+        def bpart(bank, b, start, stop):
+            j, h = b // 2, b % 2
+            mm(["nw%d" % j] + DBC[4 * h:4 * h + 4], bank, T[bank][:],
+               T.nw[:, 128 * j:128 * j + 128], T.dbc[:, 512 * h:512 * h + 512], start, stop)
+
+        def spread(d):
+            out = T.dbc[:, 128 * d:128 * d + 128]
+            if t == 1:
+                a, b = S1 * ((d - SH) % N) + 18, S1 * d + 2
+                act(["la1", "la1a", "la1b", "ones"], [DBC[d]], out, T.ones[:],
+                    scale=T.la1[:, a:a + 1], bias=T.la1[:, b:b + 1])
+            else:
+                a = S2 * d + 4
+                act(["la2", "la2a", "ones"], [DBC[d]], out, T.ones[:], scale=T.la2[:, a:a + 1])
+
+        def rem(b):
+            act([side[b]], ["nn%d" % b], T.nn[:, 512 * b:512 * b + 512], T[side[b]][:],
+                bias=QOFF + 0.5 / 4096 - 0.5, scale=1.0 / 4096)
+
+        def sub(b):
+            bank = "p%d" % b
+            mm(["nn%d" % b, "idq"], bank, T[bank][:], T.idq[:], T.nn[:, 512 * b:512 * b + 512], False, True)
+
+        def out1(h):
+            act(["p%d" % h], ["u1%d" % h], T.u1[:, 512 * h:512 * h + 512], T["p%d" % h][:], bias=4096.0 * QOFF)
+
+        const(2)
+        const(3)
+        if t == 1:
+            for d in range(8):
+                spread(d)
+            late_sums()
+            for b in (0, 2, 1, 3):
+                bpart(side[b], b, True, False)
+                bpart("p%d" % b, b, b < 2, False)
+            for h in range(2):
+                apart(side[h], h, False, True); rem(h)
+                apart(side[2 + h], 2 + h, False, True); rem(2 + h)
+                apart("p%d" % h, h, False, False); sub(h); out1(h)
+                apart("p%d" % (2 + h), 2 + h, False, False); sub(2 + h)
+        else:
+            for b in (0, 2, 1, 3):
+                apart(side[b], b, True, False)
+                apart("p%d" % b, b, b < 2, False)
+            for h in range(2):
+                for d in range(4 * h, 4 * h + 4):
+                    spread(d)
+                bpart(side[h], h, False, True); bpart(side[2 + h], 2 + h, False, True)
+                bpart("p%d" % h, h, False, False); bpart("p%d" % (2 + h), 2 + h, False, False)
+                rem(h); rem(2 + h); sub(h); sub(2 + h); out1(h)
+        for j in range(2):
+            mm(["nw%d" % j] + DBC, "m0", T.m0[:, 8 * j:8 * j + 8],
+               T.nw[:, 128 * j:128 * j + 128], T.dbc[:, 0::128], j == 0, j == 1)
+
+    def lists_back(parts):
+        for step in range(4):
+            for (a, b) in parts:
+                h = a // 512
+                bank = "p%d" % (2 + h)
+                u2 = T[bank][:, a - 512 * h:b - 512 * h]
+                if step == 0:
+                    tt(["u1%d" % h, bank], ["mm%d" % a], T.mm[:, a:b], T.u1[:, a:b], u2, MUL)
+                elif step == 1:
+                    ts(["mm%d" % a], ["kk%d" % a], T.kk[:, a:b], T.mm[:, a:b], 5, SHR, 8191, AND)
+                elif step == 2:
+                    tt(["kk%d" % a, bank], ["hh%d" % a], T.hh[:, a:b], T.kk[:, a:b], u2, ADD)
+                else:
+                    cp(["hh%d" % a], ["lst%d" % d for d in range(a // 128, b // 128)], T.lst[:, a:b], T.hh[:, a:b])
+
+    def look(q, d, q0, q1):
+        out = T.ga[:, NV * d + 512 * q0:NV * d + 512 * q1]
+        src = T.tab[:].indirect(T.lst[:, 128 * d + 32 * q0:128 * d + 32 * q1])
+        nd = T.dbc[:, 128 * d:128 * d + 1]
+        r, w = TAB + ["lst%d" % d, DBC[d]], ["ga%d_%d" % (d, k) for k in range(q0, q1)]
+        if q == "s":
+            act(r, w, out, src, bias=nd)
+        else:
+            ts(r, w, out, src, nd, ADD)
+
+    def packa(bank, src, name, order=(0, 1, 2), start=True, stop=True):
+        for n, k in enumerate(order):
+            o = 96 - 8 * (6 * k)
+            mm([name(k), "zp"], bank, T[bank][:], T.zp[:, o:o + 128], src(k), start and n == 0, stop and n == len(order) - 1)
+
+    def packb(bank, src, name, odd, first):
+        o = 96 - 8 * (4 if odd else -4)
+        mm([name(2), "zq"], bank, T[bank][:], T.zq[:, o:o + 128], src(2), first, False)
+        o = 96 - 8 * (10 if odd else 2)
+        mm([name(3), "zp"], bank, T[bank][:], T.zp[:, o:o + 128], src(3), False, not first)
+
+    def gsrc(d):
+        return lambda k: T.ga[:, NV * d + 512 * k:NV * d + 512 * k + 512]
+
+    def gname(d):
+        return lambda k: "ga%d_%d" % (d, k)
+
+    def main(t):
+        W = T["w_%d" % t]
+        nei = [0]
+        started = {}
+
+        def pa_(d, bank, order=(0, 1, 2), start=True, stop=True):
+            packa(bank, gsrc(d), gname(d), order, start, stop)
+
+        def pb_(d, bank, first):
+            packb(bank, gsrc(d), gname(d), d % 2 == 1, first)
+
+        def cmp_(bank, kind):
+            j = nei[0]
+            nei[0] += 1
+            tt([bank, "xpk%d" % kind], ["ne%d" % j], T.ne[:, 512 * j:512 * j + 512], T[bank][:],
+               T.xpk[:, 512 * kind:512 * kind + 512], OP.not_equal)
+            return j
+
+        def sum_(j, d, kind, last=False):
+            rb = "r%d" % (d // 4)
+            first = rb not in started
+            started[rb] = True
+            if kind == 0:
+                o = 12 - 4 * (d % 4)
+                mm(["ne%d" % j, "ya"], rb, T[rb][:], T.ya[:, o:o + 128], T.ne[:, 512 * j:512 * j + 512], first, last)
+            else:
+                o = 8 - 4 * (d % 4)
+                mm(["ne%d" % j, "y1"], rb, T[rb][:], T.y1[:, o:o + 128], T.ne[:, 512 * j:512 * j + 512], first, last)
+
+        def count(tau):
+            c = 2 * (t - 1) + tau
+            act(["r%d" % tau], ["fit%d" % tau, "cnt%d" % c], T.fit[:, 512 * tau:512 * tau + 512], T["r%d" % tau][:],
+                ACT.Relu, bias=1.0, scale=-1.0, accum=T.cnt[:, c:c + 1])
+
+        def halves(q, d):
+            look(q, d, 0, 2)
+            look(q, d, 2, 4)
+
+        def front(d, bank):
+            pa_(d, bank, (0, 1), True, False)
+
+        def back(d, bank):
+            pa_(d, bank, (2,), False, True)
+
+        if t == 2:
+            for rb in ("r0", "r1"):
+                started[rb] = True
+                for s in range(4):
+                    for m in ("mf1", "rj1"):
+                        mm([m, "xm"], rb, T[rb][:, 128 * s:128 * s + 128], T.xm[:, 128 * s:128 * s + 128], T[m][:],
+                           s == 0 and m == "mf1", False)
+        lists_back([(0, 128), (128, 256)])
+        halves("s", 0)
+        lists_back([(384, 512), (256, 384)])
+        cp(["m0"], ["wb%d" % t], W[:, 8:24], T.m0[:, 0:16])
+        if t == 1:
+            xs_ = lambda k: T.xp[:, 512 * k:512 * k + 512]
+            xn_ = lambda k: "xp"
+            late_sends()
+            packa("m0", xs_, xn_)
+            packb("mb", xs_, xn_, False, True)
+            packb("mb", xs_, xn_, True, False)
+        halves("s", 1)
+        halves("s", 2)
+        halves("v", 3)
+        front(0, "p0"); front(3, "p2"); back(0, "p0"); pb_(0, "p1", True); back(3, "p2")
+        if t == 1:
+            cp(["mb"], ["xpk1"], T.xpk[:, 512:1024], T.mb[:])
+            cp(["m0"], ["xpk0"], T.xpk[:, 0:512], T.m0[:])
+        lists_back([(512, 768), (768, 1024)])
+        halves("s", 4)
+        halves("s", 6)
+        pb_(3, "mb", True)
+        pb_(1, "p1", False); pa_(1, "p3")
+        a, c, b, e = cmp_("p0", 0), cmp_("p2", 0), cmp_("p1", 1), cmp_("p3", 0)
+        sum_(a, 0, 0); sum_(c, 3, 0)
+        front(2, "m0")
+        sum_(b, 0, 1); sum_(e, 1, 0)
+        back(2, "m0"); pb_(2, "mb", False)
+        halves("v", 5)
+        front(5, "p0"); front(4, "p2"); back(5, "p0"); pb_(5, "p1", True)
+        a, b = cmp_("m0", 0), cmp_("mb", 1)
+        sum_(a, 2, 0)
+        back(4, "p2")
+        sum_(b, 2, 1, True)
+        pb_(4, "p1", False)
+        count(0)
+        for k in range(SQ7):
+            look("s", 7, k, k + 1)
+        c = cmp_("p0", 0)
+        sum_(c, 5, 0)
+        look("v", 7, SQ7, 4)
+        prep(t)
+        front(6, "p3")
+        pb_(7, "m0", True)
+        pa_(7, "mb", tuple(range(SQ7, 3)), True, False)
+        a, b = cmp_("p2", 0), cmp_("p1", 1)
+        sum_(a, 4, 0)
+        back(6, "p3")
+        pb_(6, "m0", False)
+        sum_(b, 4, 1)
+        a, b = cmp_("p3", 0), cmp_("m0", 1)
+        sum_(a, 6, 0)
+        pa_(7, "mb", tuple(range(SQ7 - 1)), False, False)
+        sum_(b, 6, 1)
+        pa_(7, "mb", (SQ7 - 1,), False, True)
+        cl = T["cl%d" % t]
+        o = 8 * rank
+        ts(["wv%da" % t, "cnt%d" % (2 * t - 2)], ["cla%d" % t], cl[:, o:o + 4], W[:, 24:28], T.cnt[:, 2 * t - 2:2 * t - 1], MUL)
+        a = cmp_("mb", 0)
+        sum_(a, 7, 0, True)
+        count(1)
+        ts(["wv%d" % t, "cnt%d" % (2 * t - 1)], ["clb%d" % t], cl[:, o + 4:o + 8], W[:, 36:40], T.cnt[:, 2 * t - 1:2 * t], MUL)
+        gather_all(["cla%d" % t, "clb%d" % t], "ac%d" % t, cl[:, o:o + 8], "cl%d" % t)
+
+    def prep(t):
+        W = T["w_%d" % t]
+        wv = "wv%d" % t
+        if t == 1:
+            ts(["nrow", "cf"], ["wv1a"], W[:, 24:28], T.nrow[:, 96:100], cf(6), EQ)
+            ts(["nrow", "cf"], [wv], W[:, 36:40], T.nrow[:, 96:100], cf(6), EQ)
+        else:
+            lr = ["la2", "la2b"]
+            tt(lr + ["wv1a"], ["wv2a"], W[:, 24:28], T.w_1[:, 24:28], T.la2[:, 3:4 * S2:S2], MUL)
+            tt(lr + ["wv1a"], [wv], W[:, 36:40], T.w_1[:, 24:28], T.la2[:, 4 * S2 + 3::S2], MUL)
+
+    def prep2(t):
+        W = T["w_%d" % t]
+        bs = T.base[:, 8 * t - 8:8 * t]
+        if t == 1:
+            ts(["rv1", "cf"], ["b8"], T.b8[:], T.rv1[:], cf(2), EQ, 8.0, MUL)
+            ts(["nrow"], ["base1"], bs, T.nrow[:, 96:104], -15.0, ADD, -1.0 / 128, MUL)
+            fill(["wz1"], W[:, 28:36], 0.0)
+            fill(["wy1"], W[:, 40:48], 1.0)
+            cp(["nrow"], ["wd1"], W[:, 48:56], T.nrow[:, 96:104])
+        else:
+            val = T.la2[:, 3::S2]
+            lr = ["la2", "la2b"]
+            ts(lr, ["b2a"], T.ta[:, 0:8], val, -1.0, ADD, 8.0 / 128, MUL)
+            tt(lr + ["nrow"], ["wd2a"], T.ct[:, 20:28], val, T.nrow[:, 97:105], MUL)
+            fill(["wz2"], W[:, 28:36], 0.0)
+            tt(["b2a", "base1"], ["base2"], bs, T.ta[:, 0:8], T.base[:, 0:8], ADD)
+            ts(lr, ["wy2"], W[:, 40:48], val, 2.0, MUL)
+            ts(["wd2a"], ["wd2"], W[:, 48:56], T.ct[:, 20:28], -1.0, ADD)
+        cp(DBC, ["wn%d" % t], W[:, 0:8], T.dbc[:, 0::128])
+        mm(["b8", "base%d" % t], "m0", T.m0[:, 0:8], T.b8[:], bs, True, False)
+
+    def idle1():
+        packa("p1", lambda k: T.xs[:, 512 * k:512 * k + 512], lambda k: "xs", (0, 1))
+        act(["p1"], ["xpk2"], T.xpk[:, 1024:1536], T.p1[:], scale=-1.0)
+        ts(["cf"], ["ct12"], ct(12), cf(1), 6.0, OP.min, 8.0, MUL)
+        ts(["cf"], ["ct13"], ct(13), cf(5), 4.0, MUL, cf(0), ADD)
+        ts(["ct4", "ct8"], ["ct16"], ct(16), ct(4), 3.0, MUL, ct(8), ADD)
+        cp(["ew"], ["pl0"], T.pl[:, 0:32], T.ew[:, 2:34])
+        cp(["pbi"], ["pl1"], T.pl[:, 32:64], T.pbi[:])
+        ts(["ct12"], ["ct14"], ct(14), ct(12), 7.0, ADD)
+        ts(["nrow", "ct13"], ["ys"], T.ys[:], T.nrow[:, 93:237], ct(13), EQ)
+        ts(["nrow", "ct16"], ["yr"], T.yr[:], T.nrow[:, 93:237], ct(16), EQ)
+        act(XB + ["pl1"], ["xbk"], T.xbk[:], T.xb[:].indirect(T.pl[:, 32:64]))
+        ts(["ew"], ["pt0"], T.pt[:, 0:32], T.ew[:, 2:34], 127, AND)
+        ts(["pbi"], ["pt1"], T.pt[:, 32:64], T.pbi[:], 127, AND)
+        ts(["ew"], ["pt2"], T.pt[:, 64:96], T.ew[:, 2:34], 7, SHR)
+        ts(["pbi"], ["pt3"], T.pt[:, 96:128], T.pbi[:], 7, SHR)
+        ts(["rv1", "cf"], ["b1k"], T.b1k[:], T.rv1[:], cf(2), EQ, 1024.0, MUL)
+        cp(["pt0", "pt1", "pt2", "pt3"], ["pl2"], T.pl[:, 64:192], T.pt[:])
+        fill(["onef"], T.onef[0:1, :], 1.0)
+        ts(["nrow", "pl2", "cf"], ["em"], T.em[:], T.nrow[:, 96:112].indirect(T.pl[:, 128:192]), cf(1), EQ)
+
+    def blocked(j, src, side):
+        tt([src, "pl2", "em"], ["gm%d" % j], T.gm[:, 512 * j:512 * j + 512],
+           T[src][:].indirect(T.pl[:, 64 + 32 * side:96 + 32 * side]), T.em[:, 512 * side:512 * side + 512], MUL)
+        mm(["b1k", "gm%d" % j], "m0", T.m0[:], T.b1k[:], T.gm[:, 512 * j:512 * j + 512], False, j == 2)
+
+    def idle2():
+        mm(["onef", "krow"], "m0", T.m0[:], T.onef[0:1, :], T.krow[0:1, :], True, False)
+        ts(["cf"], ["ct15"], ct(15), cf(0), cf(6), ADD)
+        ts(["nrow", "cf"], ["ohs"], T.oh[:, 4:8], T.nrow[:, 96:100], cf(5), EQ)
+        ts(["nrow", "cf"], ["ohb"], T.oh[:, 8:24], T.nrow[:, 96:112], cf(1), EQ, BIG, MUL)
+        tt(["xp", "pl0", "xbk"], ["dall"], T.dall[:], T.xp[:].indirect(T.pl[:, 0:32]), T.xbk[:], SUB)
+        blocked(0, "mf1", 0)
+        for s in range(4):
+            ts(["rv2", "ct15", "ohs"], ["xm%d" % s], T.xm[:, 128 * s:128 * s + 128], T.rv2[:], ct(15), EQ, T.oh[:, 4 + s:5 + s], MUL)
+        lastw["xm"] = lastw["xm3"]
+
+    def choose(t):
+        W, cl = T["w_%d" % t], T["cl%d" % t]
+        wo = 16 * (t - 1)
+        ko = 4 * (t - 1)
+        for r in range(N):
+            mm(["b8", "cl%d" % t, "cla%d" % t, "clb%d" % t], "m0", T.m0[:, 0:8], T.b8[:], cl[:, 8 * r:8 * r + 8], False, r == N - 1)
+        red(["m0"], ["km%d" % t], T.km[:, ko:ko + 1], T.m0[:, 0:8], OP.max)
+        ts(["km%d" % t], ["kn%d" % t], T.km[:, ko + 1:ko + 2], T.km[:, ko:ko + 1], 7, AND)
+        ts(["kn%d" % t, "ct14"], ["wl%d" % t], T.wl[:, 2 * t - 2:2 * t - 1], T.km[:, ko + 1:ko + 2], -1.0, MUL, ct(14), ADD)
+        cp(["wl%d" % t, "wv%da" % t] + [x % t for x in ("wb%d", "wn%d", "wv%d", "wz%d", "wy%d", "wd%d")], ["wo%d" % t],
+           T.wo[:, wo:wo + 16], W[:].indirect(T.wl[:, 2 * t - 2:2 * t - 1]))
+        w = "wo%d" % t
+
+        def col(j):
+            return T.wo[:, wo + j:wo + j + 1]
+        ts(["asi", w], ["s12a"], T.s12[:, 0:128], T.asi[:, 0:128], col(1), SUB, 32768.0, ADD)
+        ts(["asi", w], ["s12b"], T.s12[:, 128:256], T.asi[:, 128:256], col(2), SUB, 32768.0, ADD)
+        mf, mr = "mf%d" % t, "mr%d" % t
+
+        def sel(tau):
+            ts(["ys", w], ["ysel%d" % tau], T.ysel[:, 144 * tau:144 * tau + 144], T.ys[:], col(3 + tau), MUL)
+        slots(T.rl[:], "rl", [lambda: sel(0), lambda: sel(1)])
+        for tau in range(2):
+            for s in range(4):
+                o = 144 * tau + 3 - s
+                mm(["ysel%d" % tau, "fit%d" % tau], "mb", T.mb[:, 0:128], T.ysel[:, o:o + 128],
+                   T.fit[:, 512 * tau + 128 * s:512 * tau + 128 * s + 128], tau == 0 and s == 0, tau == 1 and s == 3)
+        for j in range(2):
+            act(["xs", w], ["xsd%d" % j], T.xsd[:, 512 * j:512 * j + 512], T.xs[:, 1024 + 512 * j:1536 + 512 * j], bias=col(0))
+        act(["mb"], [mf], T[mf][:], T.mb[:, 0:128], scale=float(t))
+        shift([mf], [(T[mf][:], -SH, "fi%d" % t, "af%d" % t)])
+        for j in range(2):
+            act(TAB + ["rl", w], ["ga0_%d" % j], T.ga[:, 512 * j:512 * j + 512],
+                T.tab[:].indirect(T.rl[:, 32 * j:32 * j + 32]), bias=col(0), scale=-1.0)
+            tt(TAB + ["rl", "xsd%d" % j], ["ner%d" % j], T.ner[:, 512 * j:512 * j + 512],
+               T.tab[:].indirect(T.rl[:, 64 + 32 * j:96 + 32 * j]), T.xsd[:, 512 * j:512 * j + 512], OP.not_equal)
+            packa("p0", gsrc(0), gname(0), (j,), j == 0, j == 1)
+            for c in range(8 + 4 * j, 12 + 4 * j):
+                mm(["zone", "ner%d" % j], "r0", T.r0[:, 0:128], T.zone[:, 15 - c:143 - c],
+                   T.ner[:, 128 * (c - 8):128 * (c - 7)], c == 8, False)
+        tt(["p0", "xpk2"], ["ne0"], T.ne[:, 0:512], T.p0[:], T.xpk[:, 1024:1536], OP.not_equal)
+        for s in range(4):
+            mm(["yr", "ne0"], "r0", T.r0[:, 0:128], T.yr[:, 3 - s:131 - s], T.ne[:, 128 * s:128 * s + 128], False, s == 3)
+        act(["r0", w], [mr], T[mr][:], T.r0[:, 0:128], ACT.Relu, bias=col(5), scale=-float(t))
+        if t == 1:
+            shift([mr], [(T[mr][:], SH, "ri1", "ar1"), (T[mr][:], 2 * SH, "rj1", "aj1")])
+        else:
+            shift([mr], [(T[mr][:], SH, "ri2", "ar2")])
+        ts(["km%d" % t], ["ko%d" % t], T.km[:, ko + 2:ko + 3], T.km[:, ko:ko + 1], 3, SHR)
+        cp([w], ["yw%d" % t], T.ywo[:, t - 1:t], col(6))
+        ts(["ko%d" % t], ["yx%d" % t], T.ywo[:, 1 + t:2 + t], T.km[:, ko + 2:ko + 3], -1.0, ADD)
+
+    lists_front(1)
+    main(1)
+    prep2(1)
+    idle1()
+    choose(1)
+    idle2()
+
+    tt(["fi1", "ri1"], ["cov"], T.cov[:], T.fi1[:], T.ri1[:], ADD)
+    for c in range(16):
+        act(["cov", "ohb"], ["in1_%d" % c], T.in1[:, 128 * c:128 * c + 128], T.cov[:], scale=T.oh[:, 8 + c:9 + c])
+    blocked(1, "rj1", 0)
+    blocked(2, "cov", 1)
+    red(["m0"], ["kf"], T.kf[:, 0:1], T.m0[:], OP.min)
+    o2 = S2 * rank
+    ts(["kf"], ["kl"], T.kl[:, 0:1], T.kf[:, 0:1], 511.0, OP.min)
+    ts(["kf"], ["la2b"], T.la2[:, o2 + 3:o2 + 4], T.kf[:, 0:1], 512.0, OP.is_lt)
+    cp(["dall", "kl"], ["la2a"], T.la2[:, o2 + 4:o2 + 20], T.dall[:].indirect(T.kl[:, 0:1]))
+    gather_all(["la2a", "la2b"], "al2", T.la2[:, o2 + 3:o2 + 5], "la2")
+    for j in range(4):
+        tt(["own", XB[j]] + ["in1_%d" % c for c in range(4 * j, 4 * j + 4)], TAB,
+           T.tab[:].indirect(T.own[:, 32 * j:32 * j + 32]), T.xb[:, 512 * j:512 * j + 512], T.in1[:, 512 * j:512 * j + 512], ADD)
+
+    lists_front(2)
+    main(2)
+    prep2(2)
+    ts(["cov"], ["c1"], T.c1[:], T.cov[:], 1.0, OP.min)
+    ts(["c1"], ["lim"], T.lim[:], T.c1[:], -1.0, MUL, 2.0, ADD)
+    choose(2)
+    dma("y", "dz", ["yw1", "yw2", "yx1", "yx2"], [], T.yw[:], T.ywo[0:128:16, :])
+    tt(["fi2", "lim"], ["ta", "b2a"], T.ta[:], T.fi2[:], T.lim[:], OP.min)
+    tt(["ta", "c1"], ["ta2"], T.yo[:], T.ta[:], T.c1[:], OP.max)
+    tt(["ri2", "lim"], ["tb"], T.tb[:], T.ri2[:], T.lim[:], OP.min)
+    tt(["ta2", "tb"], ["yo"], T.yo[:], T.yo[:], T.tb[:], OP.max)
+    dma("y", "dy", ["yo"], [], T.yc[:], T.yo[:])
+    for s, v in cnt.items():
+        if max([x for (q, n), x in waited.items() if n == s] + [0]) < v:
+            need("y", [(s, v)])

@@ -4,10 +4,50 @@ from concourse.mybir import AluOpType, AxisListType, ActivationFunctionType
 N, SH, NV, NP = 8, 3, 2048, 512
 TW = 12288
 BIG = float(2 ** 26)
-VFILL = 4096
-S1, S2 = 36, 24
+EMPTY = 2 ** 23
+S1, S2 = 32, 24
 QOFF = 137
-SQ7 = 2
+
+SCALAR = "g00 g10 c00 g20 c10 c40 g30 c20 c50 g01 c30 g11 c01 g21 c11 n4 n0 g70 c21 n5 n1 c31 c70 n6 n2 n3 n7".split()
+VECTOR = "L g40 g50 g60 g41 c60 g51 c41 g61 c51 g31 c61 g71 c71".split()
+COST = {"g": 1.4, "c": 0.33, "n": 0.13, "L": 2.6, "m": 0.22, "w": 0.22, "s": 0.38}
+LAG, YIELD = 0.1, 0.3
+
+
+def timetable():
+    end, order, free = {}, [], {"S": 0.0, "V": 0.0, "P": 0.0}
+    left = {"S": list(SCALAR), "V": list(VECTOR)}
+    guess = {}
+    for q in left:
+        t = 0.0
+        for x in left[q]:
+            guess[x] = t
+            t += COST[x[0]]
+    turns = sorted((x[1:] for x in guess if x[0] == "c"), key=lambda x: guess["c" + x])
+    sums = sorted("01234567", key=lambda d: max(guess["c" + d + "0"], guess["c" + d + "1"]))
+    left["P"] = ["m" + x for x in turns] + ["w" + x for x in turns] + ["s" + d for d in sums]
+
+    def after(x):
+        k, y = x[0], x[1:]
+        if k == "g":
+            return [] if y[0] in "01" else ["L"]
+        if k == "m":
+            return ["c" + turns[turns.index(y) - 4]] if turns.index(y) >= 4 else []
+        if k == "s":
+            return ["c" + y + "0", "c" + y + "1"] + (["n" + sums[sums.index(y) - 4]] if sums.index(y) >= 4 else [])
+        return {"w": ["g" + y, "m" + y], "c": ["w" + y], "n": ["s" + y], "L": []}[k]
+    while any(left.values()):
+        ready = []
+        for q in left:
+            for x in (left[q] if q == "P" else left[q][:1]):
+                if all(y in end for y in after(x)):
+                    at = max([free[q]] + [end[y] + (0.0 if q == "P" and y[0] == "m" else LAG) for y in after(x)])
+                    ready.append((at + (YIELD if x[0] == "s" else 0.0), at, q, x))
+        _, at, q, x = min(ready)
+        left[q].remove(x)
+        free[q] = end[x] = at + COST[x[0]]
+        order.append((q, x))
+    return order, turns, sums
 
 
 def _sb(n, dt):
@@ -16,34 +56,35 @@ def _sb(n, dt):
 
 B16, F32, I32, U16, F16 = "bfloat16", "float32", "int32", "uint16", "float16"
 SCRATCH = {
-    "tab": _sb(TW, B16), "xi": _sb(NV, I32), "xb": _sb(NV, B16), "xp": _sb(NV, B16), "xs": _sb(NV, B16),
-    "ga": _sb(8 * NV, B16), "ne": _sb(12 * 512, B16), "xpk": _sb(1536, F32), "dbc": _sb(1024, B16),
+    "tab": _sb(TW, B16), "xi": _sb(NV, I32), "xb": _sb(NV, B16), "ga": _sb(8 * NV, B16), "ne": _sb(8 * 768, B16),
+    "xp": _sb(NV, B16), "xs": _sb(NV, B16), "dbc": _sb(1024, B16), "zone": _sb(144, B16), "zw": _sb(288, B16),
+    "npk": _sb(48, B16), "na": _sb(256, B16), "rr": _sb(256, B16), "ff": _sb(256, B16),
     "nn": _sb(2048, B16), "u1": _sb(1024, F32), "mm": _sb(1024, I32), "kk": _sb(1024, I32), "hh": _sb(1024, F32),
-    "lst": _sb(1024, U16), "in1": _sb(NV, B16), "xsd": _sb(1024, B16), "ner": _sb(1024, B16), "fit": _sb(1024, B16),
-    "ew": _sb(36, I32), "pbi": _sb(32, I32), "es": _sb(2, F32), "el": _sb(4, U16), "wf": _sb(4, F32),
-    "pcol": _sb(1, I32), "ci": _sb(12, I32), "cf": _sb(12, F32), "ct": _sb(28, F32), "i3": _sb(1, I32),
-    "nrow": _sb(352, B16), "rv1": _sb(128, B16), "rv2": _sb(128, B16), "krow": _sb(512, F32),
-    "zone": _sb(144, B16), "zw": _sb(6 * 144, B16), "zp": _sb(256, B16), "zq": _sb(256, B16),
-    "ya": _sb(144, B16), "y1": _sb(144, B16), "ys": _sb(144, B16), "yr": _sb(144, B16), "ysel": _sb(288, B16),
-    "xm": _sb(512, B16), "idh": _sb(128, F16), "idq": _sb(128, B16), "nw": _sb(256, B16), "b8": _sb(128, F16),
-    "b1k": _sb(128, B16), "ones": _sb(128, B16), "onef": _sb(128, F32), "crow": _sb(512, B16), "oh": _sb(24, F32),
+    "lst": _sb(1024, U16), "in1": _sb(NV, B16), "fit": _sb(1024, B16),
+    "ew": _sb(36, I32), "pbi": _sb(32, I32), "es": _sb(2, F32), "ep": _sb(2, F32), "el": _sb(4, U16), "l0": _sb(4, U16),
+    "wf": _sb(4, F32), "pcol": _sb(1, I32), "pf": _sb(1, F32), "ci": _sb(4, I32), "cf": _sb(4, F32), "ct": _sb(28, F32),
+    "i3": _sb(1, I32), "nrow": _sb(144, B16), "rv1": _sb(128, B16), "krow": _sb(512, F32), "gs": _sb(8, B16),
+    "wm": _sb(32, B16), "pk": _sb(48, B16), "idh": _sb(128, F16), "idq": _sb(128, B16), "idb": _sb(128, B16),
+    "idf": _sb(128, F32), "nw": _sb(256, B16), "b8": _sb(128, B16), "bm": _sb(128, B16), "b1k": _sb(128, B16),
+    "ones": _sb(128, B16), "onef": _sb(128, F32), "crow": _sb(256, B16), "oh": _sb(16, F32), "c8": _sb(8, F32),
     "s12": _sb(256, I32), "u12": _sb(256, I32), "m1": _sb(128, I32), "k1": _sb(128, I32), "h1": _sb(128, F32),
-    "own": _sb(128, U16), "rl": _sb(128, U16), "l0": _sb(4, U16), "lb": _sb(2, U16), "ao": _sb(256, F16),
+    "own": _sb(128, U16), "rl": _sb(128, U16), "la": _sb(32, U16), "lb": _sb(32, U16), "ao": _sb(256, F16),
     "ah": _sb(256, F16), "aso": _sb(256, F32), "asi": _sb(256, F32), "la1": _sb(8 * S1, F32), "la2": _sb(8 * S2, F32),
-    "cl1": _sb(64, F16), "cl2": _sb(64, F16), "cnt": _sb(4, F32), "base": _sb(16, F16),
-    "w_1": _sb(56, F32), "w_2": _sb(56, F32), "wo": _sb(32, F32), "km": _sb(8, I32), "wl": _sb(4, U16),
-    "mf1": _sb(128, B16), "mf2": _sb(128, B16), "mr1": _sb(128, B16), "mr2": _sb(128, B16),
-    "fi1": _sb(128, B16), "fi2": _sb(128, B16), "ri1": _sb(128, B16), "ri2": _sb(128, B16), "rj1": _sb(128, B16),
-    "cov": _sb(128, B16), "pt": _sb(128, I32), "pl": _sb(192, U16),
-    "xbk": _sb(512, B16), "dall": _sb(512, B16), "em": _sb(1024, B16), "gm": _sb(1536, B16),
-    "kf": _sb(4, F32), "kl": _sb(2, U16), "c1": _sb(128, F32), "lim": _sb(128, F32), "ta": _sb(128, F32),
-    "tb": _sb(128, F32), "yo": _sb(128, F32), "ywo": _sb(4, F32),
+    "cl1": _sb(64, B16), "cl2": _sb(64, B16), "cnt": _sb(16, F32), "base": _sb(16, B16),
+    "w_1": _sb(40, F32), "w_2": _sb(40, F32), "wo": _sb(32, F32), "km": _sb(8, I32), "wl": _sb(4, U16),
+    "fl": _sb(16, U16), "mf2": _sb(128, B16), "mr1": _sb(128, B16), "mr2": _sb(128, B16), "fi2": _sb(128, B16),
+    "ri2": _sb(128, B16), "cov": _sb(128, B16), "cs1": _sb(128, B16), "pt": _sb(128, I32), "pl": _sb(128, U16),
+    "pai": _sb(512, B16), "dall": _sb(512, B16), "em": _sb(1024, B16), "gm": _sb(2048, B16),
+    "kf": _sb(4, F32), "kl": _sb(2, U16), "c1": _sb(128, F32), "ta": _sb(128, F32), "yo": _sb(128, F32), "ywo": _sb(4, F32),
 }
-BANKS = ("p0", "p1", "p2", "p3", "r0", "r1", "m0", "mb")
+WB = ("q0", "q1", "q2", "q3")
+PB = ("p0", "p1", "p2", "p3")
+BANKS = WB + PB
 for _n in BANKS:
     SCRATCH[_n] = ("psum", [128, 512], F32)
-SEMAPHORES = ["qv", "qs", "qp", "qg", "sent", "dx0", "dx1", "dx2", "dx3", "dw", "dpb", "dy", "dz",
-              "ael", "aes", "al1", "aah", "axp", "axs", "aas", "ac1", "af1", "ar1", "aj1", "al2", "ac2", "af2", "ar2"]
+SEMAPHORES = ["qv", "qs", "qp", "qg", "sent", "dx0", "dx1", "dx2", "dx3", "dw", "dpb", "dy", "dz", "dy2",
+              "hx0", "hx1", "has", "aes", "ael", "aep", "al1", "aah", "axp0", "axp1", "axs", "aas", "ac1", "af1", "ar1",
+              "aj1", "acs", "al2", "ac2", "af2", "ar2"]
 
 OP = AluOpType
 ACT = ActivationFunctionType
@@ -54,12 +95,43 @@ def _count(mask):
     return bin(mask).count("1")
 
 
+def _helper(r, cores, topo):
+    c = cores[r]
+    near = [cores[(r + k) % N] for k in (SH, -SH)]
+    free = [h for h in topo.cores_of(c) if h not in cores and topo.die(h) != topo.die(c)
+            and all(topo.may_write(h, d) for d in near)]
+    return free[[x for x in cores if topo.chip(x) == topo.chip(c)].index(c)]
+
+
+def _inner(r, cores, topo):
+    return topo.mask(cores[r], _helper(r, cores, topo)) & ~topo.mask(cores[r], cores[(r + SH) % N])
+
+
+def _handed(T):
+    return [("hx1", T.xb[:, 1024:2048], SH, T.xp[:, 1024:2048], "xp1", "axp1"),
+            ("has", T.aso[:], -SH, T.asi[:], "asi", "aas"),
+            ("hx0", T.xb[:], -SH, T.xs[:], "xs", "axs")]
+
+
+def helper_program(g, core, r, T, topo):
+    cores, sent = list(T.cores), 0
+    for sem, src, off, dst, _, there in _handed(T):
+        to = cores[(r + off) % N]
+        rid, pid, _ = topo.addr(to)
+        g.wait_ge(T.sem[sem], _count(_inner(r, cores, topo)))
+        g.remote_dma(dst, src, T.sem[there], T.sem.sent, pid, rid, topo.mask(core, to))
+        sent += _count(topo.mask(core, to))
+    g.wait_ge(T.sem.sent, sent)
+
+
 def rank_program(g, core, T, topo):
     rank = T.rank_of(core)
-    if rank is None:
-        return
     cores = list(T.cores)
-    pred = (rank - SH) % N
+    if rank is None:
+        for r in range(N):
+            if _helper(r, cores, topo) == core:
+                helper_program(g, core, r, T, topo)
+        return
     Q = {"v": g.vector, "s": g.scalar, "p": g.tensor, "g": g, "y": g.sync}
     cnt = {}
     waited = {}
@@ -188,38 +260,38 @@ def rank_program(g, core, T, topo):
             return [sum(1 << e for e in es[j * per:(j + 1) * per]) for j in range(len(items))]
         mine = masks(rank)
         if len(items) == 1:
-            src, off, land, sem = items[0]
+            src, off, dst, land, sem = items[0]
             rid, pid, _ = topo.addr(cores[(rank + off) % N])
-            g.remote_dma(T[land][:], src, T.sem[sem], T.sem.sent, pid, rid, mine[0])
+            g.remote_dma(dst, src, T.sem[sem], T.sem.sent, pid, rid, mine[0])
         else:
             g.remote_dma_fused([RemoteDMATransfer(dst_ids=[dst_id((rank + it[1]) % N)], dma_engine_mask=m,
-                                                  remote_sem=T.sem[it[3]], src=it[0], dst=T[it[2]][:])
+                                                  remote_sem=T.sem[it[4]], src=it[0], dst=it[2])
                                 for it, m in zip(items, mine)], local_sem=T.sem.sent)
         for j, it in enumerate(items):
             cnt["sent"] = cnt.get("sent", 0) + _count(mine[j])
-            cnt[it[3]] = _count(masks((rank - it[1]) % N)[j])
-            lastw[it[2]] = (it[3], cnt[it[3]])
+            cnt[it[4]] = _count(masks((rank - it[1]) % N)[j])
+            lastw[it[3]] = (it[4], cnt[it[4]])
+
+    def send(name, off, land, sem):
+        shift([name], [(T[name][:], off, T[land][:], land, sem)])
+
+    def hand(r, src, sem):
+        deps("g", r, [])
+        rid, pid, _ = topo.addr(_helper(rank, cores, topo))
+        g.remote_dma(src, src, T.sem[sem], T.sem.sent, pid, rid, _inner(rank, cores, topo))
+        cnt["sent"] = cnt.get("sent", 0) + _count(_inner(rank, cores, topo))
+
+    for _, _, off, _, land, sem in _handed(T):
+        cnt[sem] = _count(topo.mask(_helper((rank - off) % N, cores, topo), core))
+        lastw[land] = (sem, cnt[sem])
 
     TAB = ["tab%d" % j for j in range(TW // 2048)]
     XB = ["xb%d" % j for j in range(4)]
     DBC = ["dbc%d" % d for d in range(8)]
-
-    dma("s", "dw", [], ["ew"], T.ew[:, 0:1], T.w1[:])
-    dma("y", "dw", [], ["ew1"], T.ew[:, 1:2], T.w2[:])
-    dma("s", "dw", [], ["ew2"], T.ew[:, 2:34], T.pa[:])
-    lastw["ew"] = lastw["ew2"]
-    dma("y", "dx0", [], ["xi0"], T.xi[:, 0:512], T.x[:, 0:512])
-    dma("s", "dpb", [], ["pbi"], T.pbi[:], T.pb[:])
-    for j in range(1, 4):
-        dma("y", "dx%d" % j, [], ["xi%d" % j], T.xi[:, 512 * j:512 * j + 512], T.x[:, 512 * j:512 * j + 512])
-
-    iota(["pcol"], T.pcol[:], [[0, 1]], 0, 1, small=False)
-    iota(["nrow"], T.nrow[:], [[1, 352]], -96, 0)
-    iota(["rv1"], T.rv1[:], [[1, 8], [0, 16]], 0, 0)
-    iota(["rv2"], T.rv2[:], [[16, 8], [0, 4], [1, 4]], 0, 0)
-    fill(["tab0"], T.tab[:, 0:2048], BIG)
-    for j in range(VFILL // 2048, TW // 2048):
-        act(["tab0"], [TAB[j]], T.tab[:, 2048 * j:2048 * j + 2048], T.tab[:, 0:2048])
+    M = {"mf1": T.ff[:, 0:128], "fi1": T.ff[:, 128:256], "rj1": T.rr[:, 0:128], "ri1": T.rr[:, 128:256],
+         "cs1": T.cs1[:], "mf2": T.mf2[:], "fi2": T.fi2[:]}
+    AND, SHR = OP.bitwise_and, OP.arith_shift_right
+    EQ, MUL, ADD, SUB, GE = OP.is_equal, OP.mult, OP.add, OP.subtract, OP.is_ge
 
     def cf(j):
         return T.cf[:, j:j + 1]
@@ -230,493 +302,429 @@ def rank_program(g, core, T, topo):
     def wf(j):
         return T.wf[:, j:j + 1]
 
+    def part(j):
+        return T.tab[:, 2048 * j:2048 * j + 2048]
+
     def cast(j):
         cp(["xi%d" % j], [XB[j]], T.xb[:, 512 * j:512 * j + 512], T.xi[:, 512 * j:512 * j + 512])
 
-    AND, SHR = OP.bitwise_and, OP.arith_shift_right
-    EQ, MUL, ADD, SUB, GE = OP.is_equal, OP.mult, OP.add, OP.subtract, OP.is_ge
-    bit = [(0x70, AND, None), (15, AND, None), (4, SHR, None), (7, AND, None), (3, SHR, None), (3, AND, None),
-           (2, SHR, 3), (6, SHR, None), (3, SHR, 7), (127, AND, None)]
-    for j, (a, op, b) in enumerate(bit):
+    dma("s", "dw", [], ["ew"], T.ew[:, 0:1], T.w1[:])
+    dma("y", "dw", [], ["ew1"], T.ew[:, 1:2], T.w2[:])
+    dma("s", "dw", [], ["ew2"], T.ew[:, 2:34], T.pa[:])
+    lastw["ew"] = lastw["ew2"]
+    for j in range(4):
+        dma("y", "dx%d" % j, [], ["xi%d" % j], T.xi[:, 512 * j:512 * j + 512], T.x[:, 512 * j:512 * j + 512])
+    dma("s", "dpb", [], ["pbi"], T.pbi[:], T.pb[:])
+
+    iota(["pcol"], T.pcol[:], [[0, 1]], 0, 1, small=False)
+    iota(["pf"], T.pf[:], [[0, 1]], 0, 1)
+    iota(["nrow"], T.nrow[:], [[1, 144]], 0, 0)
+    iota(["rv1"], T.rv1[:], [[1, 8], [0, 16]], 0, 0)
+    fill([TAB[0]], part(0), float(EMPTY))
+    for j in (2, 3, 4):
+        act([TAB[0]], [TAB[j]], part(j), part(0))
+    for j, (a, op, b) in enumerate([(15, AND, None), (4, SHR, None), (1, SHR, 7), (1, AND, None)]):
         ts(["pcol"], ["ci%d" % j], T.ci[:, j:j + 1], T.pcol[:], a, op, b, None if b is None else AND)
     fill(["ones"], T.ones[:], 1.0)
-    cp(["ci%d" % j for j in range(10)], ["cf"], T.cf[:, 0:10], T.ci[:, 0:10])
+    cp(["ci%d" % j for j in range(4)], ["cf"], T.cf[:, 0:4], T.ci[:, 0:4])
     fill(["crow"], T.crow[0:1, :], 4096.0 * QOFF)
-    ts(["nrow", "cf"], ["zone"], T.zone[:], T.nrow[:, 81:225], cf(0), EQ)
-    o1 = S1 * rank
-    cp(["ew"], ["wf0"], T.wf[:, 0:2], T.ew[:, 0:2])
-    cp(["ew"], ["l0"], T.l0[:], T.ew[:, 2:6])
-    shift(["wf0", "l0"], [(T.wf[:, 0:2], -SH, "es", "aes"), (T.l0[:], -SH, "el", "ael")])
-    cp(["ew"], ["la1w"], T.la1[:, o1:o1 + 2], T.ew[:, 0:2])
-    for j in range(2):
-        ts(["zone", "wf0"], ["zw%d" % j], T.zw[:, 144 * j:144 * j + 144], T.zone[:], wf(j), MUL)
-    ts(["wf0"], ["wf2"], T.wf[:, 2:4], T.wf[:, 0:2], -1.0, MUL)
-    for j in range(1, VFILL // 2048):
-        fill([TAB[j]], T.tab[:, 2048 * j:2048 * j + 2048], BIG)
-    cast(0)
-    cp(["pbi"], ["lb"], T.lb[:], T.pbi[:, 0:2])
-    for j in range(2):
-        ts(["rv1", "cf", "wf2"], ["nw%d" % j], T.nw[:, 128 * j:128 * j + 128], T.rv1[:], cf(2), EQ, wf(2 + j), MUL)
-    ts(["nrow", "cf"], ["idh"], T.idh[:], T.nrow[:, 96:224], cf(9), EQ)
-    ts(["nrow", "cf"], ["idq"], T.idq[:], T.nrow[:, 96:224], cf(9), EQ, -4096.0, MUL)
-    cast(1)
-
-    def sums(bank, z0, halves):
-        for h in halves:
-            a, b = (0, NV) if h is None else (1024 * h, 1024 * h + 1024)
-            rd = XB[a // 512:b // 512]
-            for j in range(2):
-                for r in range(16):
-                    o = 144 * (z0 + j) + 15 - r
-                    mm(rd + ["zw%d" % (z0 + j)], bank, T[bank][:, 128 * j + a // 16:128 * j + b // 16], T.zw[:, o:o + 128],
-                       T.xb[:, a + r:b:16], a == 0 and j == 0 and r == 0, b == NV and j == 1 and r == 15)
-
-    sums("m0", 0, [0])
-    ts(["cf"], ["i3"], T.i3[:], cf(1), -1.0, ADD, 1.0 / 3.0, MUL)
-    ts(["cf"], ["ct0"], ct(0), cf(4), 6.0, GE)
-    ts(["cf"], ["ct1"], ct(1), cf(8), 2.0, GE, 2.0, ADD)
-    ts(["i3", "cf"], ["ct2"], ct(2), T.i3[:], 8.0, MUL, cf(2), ADD)
-    ts(["i3", "cf"], ["ct3"], ct(3), T.i3[:], -3.0, MUL, cf(1), ADD)
-    ts(["cf", "ct0"], ["ct4"], ct(4), cf(4), 12.0, GE, ct(0), ADD)
-    ts(["cf", "ct1"], ["ct5"], ct(5), cf(7), 4.0, MUL, ct(1), ADD)
-    cast(2)
+    ts(["cf"], ["i3"], T.i3[:], cf(0), -1.0, ADD, 1.0 / 3.0, MUL)
+    ts(["nrow", "cf"], ["gs"], T.gs[:], T.nrow[:, 0:8], cf(1), EQ)
+    ts(["i3", "cf"], ["ct2"], ct(2), T.i3[:], 8.0, MUL, cf(1), ADD)
+    ts(["i3", "cf"], ["ct3"], ct(3), T.i3[:], -3.0, MUL, cf(0), ADD)
+    ts(["cf"], ["ct4"], ct(4), cf(1), 16.0, MUL, 15.0, ADD)
+    ts(["nrow", "pf"], ["idb"], T.idb[:], T.nrow[:, 0:128], T.pf[:], EQ)
+    ts(["nrow", "ct4"], ["zone"], T.zone[:], T.nrow[:], ct(4), EQ)
     ts(["ct3"], ["ct6"], ct(6), ct(3), 1.0, GE, 255.0, MUL)
     ts(["ct3"], ["ct7"], ct(7), ct(3), 2.0, GE, 65280.0, MUL)
-    ts(["cf", "ct4"], ["ct8"], ct(8), cf(3), 16.0, MUL, ct(4), ADD)
-    ts(["cf", "ct5"], ["ct9"], ct(9), cf(3), 16.0, MUL, ct(5), ADD)
+    cp(["ew"], ["wf0"], T.wf[:, 0:2], T.ew[:, 0:2])
+    cp(["ew"], ["l0"], T.l0[:], T.ew[:, 2:6])
+    shift(["wf0", "l0"], [(T.wf[:, 0:2], -SH, T.es[:], "es", "aes"), (T.l0[:], -SH, T.el[:], "el", "ael")])
+    shift(["wf0"], [(T.wf[:, 0:2], SH, T.ep[:], "ep", "aep")])
+    iota([TAB[5]], part(5), [[0, 2048]], EMPTY, 0)
     ts(["ct6", "ct7"], ["ct10"], ct(10), ct(6), ct(7), ADD, 1.0, ADD)
-    cast(3)
-    sums("m0", 0, [1])
-    ts(["cf", "ct10"], ["ct11"], ct(11), cf(1), 12.0, GE, ct(10), MUL)
-    ts(["nrow", "ct8"], ["ya"], T.ya[:], T.nrow[:, 84:228], ct(8), EQ)
-    ts(["nrow", "ct9"], ["y1"], T.y1[:], T.nrow[:, 88:232], ct(9), EQ)
-    ts(["nrow", "ct2", "ct10"], ["zp"], T.zp[:], T.nrow[:, 0:256], ct(2), EQ, ct(10), MUL)
-    ts(["nrow", "ct2", "ct11"], ["zq"], T.zq[:], T.nrow[:, 0:256], ct(2), EQ, ct(11), MUL)
+    ts(["nrow", "ct2", "ct10"], ["pk"], T.pk[:], T.nrow[:, 0:48], ct(2), EQ, ct(10), MUL)
+    ts(["wf0"], ["wf2"], T.wf[:, 2:4], T.wf[:, 0:2], -1.0, MUL)
+    for j in range(2):
+        ts(["zone", "wf0"], ["zw%d" % j], T.zw[:, 144 * j:144 * j + 144], T.zone[:], wf(j), MUL)
+    fill([TAB[1] + "a"], T.tab[:, 2048:3072], float(EMPTY))
+    cast(0)
+    cp(["pbi"], ["lb"], T.lb[:], T.pbi[:])
+    ts(["rv1", "cf"], ["bm"], T.bm[:], T.rv1[:], cf(1), EQ)
+    fill([TAB[1]], T.tab[:, 3072:4096], float(EMPTY))
+    cast(1)
 
-    def slots(out, outname, between=()):
-        rest = list(between) + [lambda: None] * 5
-        ts(["s12a", "s12b"], ["u12"], T.u12[:], T.s12[:], 4095, AND)
-        rest[0]()
-        tt(["u12"], ["m1"], T.m1[:], T.u12[:, 0:128], T.u12[:, 128:256], MUL)
-        rest[1]()
-        ts(["m1"], ["k1"], T.k1[:], T.m1[:], 5, SHR, 8191, AND)
-        rest[2]()
-        tt(["k1", "u12"], ["h1"], T.h1[:], T.k1[:], T.u12[:, 128:256], ADD)
-        rest[3]()
-        cp(["h1"], [outname], out, T.h1[:])
+    def own_sums(h):
+        for j in range(2):
+            for r in range(16):
+                o = 144 * j + 15 - r
+                mm(XB[2 * h:2 * h + 2] + ["zw%d" % j], PB[h], T[PB[h]][:, 64 * j:64 * j + 64], T.zw[:, o:o + 128],
+                   T.xb[:, 1024 * h + r:1024 * h + 1024:16], j == 0 and r == 0, j == 1 and r == 15)
+
+    def sums(bank, s, stop=True):
+        for r in range(16):
+            mm(XB + ["wm%d0" % s, "wm%d1" % s], bank, T[bank][:, r:256:16], T.xb[:, r::16], T.wm[:, 16 * s:16 * s + 16],
+               r == 0, stop and r == 15)
+
+    def words(bank, src, name, h, pk, first, blocks=range(8)):
+        for b in blocks:
+            o = 1024 * h + 128 * b
+            mm(name(o) + [pk], bank, T[bank][:, b:384:8], src(o), T[pk][:], first and b == 0, not first and b == 7)
+
+    def slots(h, out, name):
+        a, m, b = 128 * h, 128 * h + 64, 128 * h + 128
+        c = slice(64 * h, 64 * h + 64)
+        return [lambda: ts(["s12a%d" % h, "s12b%d" % h], ["u12%d" % h], T.u12[:, a:b], T.s12[:, a:b], 4095, AND),
+                lambda: tt(["u12%d" % h], ["m1%d" % h], T.m1[:, c], T.u12[:, a:m], T.u12[:, m:b], MUL),
+                lambda: ts(["m1%d" % h], ["k1%d" % h], T.k1[:, c], T.m1[:, c], 5, SHR, 8191, AND),
+                lambda: tt(["k1%d" % h, "u12%d" % h], ["h1%d" % h], T.h1[:, c], T.k1[:, c], T.u12[:, m:b], ADD),
+                lambda: cp(["h1%d" % h], [name + str(h)], out[:, c], T.h1[:, c])]
+
+    def own_slots(h):
+        cp([PB[h]], ["s12a%d" % h, "s12b%d" % h], T.s12[:, 128 * h:128 * h + 128], T[PB[h]][:, 0:128])
+        return slots(h, T.own, "own")
 
     def put(j):
-        cp(["own", XB[j]], TAB, T.tab[:].indirect(T.own[:, 32 * j:32 * j + 32]), T.xb[:, 512 * j:512 * j + 512])
+        cp(["own%d" % (j // 4), XB[j // 2]], TAB + [TAB[1] + "a"], T.tab[:].indirect(T.own[:, 16 * j:16 * j + 16]),
+           T.xb[:, 256 * j:256 * j + 256])
 
-    cp(["m0"], ["s12a", "s12b"], T.s12[:], T.m0[:, 0:256])
-    slots(T.own[:], "own")
+    own_sums(0)
+    ts(["nrow", "pf"], ["idh"], T.idh[:], T.nrow[:, 0:128], T.pf[:], EQ)
+    cast(2)
+    steps = own_slots(0)
+    steps[0]()
+    steps[1]()
+    cast(3)
+    for step in steps[2:]:
+        step()
     put(0)
+    for j in range(2):
+        act(["gs", "es"], ["wm0%d" % j], T.wm[:, 8 * j:8 * j + 8], T.gs[:], scale=T.es[:, j:j + 1])
+    o1 = S1 * rank
+    act(XB + ["lb"], ["la1a"], T.la1[:, o1 + 15:o1 + 31], T.xb[:].indirect(T.lb[:, 0:1]), scale=-1.0)
+    act(XB + ["el", "la1a"], ["la1b"], T.la1[:, o1 + 16:o1 + 32], T.xb[:].indirect(T.el[:, 0:1]))
+    gather_all(["la1a", "la1b"], "al1", T.la1[:, o1 + 15:o1 + 17], "la1")
+    hand(XB, T.xb[:, 1024:2048], "hx1")
+    act(["idb"], ["idq"], T.idq[:], T.idb[:], scale=-4096.0)
+    sums("q0", 0)
+    sums("q1", 0, False)
+    act(["q0"], ["na"], T.na[:], T.q0[:, 0:256], bias=QOFF + 0.5 / 4096, scale=1.0 / 4096)
+    mm(["na", "idq"], "q1", T.q1[:, 0:256], T.idq[:], T.na[:], False, True)
+    own_sums(1)
+    ts(["q1"], ["ao"], T.ao[:], T.q1[:, 0:256], 4096.0 * QOFF, ADD)
+    send("ao", SH, "ah", "aah")
+    shift(XB, [(T.xb[:, 0:1024], SH, T.xp[:, 0:1024], "xp0", "axp0")])
+    hand(XB, T.xb[:, 0:1024], "hx0")
     put(1)
-    act(XB + ["lb"], ["la1a"], T.la1[:, o1 + 2:o1 + 18], T.xb[:].indirect(T.lb[:, 0:1]), scale=-1.0)
-    act(XB + ["el"], ["la1b"], T.la1[:, o1 + 18:o1 + 34], T.xb[:].indirect(T.el[:, 0:1]))
-    gather_all(["la1a", "la1b", "la1w"], "al1", T.la1[:, o1:o1 + 19], "la1")
-    for j in (2, 3):
-        act(["zone", "es"], ["zw%d" % j], T.zw[:, 144 * j:144 * j + 144], T.zone[:], scale=T.es[:, j - 2:j - 1])
-    sums("mb", 2, [None])
-    ts(["mb"], ["s12a", "s12b"], T.s12[:], T.mb[:, 0:256], 2048.0, ADD)
-    ts(["s12a", "s12b"], ["u12"], T.u12[:], T.s12[:], 4095, AND)
-    ts(["u12"], ["ao"], T.ao[:], T.u12[:], -2048.0, ADD)
-    shift(["ao"], [(T.ao[:], SH, "ah", "aah")])
-    shift(XB, [(T.xb[:], SH, "xp", "axp")])
-    iota(["krow"], T.krow[0:1, :], [[1, 512]], 0, 0)
+    steps = own_slots(1)
     put(2)
+    steps[0]()
+    steps[1]()
     put(3)
+    for step in steps[2:]:
+        step()
+    for j in range(2):
+        act(["gs", "ep"], ["wm1%d" % j], T.wm[:, 16 + 8 * j:24 + 8 * j], T.gs[:], scale=T.ep[:, j:j + 1])
+    for j in range(2):
+        act(["bm", "wf2"], ["nw%d" % j], T.nw[:, 128 * j:128 * j + 128], T.bm[:], scale=wf(2 + j))
+    act(["pk"], ["npk"], T.npk[:], T.pk[:], scale=-1.0)
+    act(["idb"], ["idf"], T.idf[:], T.idb[:])
+    act(["bm"], ["b8"], T.b8[:], T.bm[:], scale=8.0)
+    act(["bm"], ["b1k"], T.b1k[:], T.bm[:], scale=1024.0)
+    sums("q2", 1)
+    act(["q2"], ["aso"], T.aso[:], T.q2[:, 0:256])
+    hand(["aso"], T.aso[:], "has")
+    iota(["krow"], T.krow[0:1, :], [[1, 512]], 0, 0)
+    iota(["c8"], T.c8[:], [[16, 8]], 0, 1)
 
-    def late_sums():
-        for j in (4, 5):
-            c = S1 * pred + j - 4
-            act(["zone", "la1"], ["zw%d" % j], T.zw[:, 144 * j:144 * j + 144], T.zone[:], scale=T.la1[:, c:c + 1])
+    def const(c):
+        mm(["ones", "crow"], PB[c], T[PB[c]][:, 256:512], T.ones[0:1, :], T.crow[0:1, :], True, False)
 
-    def late_sends():
-        sums("r0", 4, [None])
-        act(["r0"], ["aso"], T.aso[:], T.r0[:, 0:256])
-        shift(["aso"], [(T.aso[:], -SH, "asi", "aas")])
-        shift(XB, [(T.xb[:], -SH, "xs", "axs")])
+    def apart(bank, start, stop):
+        for k in range(4):
+            o = 128 * (k // 2)
+            mm(["ah", "idh"], bank, T[bank][:, 128 * k:128 * k + 128], T.ah[:, o:o + 128], T.idh[:], start and k == 0, stop and k == 3)
 
-    def lists_front(t):
-        side = ("r0", "r1", "mb", "m0")
+    def bpart(bank, c, start, stop):
+        for j in range(2):
+            mm(["nw%d" % j] + DBC[2 * c:2 * c + 2], bank, T[bank][:, 256 * j:256 * j + 256],
+               T.nw[:, 128 * j:128 * j + 128], T.dbc[:, 256 * c:256 * c + 256], start and j == 0, stop and j == 1)
 
-        def apart(bank, b, start, stop):
-            o = 128 * (b // 2)
-            for dd in range(4):
-                mm(["ah", "idh"], bank, T[bank][:, 128 * dd:128 * dd + 128], T.idh[:], T.ah[:, o:o + 128],
-                   start and dd == 0, stop and dd == 3)
+    def front(t):
+        def spread(c):
+            for d in (2 * c, 2 * c + 1):
+                out = T.dbc[:, 128 * d:128 * d + 128]
+                if t == 1:
+                    a, b = S1 * ((d - SH) % N) + 16, S1 * d + 15
+                    act(["la1", "la1a", "la1b", "ones"], [DBC[d]], out, T.ones[:],
+                        scale=T.la1[:, a:a + 1], bias=T.la1[:, b:b + 1])
+                else:
+                    a = S2 * d + 4
+                    act(["la2", "la2a", "ones"], [DBC[d]], out, T.ones[:], scale=T.la2[:, a:a + 1])
 
-        def const(b):
-            bank = "p%d" % b
-            mm(["ones", "crow"], bank, T[bank][:], T.ones[0:1, :], T.crow[0:1, :], True, False)
-
-        def bpart(bank, b, start, stop):
-            j, h = b // 2, b % 2
-            mm(["nw%d" % j] + DBC[4 * h:4 * h + 4], bank, T[bank][:],
-               T.nw[:, 128 * j:128 * j + 128], T.dbc[:, 512 * h:512 * h + 512], start, stop)
-
-        def spread(d):
-            out = T.dbc[:, 128 * d:128 * d + 128]
+        def side(c):
+            bpart(WB[c], c, t == 1, t == 2)
             if t == 1:
-                a, b = S1 * ((d - SH) % N) + 18, S1 * d + 2
-                act(["la1", "la1a", "la1b", "ones"], [DBC[d]], out, T.ones[:],
-                    scale=T.la1[:, a:a + 1], bias=T.la1[:, b:b + 1])
-            else:
-                a = S2 * d + 4
-                act(["la2", "la2a", "ones"], [DBC[d]], out, T.ones[:], scale=T.la2[:, a:a + 1])
+                apart(WB[c], False, True)
 
-        def rem(b):
-            act([side[b]], ["nn%d" % b], T.nn[:, 512 * b:512 * b + 512], T[side[b]][:],
+        def full(c):
+            bpart(PB[c], c, False, False)
+            if t == 1:
+                apart(PB[c], False, False)
+
+        def rem(c):
+            act([WB[c]], ["nn%d" % c], T.nn[:, 512 * c:512 * c + 512], T[WB[c]][:],
                 bias=QOFF + 0.5 / 4096 - 0.5, scale=1.0 / 4096)
 
-        def sub(b):
-            bank = "p%d" % b
-            mm(["nn%d" % b, "idq"], bank, T[bank][:], T.idq[:], T.nn[:, 512 * b:512 * b + 512], False, True)
+        def sub(c):
+            mm(["nn%d" % c, "idq"], PB[c], T[PB[c]][:], T.idq[:], T.nn[:, 512 * c:512 * c + 512], False, True)
 
-        def out1(h):
-            act(["p%d" % h], ["u1%d" % h], T.u1[:, 512 * h:512 * h + 512], T["p%d" % h][:], bias=4096.0 * QOFF)
+        def out1(c):
+            act([PB[c]], ["u1%d" % c], T.u1[:, 256 * c:256 * c + 256], T[PB[c]][:, 0:256], bias=4096.0 * QOFF)
 
-        const(2)
-        const(3)
-        if t == 1:
-            for d in range(8):
-                spread(d)
-            late_sums()
-            for b in (0, 2, 1, 3):
-                bpart(side[b], b, True, False)
-                bpart("p%d" % b, b, b < 2, False)
-            for h in range(2):
-                apart(side[h], h, False, True); rem(h)
-                apart(side[2 + h], 2 + h, False, True); rem(2 + h)
-                apart("p%d" % h, h, False, False); sub(h); out1(h)
-                apart("p%d" % (2 + h), 2 + h, False, False); sub(2 + h)
-        else:
-            for b in (0, 2, 1, 3):
-                apart(side[b], b, True, False)
-                apart("p%d" % b, b, b < 2, False)
-            for h in range(2):
-                for d in range(4 * h, 4 * h + 4):
-                    spread(d)
-                bpart(side[h], h, False, True); bpart(side[2 + h], 2 + h, False, True)
-                bpart("p%d" % h, h, False, False); bpart("p%d" % (2 + h), 2 + h, False, False)
-                rem(h); rem(2 + h); sub(h); sub(2 + h); out1(h)
-        for j in range(2):
-            mm(["nw%d" % j] + DBC, "m0", T.m0[:, 8 * j:8 * j + 8],
-               T.nw[:, 128 * j:128 * j + 128], T.dbc[:, 0::128], j == 0, j == 1)
+        for c in range(4):
+            const(c)
+            if t == 2:
+                apart(WB[c], True, False)
+                apart(PB[c], False, False)
+        a, b, c, d = 0, 2, 1, 3
+        spread(a); side(a); full(a)
+        spread(b); side(b)
+        rem(a); sub(a); full(b)
+        spread(c); side(c)
+        out1(a); rem(b); sub(b); full(c)
+        spread(d); side(d)
+        out1(b); rem(c); sub(c); full(d)
+        rem(d); sub(d)
+        out1(c); out1(d)
 
-    def lists_back(parts):
-        for step in range(4):
-            for (a, b) in parts:
-                h = a // 512
-                bank = "p%d" % (2 + h)
-                u2 = T[bank][:, a - 512 * h:b - 512 * h]
-                if step == 0:
-                    tt(["u1%d" % h, bank], ["mm%d" % a], T.mm[:, a:b], T.u1[:, a:b], u2, MUL)
-                elif step == 1:
-                    ts(["mm%d" % a], ["kk%d" % a], T.kk[:, a:b], T.mm[:, a:b], 5, SHR, 8191, AND)
-                elif step == 2:
-                    tt(["kk%d" % a, bank], ["hh%d" % a], T.hh[:, a:b], T.kk[:, a:b], u2, ADD)
-                else:
-                    cp(["hh%d" % a], ["lst%d" % d for d in range(a // 128, b // 128)], T.lst[:, a:b], T.hh[:, a:b])
+    def back(c):
+        a, b = 256 * c, 256 * c + 256
+        u2 = T[PB[c]][:, 256:512]
+        return [lambda: tt(["u1%d" % c, PB[c]], ["mm%d" % c], T.mm[:, a:b], T.u1[:, a:b], u2, MUL),
+                lambda: ts(["mm%d" % c], ["kk%d" % c], T.kk[:, a:b], T.mm[:, a:b], 5, SHR, 8191, AND),
+                lambda: tt(["kk%d" % c, PB[c]], ["hh%d" % c], T.hh[:, a:b], T.kk[:, a:b], u2, ADD),
+                lambda: cp(["hh%d" % c], ["lst%d" % c], T.lst[:, a:b], T.hh[:, a:b])]
 
-    def look(q, d, q0, q1):
-        out = T.ga[:, NV * d + 512 * q0:NV * d + 512 * q1]
-        src = T.tab[:].indirect(T.lst[:, 128 * d + 32 * q0:128 * d + 32 * q1])
-        nd = T.dbc[:, 128 * d:128 * d + 1]
-        r, w = TAB + ["lst%d" % d, DBC[d]], ["ga%d_%d" % (d, k) for k in range(q0, q1)]
-        if q == "s":
-            act(r, w, out, src, bias=nd)
-        else:
-            ts(r, w, out, src, nd, ADD)
-
-    def packa(bank, src, name, order=(0, 1, 2), start=True, stop=True):
-        for n, k in enumerate(order):
-            o = 96 - 8 * (6 * k)
-            mm([name(k), "zp"], bank, T[bank][:], T.zp[:, o:o + 128], src(k), start and n == 0, stop and n == len(order) - 1)
-
-    def packb(bank, src, name, odd, first):
-        o = 96 - 8 * (4 if odd else -4)
-        mm([name(2), "zq"], bank, T[bank][:], T.zq[:, o:o + 128], src(2), first, False)
-        o = 96 - 8 * (10 if odd else 2)
-        mm([name(3), "zp"], bank, T[bank][:], T.zp[:, o:o + 128], src(3), False, not first)
-
-    def gsrc(d):
-        return lambda k: T.ga[:, NV * d + 512 * k:NV * d + 512 * k + 512]
+    def first_lists(scatter):
+        steps = back(0)
+        steps[0]()
+        scatter(6)
+        for x in steps[1:]:
+            x()
+        scatter(7)
 
     def gname(d):
-        return lambda k: "ga%d_%d" % (d, k)
+        return lambda o: ["ga%d_%d" % (d, o // 256)]
+
+    def gsrc(d):
+        return lambda o: T.ga[:, NV * d + o:NV * d + o + 128]
+
+    def look(q, d, a, b, lst, lname, bias, bname):
+        out = T.ga[:, NV * d + a:NV * d + b]
+        src = T.tab[:].indirect(lst(a // 16, b // 16))
+        r, w = TAB + lname + [bname], ["ga%d_%d" % (d, k) for k in range(a // 256, b // 256)]
+        if q == "S":
+            act(r, w, out, src, bias=bias)
+        else:
+            ts(r, w, out, src, bias, ADD)
+
+    def minus(bank, ref, h):
+        words(bank, lambda o: T[ref][:, o:o + 128], lambda o: [ref + "%d" % h if ref == "xp" else ref], h, "npk", True)
+
+    def compare(q, bank, d, h):
+        out, w = T.ne[:, 768 * d + h:768 * d + 768:2], ["ne%d_%d" % (d, h)]
+        if q == "S":
+            act([bank], w, out, T[bank][:, 0:384], ACT.Abs)
+        else:
+            ts([bank], w, out, T[bank][:, 0:384], 0.0, OP.not_equal)
+
+    def misses(bank, d, masks):
+        for k, m in enumerate(masks):
+            mm([m, "idb"], bank, T[bank][:, 0:128], T.idb[:], M[m], k == 0, False)
+        for w in range(6):
+            o = 768 * d + 128 * w
+            mm(["ne%d_0" % d, "ne%d_1" % d, "idb"], bank, T[bank][:, 0:128], T.ne[:, o:o + 128], T.idb[:],
+               w == 0 and not masks, w == 5)
 
     def main(t):
-        W = T["w_%d" % t]
-        nei = [0]
-        started = {}
-
-        def pa_(d, bank, order=(0, 1, 2), start=True, stop=True):
-            packa(bank, gsrc(d), gname(d), order, start, stop)
-
-        def pb_(d, bank, first):
-            packb(bank, gsrc(d), gname(d), d % 2 == 1, first)
-
-        def cmp_(bank, kind):
-            j = nei[0]
-            nei[0] += 1
-            tt([bank, "xpk%d" % kind], ["ne%d" % j], T.ne[:, 512 * j:512 * j + 512], T[bank][:],
-               T.xpk[:, 512 * kind:512 * kind + 512], OP.not_equal)
-            return j
-
-        def sum_(j, d, kind, last=False):
-            rb = "r%d" % (d // 4)
-            first = rb not in started
-            started[rb] = True
-            if kind == 0:
-                o = 12 - 4 * (d % 4)
-                mm(["ne%d" % j, "ya"], rb, T[rb][:], T.ya[:, o:o + 128], T.ne[:, 512 * j:512 * j + 512], first, last)
+        order, turns, summed = timetable()
+        co = 8 * (t - 1)
+        for q, step in order:
+            k = step[0]
+            if k == "L":
+                for steps in zip(back(2), back(1), back(3)):
+                    for x in steps:
+                        x()
+                continue
+            d, h = int(step[1]), int(step[2:] or 0)
+            bank = PB[summed.index(step[1]) % 4] if k in "sn" else WB[turns.index(step[1:]) % 4]
+            if k == "g":
+                look(q, d, 1024 * h, 1024 * h + 1024, lambda a, b: T.lst[:, 128 * d + a:128 * d + b], ["lst%d" % (d // 2)],
+                     T.dbc[:, 128 * d:128 * d + 1], DBC[d])
+            elif k == "m":
+                minus(bank, "xp", h)
+            elif k == "w":
+                words(bank, gsrc(d), gname(d), h, "pk", False)
+            elif k == "c":
+                compare(q, bank, d, h)
+            elif k == "s":
+                misses(bank, d, [] if t == 1 else ["mf1", "rj1"])
             else:
-                o = 8 - 4 * (d % 4)
-                mm(["ne%d" % j, "y1"], rb, T[rb][:], T.y1[:, o:o + 128], T.ne[:, 512 * j:512 * j + 512], first, last)
-
-        def count(tau):
-            c = 2 * (t - 1) + tau
-            act(["r%d" % tau], ["fit%d" % tau, "cnt%d" % c], T.fit[:, 512 * tau:512 * tau + 512], T["r%d" % tau][:],
-                ACT.Relu, bias=1.0, scale=-1.0, accum=T.cnt[:, c:c + 1])
-
-        def halves(q, d):
-            look(q, d, 0, 2)
-            look(q, d, 2, 4)
-
-        def front(d, bank):
-            pa_(d, bank, (0, 1), True, False)
-
-        def back(d, bank):
-            pa_(d, bank, (2,), False, True)
-
-        if t == 2:
-            for rb in ("r0", "r1"):
-                started[rb] = True
-                for s in range(4):
-                    for m in ("mf1", "rj1"):
-                        mm([m, "xm"], rb, T[rb][:, 128 * s:128 * s + 128], T.xm[:, 128 * s:128 * s + 128], T[m][:],
-                           s == 0 and m == "mf1", False)
-        lists_back([(0, 128), (128, 256)])
-        halves("s", 0)
-        lists_back([(384, 512), (256, 384)])
-        cp(["m0"], ["wb%d" % t], W[:, 8:24], T.m0[:, 0:16])
-        if t == 1:
-            xs_ = lambda k: T.xp[:, 512 * k:512 * k + 512]
-            xn_ = lambda k: "xp"
-            late_sends()
-            packa("m0", xs_, xn_)
-            packb("mb", xs_, xn_, False, True)
-            packb("mb", xs_, xn_, True, False)
-        halves("s", 1)
-        halves("s", 2)
-        halves("v", 3)
-        front(0, "p0"); front(3, "p2"); back(0, "p0"); pb_(0, "p1", True); back(3, "p2")
-        if t == 1:
-            cp(["mb"], ["xpk1"], T.xpk[:, 512:1024], T.mb[:])
-            cp(["m0"], ["xpk0"], T.xpk[:, 0:512], T.m0[:])
-        lists_back([(512, 768), (768, 1024)])
-        halves("s", 4)
-        halves("s", 6)
-        pb_(3, "mb", True)
-        pb_(1, "p1", False); pa_(1, "p3")
-        a, c, b, e = cmp_("p0", 0), cmp_("p2", 0), cmp_("p1", 1), cmp_("p3", 0)
-        sum_(a, 0, 0); sum_(c, 3, 0)
-        front(2, "m0")
-        sum_(b, 0, 1); sum_(e, 1, 0)
-        back(2, "m0"); pb_(2, "mb", False)
-        halves("v", 5)
-        front(5, "p0"); front(4, "p2"); back(5, "p0"); pb_(5, "p1", True)
-        a, b = cmp_("m0", 0), cmp_("mb", 1)
-        sum_(a, 2, 0)
-        back(4, "p2")
-        sum_(b, 2, 1, True)
-        pb_(4, "p1", False)
-        count(0)
-        for k in range(SQ7):
-            look("s", 7, k, k + 1)
-        c = cmp_("p0", 0)
-        sum_(c, 5, 0)
-        look("v", 7, SQ7, 4)
-        prep(t)
-        front(6, "p3")
-        pb_(7, "m0", True)
-        pa_(7, "mb", tuple(range(SQ7, 3)), True, False)
-        a, b = cmp_("p2", 0), cmp_("p1", 1)
-        sum_(a, 4, 0)
-        back(6, "p3")
-        pb_(6, "m0", False)
-        sum_(b, 4, 1)
-        a, b = cmp_("p3", 0), cmp_("m0", 1)
-        sum_(a, 6, 0)
-        pa_(7, "mb", tuple(range(SQ7 - 1)), False, False)
-        sum_(b, 6, 1)
-        pa_(7, "mb", (SQ7 - 1,), False, True)
+                act([bank], ["fit%d" % d, "cnt%d" % (co + d)], T.fit[:, 128 * d:128 * d + 128], T[bank][:, 0:128],
+                    ACT.Relu, bias=1.0, scale=-1.0, accum=T.cnt[:, co + d:co + d + 1])
         cl = T["cl%d" % t]
         o = 8 * rank
-        ts(["wv%da" % t, "cnt%d" % (2 * t - 2)], ["cla%d" % t], cl[:, o:o + 4], W[:, 24:28], T.cnt[:, 2 * t - 2:2 * t - 1], MUL)
-        a = cmp_("mb", 0)
-        sum_(a, 7, 0, True)
-        count(1)
-        ts(["wv%d" % t, "cnt%d" % (2 * t - 1)], ["clb%d" % t], cl[:, o + 4:o + 8], W[:, 36:40], T.cnt[:, 2 * t - 1:2 * t], MUL)
-        gather_all(["cla%d" % t, "clb%d" % t], "ac%d" % t, cl[:, o:o + 8], "cl%d" % t)
-
-    def prep(t):
-        W = T["w_%d" % t]
-        wv = "wv%d" % t
+        names = ["cnt%d" % (co + d) for d in range(8)]
         if t == 1:
-            ts(["nrow", "cf"], ["wv1a"], W[:, 24:28], T.nrow[:, 96:100], cf(6), EQ)
-            ts(["nrow", "cf"], [wv], W[:, 36:40], T.nrow[:, 96:100], cf(6), EQ)
+            cp(names, ["clo1"], cl[:, o:o + 8], T.cnt[:, 0:8])
         else:
-            lr = ["la2", "la2b"]
-            tt(lr + ["wv1a"], ["wv2a"], W[:, 24:28], T.w_1[:, 24:28], T.la2[:, 3:4 * S2:S2], MUL)
-            tt(lr + ["wv1a"], [wv], W[:, 36:40], T.w_1[:, 24:28], T.la2[:, 4 * S2 + 3::S2], MUL)
+            tt(names + ["la2", "la2b"], ["clo2"], cl[:, o:o + 8], T.cnt[:, 8:16], T.la2[:, 3::S2], MUL)
+        gather_all(["clo%d" % t], "ac%d" % t, cl[:, o:o + 8], "cl%d" % t)
 
-    def prep2(t):
+    def choices(t):
         W = T["w_%d" % t]
         bs = T.base[:, 8 * t - 8:8 * t]
+        for j in range(2):
+            mm(["nw%d" % j] + DBC, "q3", T.q3[:, 8 * j:8 * j + 8], T.nw[:, 128 * j:128 * j + 128], T.dbc[:, 0::128], j == 0, j == 1)
+        for j in range(2):
+            mm(["asi", "idf"], "q0", T.q0[:, 128 * j:128 * j + 128], T.asi[:, 128 * j:128 * j + 128], T.idf[:], j == 0, j == 1)
+        minus("q1", "xs", 0)
+        minus("q2", "xs", 1)
         if t == 1:
-            ts(["rv1", "cf"], ["b8"], T.b8[:], T.rv1[:], cf(2), EQ, 8.0, MUL)
-            ts(["nrow"], ["base1"], bs, T.nrow[:, 96:104], -15.0, ADD, -1.0 / 128, MUL)
-            fill(["wz1"], W[:, 28:36], 0.0)
-            fill(["wy1"], W[:, 40:48], 1.0)
-            cp(["nrow"], ["wd1"], W[:, 48:56], T.nrow[:, 96:104])
+            cp(["ew"], ["la"], T.la[:], T.ew[:, 2:34])
+            act(["xp0", "xp1", "la"], ["pai"], T.pai[:], T.xp[:].indirect(T.la[:]))
+            ts(["nrow"], ["base1"], bs, T.nrow[:, 0:8], -15.0, ADD, -1.0 / 128, MUL)
+            ts(["cf"], ["ct12"], ct(12), cf(0), 4.0, OP.min, 8.0, MUL)
+            fill(["wy1"], W[:, 24:32], 1.0)
+            cp(["nrow"], ["wd1"], W[:, 32:40], T.nrow[:, 0:8])
+            ts(["ct12"], ["ct14"], ct(14), ct(12), 7.0, ADD)
+            ts(["cf"], ["ct15"], ct(15), cf(1), -16.0, MUL, 896.0, ADD)
+            ts(["c8", "ct15"], ["c8"], T.c8[:], T.c8[:], ct(15), ADD)
         else:
             val = T.la2[:, 3::S2]
             lr = ["la2", "la2b"]
             ts(lr, ["b2a"], T.ta[:, 0:8], val, -1.0, ADD, 8.0 / 128, MUL)
-            tt(lr + ["nrow"], ["wd2a"], T.ct[:, 20:28], val, T.nrow[:, 97:105], MUL)
-            fill(["wz2"], W[:, 28:36], 0.0)
+            tt(lr + ["nrow"], ["wd2a"], T.ct[:, 20:28], val, T.nrow[:, 1:9], MUL)
+            ts(lr, ["wy2"], W[:, 24:32], val, 2.0, MUL)
             tt(["b2a", "base1"], ["base2"], bs, T.ta[:, 0:8], T.base[:, 0:8], ADD)
-            ts(lr, ["wy2"], W[:, 40:48], val, 2.0, MUL)
-            ts(["wd2a"], ["wd2"], W[:, 48:56], T.ct[:, 20:28], -1.0, ADD)
-        cp(DBC, ["wn%d" % t], W[:, 0:8], T.dbc[:, 0::128])
-        mm(["b8", "base%d" % t], "m0", T.m0[:, 0:8], T.b8[:], bs, True, False)
+            ts(["wd2a"], ["wd2"], W[:, 32:40], T.ct[:, 20:28], -1.0, ADD)
+        ts(DBC, ["wn%d" % t], W[:, 0:8], T.dbc[:, 0::128], -1.0, MUL)
+        ts(["q3"], ["wb%d" % t], W[:, 8:24], T.q3[:, 0:16], -32768.0, ADD)
+        mm(["b8", "base%d" % t], "p3", T.p3[:, 0:8], T.b8[:], bs, True, False)
 
     def idle1():
-        packa("p1", lambda k: T.xs[:, 512 * k:512 * k + 512], lambda k: "xs", (0, 1))
-        act(["p1"], ["xpk2"], T.xpk[:, 1024:1536], T.p1[:], scale=-1.0)
-        ts(["cf"], ["ct12"], ct(12), cf(1), 6.0, OP.min, 8.0, MUL)
-        ts(["cf"], ["ct13"], ct(13), cf(5), 4.0, MUL, cf(0), ADD)
-        ts(["ct4", "ct8"], ["ct16"], ct(16), ct(4), 3.0, MUL, ct(8), ADD)
-        cp(["ew"], ["pl0"], T.pl[:, 0:32], T.ew[:, 2:34])
-        cp(["pbi"], ["pl1"], T.pl[:, 32:64], T.pbi[:])
-        ts(["ct12"], ["ct14"], ct(14), ct(12), 7.0, ADD)
-        ts(["nrow", "ct13"], ["ys"], T.ys[:], T.nrow[:, 93:237], ct(13), EQ)
-        ts(["nrow", "ct16"], ["yr"], T.yr[:], T.nrow[:, 93:237], ct(16), EQ)
-        act(XB + ["pl1"], ["xbk"], T.xbk[:], T.xb[:].indirect(T.pl[:, 32:64]))
+        ts(["cf"], ["ct16"], ct(16), cf(3), 8.0, MUL, cf(2), ADD)
         ts(["ew"], ["pt0"], T.pt[:, 0:32], T.ew[:, 2:34], 127, AND)
         ts(["pbi"], ["pt1"], T.pt[:, 32:64], T.pbi[:], 127, AND)
         ts(["ew"], ["pt2"], T.pt[:, 64:96], T.ew[:, 2:34], 7, SHR)
         ts(["pbi"], ["pt3"], T.pt[:, 96:128], T.pbi[:], 7, SHR)
-        ts(["rv1", "cf"], ["b1k"], T.b1k[:], T.rv1[:], cf(2), EQ, 1024.0, MUL)
-        cp(["pt0", "pt1", "pt2", "pt3"], ["pl2"], T.pl[:, 64:192], T.pt[:])
+        cp(["pt0", "pt1", "pt2", "pt3"], ["pl"], T.pl[:], T.pt[:])
         fill(["onef"], T.onef[0:1, :], 1.0)
-        ts(["nrow", "pl2", "cf"], ["em"], T.em[:], T.nrow[:, 96:112].indirect(T.pl[:, 128:192]), cf(1), EQ)
+        ts(["nrow", "pl", "ct16"], ["em"], T.em[:], T.nrow[:, 0:16].indirect(T.pl[:, 64:128]), ct(16), EQ)
 
     def blocked(j, src, side):
-        tt([src, "pl2", "em"], ["gm%d" % j], T.gm[:, 512 * j:512 * j + 512],
-           T[src][:].indirect(T.pl[:, 64 + 32 * side:96 + 32 * side]), T.em[:, 512 * side:512 * side + 512], MUL)
-        mm(["b1k", "gm%d" % j], "m0", T.m0[:], T.b1k[:], T.gm[:, 512 * j:512 * j + 512], False, j == 2)
+        tt([src, "pl", "em"], ["gm%d" % j], T.gm[:, 512 * j:512 * j + 512],
+           M[src].indirect(T.pl[:, 32 * side:32 + 32 * side]), T.em[:, 512 * side:512 * side + 512], MUL)
+        mm(["b1k", "gm%d" % j], "p3", T.p3[:], T.b1k[:], T.gm[:, 512 * j:512 * j + 512], False, j == 3)
 
     def idle2():
-        mm(["onef", "krow"], "m0", T.m0[:], T.onef[0:1, :], T.krow[0:1, :], True, False)
-        ts(["cf"], ["ct15"], ct(15), cf(0), cf(6), ADD)
-        ts(["nrow", "cf"], ["ohs"], T.oh[:, 4:8], T.nrow[:, 96:100], cf(5), EQ)
-        ts(["nrow", "cf"], ["ohb"], T.oh[:, 8:24], T.nrow[:, 96:112], cf(1), EQ, BIG, MUL)
-        tt(["xp", "pl0", "xbk"], ["dall"], T.dall[:], T.xp[:].indirect(T.pl[:, 0:32]), T.xbk[:], SUB)
+        mm(["onef", "krow"], "p3", T.p3[:], T.onef[0:1, :], T.krow[0:1, :], True, False)
+        ts(["nrow", "ct16"], ["oh"], T.oh[:], T.nrow[:, 0:16], ct(16), EQ, BIG, MUL)
         blocked(0, "mf1", 0)
-        for s in range(4):
-            ts(["rv2", "ct15", "ohs"], ["xm%d" % s], T.xm[:, 128 * s:128 * s + 128], T.rv2[:], ct(15), EQ, T.oh[:, 4 + s:5 + s], MUL)
-        lastw["xm"] = lastw["xm3"]
+        blocked(1, "fi1", 1)
+        tt(XB + ["lb", "pai"], ["dall"], T.dall[:], T.xb[:].indirect(T.lb[:]), T.pai[:], SUB)
 
     def choose(t):
         W, cl = T["w_%d" % t], T["cl%d" % t]
         wo = 16 * (t - 1)
         ko = 4 * (t - 1)
         for r in range(N):
-            mm(["b8", "cl%d" % t, "cla%d" % t, "clb%d" % t], "m0", T.m0[:, 0:8], T.b8[:], cl[:, 8 * r:8 * r + 8], False, r == N - 1)
-        red(["m0"], ["km%d" % t], T.km[:, ko:ko + 1], T.m0[:, 0:8], OP.max)
+            mm(["b8", "cl%d" % t, "clo%d" % t], "p3", T.p3[:, 0:8], T.b8[:], cl[:, 8 * r:8 * r + 8], False, r == N - 1)
+        red(["p3"], ["km%d" % t], T.km[:, ko:ko + 1], T.p3[:, 0:8], OP.max)
         ts(["km%d" % t], ["kn%d" % t], T.km[:, ko + 1:ko + 2], T.km[:, ko:ko + 1], 7, AND)
         ts(["kn%d" % t, "ct14"], ["wl%d" % t], T.wl[:, 2 * t - 2:2 * t - 1], T.km[:, ko + 1:ko + 2], -1.0, MUL, ct(14), ADD)
-        cp(["wl%d" % t, "wv%da" % t] + [x % t for x in ("wb%d", "wn%d", "wv%d", "wz%d", "wy%d", "wd%d")], ["wo%d" % t],
-           T.wo[:, wo:wo + 16], W[:].indirect(T.wl[:, 2 * t - 2:2 * t - 1]))
+        ts(["kn%d" % t], ["kq%d" % t], T.kf[:, 1 + t:2 + t], T.km[:, ko + 1:ko + 2], -128.0, MUL)
+        cp(["wl%d" % t] + [x % t for x in ("wb%d", "wn%d", "wy%d", "wd%d")], ["wo%d" % t],
+           T.wo[:, wo:wo + 16], W[:, 0:40].indirect(T.wl[:, 2 * t - 2:2 * t - 1]))
         w = "wo%d" % t
+        mf, mr = "mf%d" % t, "mr%d" % t
+        fl = T.fl[:, 8 * t - 8:8 * t]
 
         def col(j):
             return T.wo[:, wo + j:wo + j + 1]
-        ts(["asi", w], ["s12a"], T.s12[:, 0:128], T.asi[:, 0:128], col(1), SUB, 32768.0, ADD)
-        ts(["asi", w], ["s12b"], T.s12[:, 128:256], T.asi[:, 128:256], col(2), SUB, 32768.0, ADD)
-        mf, mr = "mf%d" % t, "mr%d" % t
-
-        def sel(tau):
-            ts(["ys", w], ["ysel%d" % tau], T.ysel[:, 144 * tau:144 * tau + 144], T.ys[:], col(3 + tau), MUL)
-        slots(T.rl[:], "rl", [lambda: sel(0), lambda: sel(1)])
-        for tau in range(2):
-            for s in range(4):
-                o = 144 * tau + 3 - s
-                mm(["ysel%d" % tau, "fit%d" % tau], "mb", T.mb[:, 0:128], T.ysel[:, o:o + 128],
-                   T.fit[:, 512 * tau + 128 * s:512 * tau + 128 * s + 128], tau == 0 and s == 0, tau == 1 and s == 3)
-        for j in range(2):
-            act(["xs", w], ["xsd%d" % j], T.xsd[:, 512 * j:512 * j + 512], T.xs[:, 1024 + 512 * j:1536 + 512 * j], bias=col(0))
-        act(["mb"], [mf], T[mf][:], T.mb[:, 0:128], scale=float(t))
-        shift([mf], [(T[mf][:], -SH, "fi%d" % t, "af%d" % t)])
-        for j in range(2):
-            act(TAB + ["rl", w], ["ga0_%d" % j], T.ga[:, 512 * j:512 * j + 512],
-                T.tab[:].indirect(T.rl[:, 32 * j:32 * j + 32]), bias=col(0), scale=-1.0)
-            tt(TAB + ["rl", "xsd%d" % j], ["ner%d" % j], T.ner[:, 512 * j:512 * j + 512],
-               T.tab[:].indirect(T.rl[:, 64 + 32 * j:96 + 32 * j]), T.xsd[:, 512 * j:512 * j + 512], OP.not_equal)
-            packa("p0", gsrc(0), gname(0), (j,), j == 0, j == 1)
-            for c in range(8 + 4 * j, 12 + 4 * j):
-                mm(["zone", "ner%d" % j], "r0", T.r0[:, 0:128], T.zone[:, 15 - c:143 - c],
-                   T.ner[:, 128 * (c - 8):128 * (c - 7)], c == 8, False)
-        tt(["p0", "xpk2"], ["ne0"], T.ne[:, 0:512], T.p0[:], T.xpk[:, 1024:1536], OP.not_equal)
-        for s in range(4):
-            mm(["yr", "ne0"], "r0", T.r0[:, 0:128], T.yr[:, 3 - s:131 - s], T.ne[:, 128 * s:128 * s + 128], False, s == 3)
-        act(["r0", w], [mr], T[mr][:], T.r0[:, 0:128], ACT.Relu, bias=col(5), scale=-float(t))
+        ts(["c8", "kq%d" % t], ["fl%d" % t], fl, T.c8[:], T.kf[:, 1 + t:2 + t], ADD)
+        for h in (1, 0):
+            for j in range(2):
+                ts(["q0", w], ["s12%s%d" % ("ab"[j], h)], T.s12[:, 128 * h + 64 * j:128 * h + 64 * j + 64],
+                   T.q0[:, 128 * j + 64 * h:128 * j + 64 * h + 64], col(1 + j), SUB)
+        act(["fit%d" % d for d in range(8)] + ["fl%d" % t, w], [mf], M[mf], T.fit[:].indirect(fl), scale=col(3))
+        shift([mf], [(M[mf], -SH, M["fi%d" % t], "fi%d" % t, "af%d" % t)])
+        for a, b in zip(slots(1, T.rl, "rl"), slots(0, T.rl, "rl")):
+            a()
+            b()
+        for q, h in (("S", 1), ("V", 0)):
+            for a in (1024 * h, 1024 * h + 512):
+                look(q, 0, a, a + 512, lambda a, b: T.rl[:, a:b], ["rl%d" % h], col(0), w)
+        for blocks in (range(4), range(4, 8)):
+            words("q2", gsrc(0), gname(0), 1, "pk", False, blocks)
+            words("q1", gsrc(0), gname(0), 0, "pk", False, blocks)
+        compare("S", "q2", 0, 1)
+        compare("V", "q1", 0, 0)
+        misses("p0", 0, [] if t == 1 else ["cs1"])
+        act(["p0", w], [mr], T[mr][:], T.p0[:, 0:128], ACT.Relu, bias=col(3), scale=-float(t))
         if t == 1:
-            shift([mr], [(T[mr][:], SH, "ri1", "ar1"), (T[mr][:], 2 * SH, "rj1", "aj1")])
+            shift([mr], [(T[mr][:], SH, M["ri1"], "ri1", "ar1"), (T[mr][:], 2 * SH, M["rj1"], "rj1", "aj1")])
         else:
-            shift([mr], [(T[mr][:], SH, "ri2", "ar2")])
+            send(mr, SH, "ri2", "ar2")
         ts(["km%d" % t], ["ko%d" % t], T.km[:, ko + 2:ko + 3], T.km[:, ko:ko + 1], 3, SHR)
-        cp([w], ["yw%d" % t], T.ywo[:, t - 1:t], col(6))
+        cp([w], ["yw%d" % t], T.ywo[:, t - 1:t], col(4))
         ts(["ko%d" % t], ["yx%d" % t], T.ywo[:, 1 + t:2 + t], T.km[:, ko + 2:ko + 3], -1.0, ADD)
 
-    lists_front(1)
+    put(4)
+    put(5)
+    front(1)
+    first_lists(put)
     main(1)
-    prep2(1)
+    choices(1)
     idle1()
     choose(1)
     idle2()
 
-    tt(["fi1", "ri1"], ["cov"], T.cov[:], T.fi1[:], T.ri1[:], ADD)
+    for k, m in enumerate(("fi1", "ri1")):
+        mm([m, "idb"], "p1", T.p1[:, 0:128], T.idb[:], M[m], k == 0, k == 1)
+    blocked(2, "rj1", 0)
+    blocked(3, "ri1", 1)
     for c in range(16):
-        act(["cov", "ohb"], ["in1_%d" % c], T.in1[:, 128 * c:128 * c + 128], T.cov[:], scale=T.oh[:, 8 + c:9 + c])
-    blocked(1, "rj1", 0)
-    blocked(2, "cov", 1)
-    red(["m0"], ["kf"], T.kf[:, 0:1], T.m0[:], OP.min)
+        act(["p1", "oh"], ["in1_%d" % c], T.in1[:, 128 * c:128 * c + 128], T.p1[:, 0:128], scale=T.oh[:, c:c + 1])
+    act(["p1"], ["cov"], T.cov[:], T.p1[:, 0:128])
+
+    def mark(j):
+        tt(["own%d" % (j // 4), XB[j // 2], "in1_%d" % (2 * j), "in1_%d" % (2 * j + 1)], TAB,
+           T.tab[:].indirect(T.own[:, 16 * j:16 * j + 16]), T.xb[:, 256 * j:256 * j + 256], T.in1[:, 256 * j:256 * j + 256], ADD)
+
+    mark(0)
+    red(["p3"], ["kf"], T.kf[:, 0:1], T.p3[:], OP.min)
     o2 = S2 * rank
     ts(["kf"], ["kl"], T.kl[:, 0:1], T.kf[:, 0:1], 511.0, OP.min)
     ts(["kf"], ["la2b"], T.la2[:, o2 + 3:o2 + 4], T.kf[:, 0:1], 512.0, OP.is_lt)
-    cp(["dall", "kl"], ["la2a"], T.la2[:, o2 + 4:o2 + 20], T.dall[:].indirect(T.kl[:, 0:1]))
+    ts(["dall", "kl"], ["la2a"], T.la2[:, o2 + 4:o2 + 20], T.dall[:].indirect(T.kl[:, 0:1]), -1.0, MUL)
     gather_all(["la2a", "la2b"], "al2", T.la2[:, o2 + 3:o2 + 5], "la2")
-    for j in range(4):
-        tt(["own", XB[j]] + ["in1_%d" % c for c in range(4 * j, 4 * j + 4)], TAB,
-           T.tab[:].indirect(T.own[:, 32 * j:32 * j + 32]), T.xb[:, 512 * j:512 * j + 512], T.in1[:, 512 * j:512 * j + 512], ADD)
+    send("cov", -SH, "cs1", "acs")
 
-    lists_front(2)
+    for j in range(1, 6):
+        mark(j)
+    front(2)
+    first_lists(mark)
     main(2)
-    prep2(2)
+    choices(2)
     ts(["cov"], ["c1"], T.c1[:], T.cov[:], 1.0, OP.min)
-    ts(["c1"], ["lim"], T.lim[:], T.c1[:], -1.0, MUL, 2.0, ADD)
     choose(2)
     dma("y", "dz", ["yw1", "yw2", "yx1", "yx2"], [], T.yw[:], T.ywo[0:128:16, :])
-    tt(["fi2", "lim"], ["ta", "b2a"], T.ta[:], T.fi2[:], T.lim[:], OP.min)
-    tt(["ta", "c1"], ["ta2"], T.yo[:], T.ta[:], T.c1[:], OP.max)
-    tt(["ri2", "lim"], ["tb"], T.tb[:], T.ri2[:], T.lim[:], OP.min)
-    tt(["ta2", "tb"], ["yo"], T.yo[:], T.yo[:], T.tb[:], OP.max)
-    dma("y", "dy", ["yo"], [], T.yc[:], T.yo[:])
+    tt(["fi2", "c1"], ["ta", "b2a"], T.ta[:], T.fi2[:], T.c1[:], OP.max)
+    tt(["ta", "ri2"], ["yo"], T.yo[:], T.ta[:], T.ri2[:], OP.max)
+    dma("y", "dy", ["yo"], [], T.yc[:, 0:1024], T.yo[0:128:2, :])
+    dma("s", "dy2", ["yo"], [], T.yc[:, 1024:2048], T.yo[1:128:2, :])
     for s, v in cnt.items():
         if max([x for (q, n), x in waited.items() if n == s] + [0]) < v:
             need("y", [(s, v)])

@@ -3,26 +3,36 @@ from concourse.mybir import AluOpType, AxisListType, ActivationFunctionType
 
 N, SH, NV, NP = 8, 3, 2048, 512
 TW = 12288
-BIG = float(2 ** 26)
+BIG = float(2 ** 52)
 EMPTY = 2 ** 23
 S1, S2 = 32, 24
 QOFF = 137
 
-SCALAR = "g00 g10 c00 g20 c10 c40 g30 c20 c50 g01 c30 g11 c01 g21 c11 n4 n0 g70 c21 n5 n1 c31 c70 n6 n2 n3 n7".split()
-VECTOR = "L g40 g50 g60 g41 c60 g51 c41 g61 c51 g31 c61 g71 c71".split()
-COST = {"g": 1.4, "c": 0.33, "n": 0.13, "L": 2.6, "m": 0.22, "w": 0.22, "s": 0.38}
+SCALAR = ("g00 g01 g10 c00 c80 c01 g20 c81 g11 g21 c10 c20 c11 c31 g30 c21 n4 n0 c30 g70 n1 n2 n3 c70 n5 n6 n7".split(),
+          "g00 g01 c00 c01 g10 g11 c10 g20 g21 c11 n0 n4 c20 c21 g30 c31 c30 g70 n3 n1 n2 c70 n5 n6 n7".split())
+VECTOR = ("L g40 g41 g50 c40 c41 g31 c50 g51 g60 g61 g71 c51 c60 c61 c71".split(),
+          "L g40 g41 c40 g50 c41 g31 g51 g60 c50 g61 g71 c51 c60 c61 c71".split())
+DEEP = "456"
+COST = {"g": 1.4, "c": 0.33, "n": 0.13, "L": 3.0, "m": 0.22, "w": 0.22, "s": 0.38}
+NW, NS = 5, 3
 LAG, YIELD = 0.1, 0.3
 
 
-def timetable():
+def cost(x):
+    if x[1:2] == "8":
+        return {"m": COST["m"], "w": 0.0, "c": 0.5 * COST["c"]}[x[0]]
+    return COST[x[0]] * ({"w": 2.0, "c": 0.5, "s": 0.6}.get(x[0], 1.0) if x != "L" and x[1] in DEEP else 1.0)
+
+
+def timetable(t):
     end, order, free = {}, [], {"S": 0.0, "V": 0.0, "P": 0.0}
-    left = {"S": list(SCALAR), "V": list(VECTOR)}
+    left = {"S": list(SCALAR[t - 1]), "V": list(VECTOR[t - 1])}
     guess = {}
     for q in left:
-        t = 0.0
+        at = 0.0
         for x in left[q]:
-            guess[x] = t
-            t += COST[x[0]]
+            guess[x] = at
+            at += cost(x)
     turns = sorted((x[1:] for x in guess if x[0] == "c"), key=lambda x: guess["c" + x])
     sums = sorted("01234567", key=lambda d: max(guess["c" + d + "0"], guess["c" + d + "1"]))
     left["P"] = ["m" + x for x in turns] + ["w" + x for x in turns] + ["s" + d for d in sums]
@@ -30,12 +40,17 @@ def timetable():
     def after(x):
         k, y = x[0], x[1:]
         if k == "g":
-            return [] if y[0] in "01" else ["L"]
+            return [] if y[0] == "0" else ["L"]
         if k == "m":
-            return ["c" + turns[turns.index(y) - 4]] if turns.index(y) >= 4 else []
+            n = turns.index(y)
+            return ["c" + turns[n - NW]] if n >= NW else ["L"] if n >= 4 else []
         if k == "s":
-            return ["c" + y + "0", "c" + y + "1"] + (["n" + sums[sums.index(y) - 4]] if sums.index(y) >= 4 else [])
-        return {"w": ["g" + y, "m" + y], "c": ["w" + y], "n": ["s" + y], "L": []}[k]
+            return ["c" + y + "0", "c" + y + "1"] + (["n" + sums[sums.index(y) - NS]] if sums.index(y) >= NS else [])
+        if k == "c":
+            return ["w" + y] + (["c8" + y[1]] if t == 1 and y[0] in DEEP else [])
+        if k == "w":
+            return ["m" + y] + (["g" + y] if y[0] != "8" else [])
+        return ["s" + y] if k == "n" else []
     while any(left.values()):
         ready = []
         for q in left:
@@ -45,7 +60,7 @@ def timetable():
                     ready.append((at + (YIELD if x[0] == "s" else 0.0), at, q, x))
         _, at, q, x = min(ready)
         left[q].remove(x)
-        free[q] = end[x] = at + COST[x[0]]
+        free[q] = end[x] = at + cost(x)
         order.append((q, x))
     return order, turns, sums
 
@@ -57,7 +72,9 @@ def _sb(n, dt):
 B16, F32, I32, U16, F16 = "bfloat16", "float32", "int32", "uint16", "float16"
 SCRATCH = {
     "tab": _sb(TW, B16), "xi": _sb(NV, I32), "xb": _sb(NV, B16), "ga": _sb(8 * NV, B16), "ne": _sb(8 * 768, B16),
-    "xp": _sb(NV, B16), "xs": _sb(NV, B16), "dbc": _sb(1024, B16), "zone": _sb(144, B16), "zw": _sb(288, B16),
+    "xp": _sb(NV, B16), "xs": _sb(NV, B16), "dbc": _sb(512, B16), "dc": _sb(16, B16), "rb": _sb(24, F32),
+    "zone": _sb(144, B16), "zw": _sb(288, B16),
+    "pkl": _sb(24, B16), "pkh": _sb(24, B16), "nph": _sb(24, B16), "xl": _sb(384, F32),
     "npk": _sb(48, B16), "na": _sb(256, B16), "rr": _sb(256, B16), "ff": _sb(256, B16),
     "nn": _sb(2048, B16), "u1": _sb(1024, F32), "mm": _sb(1024, I32), "kk": _sb(1024, I32), "hh": _sb(1024, F32),
     "lst": _sb(1024, U16), "in1": _sb(NV, B16), "fit": _sb(1024, B16),
@@ -74,7 +91,7 @@ SCRATCH = {
     "w_1": _sb(40, F32), "w_2": _sb(40, F32), "wo": _sb(32, F32), "km": _sb(8, I32), "wl": _sb(4, U16),
     "fl": _sb(16, U16), "mf2": _sb(128, B16), "mr1": _sb(128, B16), "mr2": _sb(128, B16), "fi2": _sb(128, B16),
     "ri2": _sb(128, B16), "cov": _sb(128, B16), "cs1": _sb(128, B16), "pt": _sb(128, I32), "pl": _sb(128, U16),
-    "pai": _sb(512, B16), "dall": _sb(512, B16), "em": _sb(1024, B16), "gm": _sb(2048, B16),
+    "pai": _sb(1024, B16), "dall": _sb(512, B16), "em": _sb(1024, B16), "gm": _sb(2048, B16),
     "kf": _sb(4, F32), "kl": _sb(2, U16), "c1": _sb(128, F32), "ta": _sb(128, F32), "yo": _sb(128, F32), "ywo": _sb(4, F32),
 }
 WB = ("q0", "q1", "q2", "q3")
@@ -154,9 +171,7 @@ def rank_program(g, core, T, topo):
             if x in BANKS:
                 toks += [t for t in reads.get(x, []) if t[0] != "q" + q]
         for x in w:
-            if x in lastw:
-                toks.append(lastw[x])
-            toks += reads.get(x, [])
+            toks += reads.get(x, []) + ([lastw[x]] if x in lastw else [])
         if q == "p":
             toks = [t for t in toks if t[0] != "qp"]
         need(q, toks)
@@ -224,8 +239,7 @@ def rank_program(g, core, T, topo):
             out.append((m, far))
             used = m
         if near:
-            es = [e for e in topo.engines(c, cores[near[0]]) if not used >> e & 1]
-            out.append((sum(1 << e for e in es[0:3:2]), near))
+            out.append((topo.mask(c, cores[near[0]]) & ~used, near))
         return out
 
     def dst_id(d):
@@ -320,117 +334,144 @@ def rank_program(g, core, T, topo):
     iota(["pf"], T.pf[:], [[0, 1]], 0, 1)
     iota(["nrow"], T.nrow[:], [[1, 144]], 0, 0)
     iota(["rv1"], T.rv1[:], [[1, 8], [0, 16]], 0, 0)
-    fill([TAB[0]], part(0), float(EMPTY))
-    for j in (2, 3, 4):
-        act([TAB[0]], [TAB[j]], part(j), part(0))
+    VF, GF, G0 = 3840, 2176, 448
+
+    def blank(k, a, b):
+        return lambda: fill(["tabv%d" % k], T.tab[:, a:b], float(EMPTY))
+    iota([TAB[4]], T.tab[:, TW - GF:TW - GF + G0], [[0, G0]], EMPTY, 0)
+    fill([TAB[0]], T.tab[:, 0:512], float(EMPTY))
+    act([TAB[0]], [TAB[1]], T.tab[:, VF:VF + 512], T.tab[:, 0:512])
+    blank(0, 512, 1536)()
+    for k, a in enumerate(range(VF + 512, TW - GF, 1536)):
+        b = min(a + 1536, TW - GF)
+        act([TAB[0], "tabv0"], ["tabs%d" % k], T.tab[:, a:b], T.tab[:, 0:b - a])
     for j, (a, op, b) in enumerate([(15, AND, None), (4, SHR, None), (1, SHR, 7), (1, AND, None)]):
         ts(["pcol"], ["ci%d" % j], T.ci[:, j:j + 1], T.pcol[:], a, op, b, None if b is None else AND)
     fill(["ones"], T.ones[:], 1.0)
     cp(["ci%d" % j for j in range(4)], ["cf"], T.cf[:, 0:4], T.ci[:, 0:4])
     fill(["crow"], T.crow[0:1, :], 4096.0 * QOFF)
-    ts(["cf"], ["i3"], T.i3[:], cf(0), -1.0, ADD, 1.0 / 3.0, MUL)
-    ts(["nrow", "cf"], ["gs"], T.gs[:], T.nrow[:, 0:8], cf(1), EQ)
-    ts(["i3", "cf"], ["ct2"], ct(2), T.i3[:], 8.0, MUL, cf(1), ADD)
-    ts(["i3", "cf"], ["ct3"], ct(3), T.i3[:], -3.0, MUL, cf(0), ADD)
     ts(["cf"], ["ct4"], ct(4), cf(1), 16.0, MUL, 15.0, ADD)
-    ts(["nrow", "pf"], ["idb"], T.idb[:], T.nrow[:, 0:128], T.pf[:], EQ)
+    blank(1, 1536, 2560)()
     ts(["nrow", "ct4"], ["zone"], T.zone[:], T.nrow[:], ct(4), EQ)
-    ts(["ct3"], ["ct6"], ct(6), ct(3), 1.0, GE, 255.0, MUL)
-    ts(["ct3"], ["ct7"], ct(7), ct(3), 2.0, GE, 65280.0, MUL)
     cp(["ew"], ["wf0"], T.wf[:, 0:2], T.ew[:, 0:2])
     cp(["ew"], ["l0"], T.l0[:], T.ew[:, 2:6])
     shift(["wf0", "l0"], [(T.wf[:, 0:2], -SH, T.es[:], "es", "aes"), (T.l0[:], -SH, T.el[:], "el", "ael")])
     shift(["wf0"], [(T.wf[:, 0:2], SH, T.ep[:], "ep", "aep")])
-    iota([TAB[5]], part(5), [[0, 2048]], EMPTY, 0)
-    ts(["ct6", "ct7"], ["ct10"], ct(10), ct(6), ct(7), ADD, 1.0, ADD)
-    ts(["nrow", "ct2", "ct10"], ["pk"], T.pk[:], T.nrow[:, 0:48], ct(2), EQ, ct(10), MUL)
-    ts(["wf0"], ["wf2"], T.wf[:, 2:4], T.wf[:, 0:2], -1.0, MUL)
+    iota([TAB[5]], T.tab[:, TW - GF + G0:TW], [[0, GF - G0]], EMPTY, 0)
     for j in range(2):
         ts(["zone", "wf0"], ["zw%d" % j], T.zw[:, 144 * j:144 * j + 144], T.zone[:], wf(j), MUL)
-    fill([TAB[1] + "a"], T.tab[:, 2048:3072], float(EMPTY))
+    blank(2, 2560, VF - 384)()
     cast(0)
-    cp(["pbi"], ["lb"], T.lb[:], T.pbi[:])
-    ts(["rv1", "cf"], ["bm"], T.bm[:], T.rv1[:], cf(1), EQ)
-    fill([TAB[1]], T.tab[:, 3072:4096], float(EMPTY))
-    cast(1)
+    later = [
+        lambda: ts(["cf"], ["i3"], T.i3[:], cf(0), -1.0, ADD, 1.0 / 3.0, MUL),
+        lambda: ts(["nrow", "cf"], ["gs"], T.gs[:], T.nrow[:, 0:8], cf(1), EQ),
+        lambda: cp(["pbi"], ["lb"], T.lb[:], T.pbi[:]),
+        lambda: ts(["i3", "cf"], ["ct3"], ct(3), T.i3[:], -3.0, MUL, cf(0), ADD),
+        lambda: ts(["nrow", "pf"], ["idb"], T.idb[:], T.nrow[:, 0:128], T.pf[:], EQ),
+        lambda: ts(["i3", "cf"], ["ct2"], ct(2), T.i3[:], 8.0, MUL, cf(1), ADD),
+        lambda: ts(["ct3"], ["ct6"], ct(6), ct(3), 1.0, GE, 255.0, MUL),
+        lambda: ts(["ct3"], ["ct7"], ct(7), ct(3), 2.0, GE, 65280.0, MUL),
+        blank(3, VF - 384, VF),
+        lambda: ts(["ct6", "ct7"], ["ct10"], ct(10), ct(6), ct(7), ADD, 1.0, ADD),
+        lambda: ts(["wf0"], ["wf2"], T.wf[:, 2:4], T.wf[:, 0:2], -1.0, MUL),
+        lambda: ts(["nrow", "ct2", "ct10"], ["pk"], T.pk[:], T.nrow[:, 0:48], ct(2), EQ, ct(10), MUL),
+        lambda: ts(["rv1", "cf"], ["bm"], T.bm[:], T.rv1[:], cf(1), EQ),
+        lambda: ts(["nrow", "pf"], ["idh"], T.idh[:], T.nrow[:, 0:128], T.pf[:], EQ)]
 
-    def own_sums(h):
+    SETS = ((0, 32), (32, 64), (64, 128))
+
+    def own_sums(k, bank, alone=True):
+        a, b = SETS[k]
         for j in range(2):
             for r in range(16):
                 o = 144 * j + 15 - r
-                mm(XB[2 * h:2 * h + 2] + ["zw%d" % j], PB[h], T[PB[h]][:, 64 * j:64 * j + 64], T.zw[:, o:o + 128],
-                   T.xb[:, 1024 * h + r:1024 * h + 1024:16], j == 0 and r == 0, j == 1 and r == 15)
+                mm(XB[a // 32:b // 32] + ["zw%d" % j], bank, T[bank][:, (b - a) * j:(b - a) * (j + 1)], T.zw[:, o:o + 128],
+                   T.xb[:, 16 * a + r:16 * b:16], alone and j == 0 and r == 0, alone and j == 1 and r == 15)
 
     def sums(bank, s, stop=True):
         for r in range(16):
             mm(XB + ["wm%d0" % s, "wm%d1" % s], bank, T[bank][:, r:256:16], T.xb[:, r::16], T.wm[:, 16 * s:16 * s + 16],
                r == 0, stop and r == 15)
 
-    def words(bank, src, name, h, pk, first, blocks=range(8)):
+    def words(bank, src, name, h, pk, first, last, blocks=range(8)):
         for b in blocks:
             o = 1024 * h + 128 * b
-            mm(name(o) + [pk], bank, T[bank][:, b:384:8], src(o), T[pk][:], first and b == 0, not first and b == 7)
+            mm(name(o) + [pk], bank, T[bank][:, b:8 * T[pk].shape[1]:8], src(o), T[pk][:], first and b == 0, last and b == 7)
 
-    def slots(h, out, name):
-        a, m, b = 128 * h, 128 * h + 64, 128 * h + 128
-        c = slice(64 * h, 64 * h + 64)
-        return [lambda: ts(["s12a%d" % h, "s12b%d" % h], ["u12%d" % h], T.u12[:, a:b], T.s12[:, a:b], 4095, AND),
-                lambda: tt(["u12%d" % h], ["m1%d" % h], T.m1[:, c], T.u12[:, a:m], T.u12[:, m:b], MUL),
-                lambda: ts(["m1%d" % h], ["k1%d" % h], T.k1[:, c], T.m1[:, c], 5, SHR, 8191, AND),
-                lambda: tt(["k1%d" % h, "u12%d" % h], ["h1%d" % h], T.h1[:, c], T.k1[:, c], T.u12[:, m:b], ADD),
-                lambda: cp(["h1%d" % h], [name + str(h)], out[:, c], T.h1[:, c])]
+    def slots(a, b, out, name):
+        k = str(a)
+        return [lambda: ts(["s12a" + k, "s12b" + k], ["u12" + k], T.u12[:, 2 * a:2 * b], T.s12[:, 2 * a:2 * b], 4095, AND),
+                lambda: tt(["u12" + k], ["m1" + k], T.m1[:, a:b], T.u12[:, 2 * a:a + b], T.u12[:, a + b:2 * b], MUL),
+                lambda: ts(["m1" + k], ["k1" + k], T.k1[:, a:b], T.m1[:, a:b], 5, SHR, 8191, AND),
+                lambda: tt(["k1" + k, "u12" + k], ["h1" + k], T.h1[:, a:b], T.k1[:, a:b], T.u12[:, a + b:2 * b], ADD),
+                lambda: cp(["h1" + k], [name + k], out[:, a:b], T.h1[:, a:b])]
 
-    def own_slots(h):
-        cp([PB[h]], ["s12a%d" % h, "s12b%d" % h], T.s12[:, 128 * h:128 * h + 128], T[PB[h]][:, 0:128])
-        return slots(h, T.own, "own")
+    def own_slots(k):
+        a, b = SETS[k]
+        return [lambda: cp([PB[k]], ["s12a%d" % a, "s12b%d" % a], T.s12[:, 2 * a:2 * b], T[PB[k]][:, 0:2 * (b - a)])
+                ] + slots(a, b, T.own, "own")
 
-    def put(j):
-        cp(["own%d" % (j // 4), XB[j // 2]], TAB + [TAB[1] + "a"], T.tab[:].indirect(T.own[:, 16 * j:16 * j + 16]),
-           T.xb[:, 256 * j:256 * j + 256])
+    def put(a, b):
+        cp(["own%d" % x for x, y in SETS if 16 * x < b and a < 16 * y] + XB[a // 512:(b + 511) // 512],
+           TAB + ["tab%s%d" % (q, k) for q in "vs" for k in range(4)], T.tab[:].indirect(T.own[:, a // 16:b // 16]), T.xb[:, a:b])
 
-    own_sums(0)
-    ts(["nrow", "pf"], ["idh"], T.idh[:], T.nrow[:, 0:128], T.pf[:], EQ)
-    cast(2)
-    steps = own_slots(0)
-    steps[0]()
-    steps[1]()
-    cast(3)
-    for step in steps[2:]:
+    def between(steps, scatter, a, b, n=64):
+        cuts = [a] + [b - n * k for k in range(len(steps) - 1, -1, -1)]
+        for k, step in enumerate(steps):
+            scatter(cuts[k], cuts[k + 1])
+            step()
+
+    own_sums(0, "p0")
+    for step in later[:8]:
         step()
-    put(0)
+    cast(1)
+    own_sums(1, "p1")
+    one, two = own_slots(0), own_slots(1)
+    for step in (one[0], later[8], one[1], later[9], later[10], one[2], lambda: cast(2), one[3], later[11], later[12], one[4],
+                 two[0], one[5], two[1], lambda: cast(3), two[2], lambda: put(0, 128), two[3], later[13],
+                 lambda: put(128, 256), two[4], lambda: put(256, 384), two[5]):
+        step()
     for j in range(2):
         act(["gs", "es"], ["wm0%d" % j], T.wm[:, 8 * j:8 * j + 8], T.gs[:], scale=T.es[:, j:j + 1])
     o1 = S1 * rank
     act(XB + ["lb"], ["la1a"], T.la1[:, o1 + 15:o1 + 31], T.xb[:].indirect(T.lb[:, 0:1]), scale=-1.0)
     act(XB + ["el", "la1a"], ["la1b"], T.la1[:, o1 + 16:o1 + 32], T.xb[:].indirect(T.el[:, 0:1]))
-    gather_all(["la1a", "la1b"], "al1", T.la1[:, o1 + 15:o1 + 17], "la1")
     hand(XB, T.xb[:, 1024:2048], "hx1")
+    gather_all(["la1a", "la1b"], "al1", T.la1[:, o1 + 15:o1 + 17], "la1")
     act(["idb"], ["idq"], T.idq[:], T.idb[:], scale=-4096.0)
     sums("q0", 0)
     sums("q1", 0, False)
     act(["q0"], ["na"], T.na[:], T.q0[:, 0:256], bias=QOFF + 0.5 / 4096, scale=1.0 / 4096)
     mm(["na", "idq"], "q1", T.q1[:, 0:256], T.idq[:], T.na[:], False, True)
-    own_sums(1)
+    own_sums(2, "p2")
+    mm(["ones", "crow"], "p3", T.p3[:, 0:128], T.ones[0:1, :], T.crow[0:1, 0:128], True, False)
+    own_sums(2, "p3", False)
     ts(["q1"], ["ao"], T.ao[:], T.q1[:, 0:256], 4096.0 * QOFF, ADD)
     send("ao", SH, "ah", "aah")
     shift(XB, [(T.xb[:, 0:1024], SH, T.xp[:, 0:1024], "xp0", "axp0")])
     hand(XB, T.xb[:, 0:1024], "hx0")
-    put(1)
-    steps = own_slots(1)
-    put(2)
-    steps[0]()
-    steps[1]()
-    put(3)
-    for step in steps[2:]:
-        step()
     for j in range(2):
         act(["gs", "ep"], ["wm1%d" % j], T.wm[:, 16 + 8 * j:24 + 8 * j], T.gs[:], scale=T.ep[:, j:j + 1])
     for j in range(2):
         act(["bm", "wf2"], ["nw%d" % j], T.nw[:, 128 * j:128 * j + 128], T.bm[:], scale=wf(2 + j))
     act(["pk"], ["npk"], T.npk[:], T.pk[:], scale=-1.0)
+    for w in range(3):
+        lo, hi, o = T.pk[:, 16 * w:16 * w + 8], T.pk[:, 16 * w + 8:16 * w + 16], slice(8 * w, 8 * w + 8)
+        act(["pk"], ["pkl%d" % w], T.pkl[:, o], lo)
+        act(["pk"], ["pkh%d" % w], T.pkh[:, o], hi, scale=2.0 ** 24)
+        act(["pk"], ["nph%d" % w], T.nph[:, o], hi, scale=-2.0 ** 24)
+    for x in ("pkl", "pkh", "nph"):
+        lastw[x] = lastw["nph2"]
     act(["idb"], ["idf"], T.idf[:], T.idb[:])
     act(["bm"], ["b8"], T.b8[:], T.bm[:], scale=8.0)
     act(["bm"], ["b1k"], T.b1k[:], T.bm[:], scale=1024.0)
+    act(["p2"], ["nn0_0"], T.nn[:, 0:128], T.p2[:, 0:128], bias=QOFF + 0.5 / 4096 - 0.5, scale=1.0 / 4096)
+    mm(["nn0_0", "idq"], "p3", T.p3[:, 0:128], T.idq[:], T.nn[:, 0:128], False, True)
+    act(["p3"], ["u10"], T.u1[:, 0:64], T.p3[:, 0:64])
+    between([lambda: tt(["u10", "p3"], ["m164"], T.m1[:, 64:128], T.u1[:, 0:64], T.p3[:, 64:128], MUL),
+             lambda: ts(["m164"], ["k164"], T.k1[:, 64:128], T.m1[:, 64:128], 5, SHR, 8191, AND),
+             lambda: tt(["k164", "p3"], ["h164"], T.h1[:, 64:128], T.k1[:, 64:128], T.p3[:, 64:128], ADD),
+             lambda: cp(["h164"], ["own64"], T.own[:, 64:128], T.h1[:, 64:128])], put, 384, 1024, 32)
     sums("q2", 1)
     act(["q2"], ["aso"], T.aso[:], T.q2[:, 0:256])
     hand(["aso"], T.aso[:], "has")
@@ -440,79 +481,95 @@ def rank_program(g, core, T, topo):
     def const(c):
         mm(["ones", "crow"], PB[c], T[PB[c]][:, 256:512], T.ones[0:1, :], T.crow[0:1, :], True, False)
 
-    def apart(bank, start, stop):
-        for k in range(4):
-            o = 128 * (k // 2)
-            mm(["ah", "idh"], bank, T[bank][:, 128 * k:128 * k + 128], T.ah[:, o:o + 128], T.idh[:], start and k == 0, stop and k == 3)
-
-    def bpart(bank, c, start, stop):
-        for j in range(2):
-            mm(["nw%d" % j] + DBC[2 * c:2 * c + 2], bank, T[bank][:, 256 * j:256 * j + 256],
-               T.nw[:, 128 * j:128 * j + 128], T.dbc[:, 256 * c:256 * c + 256], start and j == 0, stop and j == 1)
+    def apart(bank, order, first):
+        for k, u in enumerate(order):
+            mm(["ah", "idh"], bank, T[bank][:, 128 * k:128 * k + 128], T.ah[:, 128 * u:128 * u + 128], T.idh[:],
+               first and k == 0, first and k == len(order) - 1)
 
     def front(t):
+        if t == 1:
+            k = S1 * (N - SH) + 16
+            cols = [(T.dc[:, 0:SH], T.la1[:, k::S1]), (T.dc[:, SH:N], T.la1[:, 16:k:S1]), (T.dc[:, N:2 * N], T.la1[:, 15::S1])]
+            src = ["la1", "la1a", "la1b"]
+        else:
+            cols, src = [(T.dc[:, 0:N], T.la2[:, 4::S2])], ["la2", "la2a"]
+
+        def sides():
+            apart("q0", (0, 1), True)
+
+        def offers():
+            for k, (out, in_) in enumerate(cols):
+                act(src, ["dc%d" % k], out, in_)
+            parts = range(3 - t)
+            for u in range(2):
+                for k in parts:
+                    mm(["nw%d" % u, "dc0", "dc1", "dc2"], "q1", T.q1[:, 8 * u:8 * u + 8], T.nw[:, 128 * u:128 * u + 128],
+                       T.dc[:, N * k:N * k + N], u == 0 and k == 0, u == 1 and k == parts[-1])
+
+        def biases():
+            act(["q1"], ["rb"], T.rb[:, 0:16], T.q1[:, 0:16], bias=QOFF + 0.5 / 4096 - 0.5, scale=1.0 / 4096)
+            act(["q1"], ["ob"], T.rb[:, 16:24], T.q1[:, 0:8], bias=4096.0 * QOFF)
+            act(["q1"], ["wb%d" % t], T["w_%d" % t][:, 8:24], T.q1[:, 0:16], bias=-32768.0)
+
         def spread(c):
             for d in (2 * c, 2 * c + 1):
-                out = T.dbc[:, 128 * d:128 * d + 128]
+                out = T.dbc[:, 64 * d:64 * d + 64]
                 if t == 1:
                     a, b = S1 * ((d - SH) % N) + 16, S1 * d + 15
-                    act(["la1", "la1a", "la1b", "ones"], [DBC[d]], out, T.ones[:],
-                        scale=T.la1[:, a:a + 1], bias=T.la1[:, b:b + 1])
+                    act(src + ["ones"], [DBC[d]], out, T.ones[:, 0:64], scale=T.la1[:, a:a + 1], bias=T.la1[:, b:b + 1])
                 else:
                     a = S2 * d + 4
-                    act(["la2", "la2a", "ones"], [DBC[d]], out, T.ones[:], scale=T.la2[:, a:a + 1])
-
-        def side(c):
-            bpart(WB[c], c, t == 1, t == 2)
-            if t == 1:
-                apart(WB[c], False, True)
-
-        def full(c):
-            bpart(PB[c], c, False, False)
-            if t == 1:
-                apart(PB[c], False, False)
+                    act(src + ["ones"], [DBC[d]], out, T.ones[:, 0:64], scale=T.la2[:, a:a + 1])
+            for k in range(4):
+                d = 2 * c + k // 2
+                mm(["nw1", DBC[d]], PB[c], T[PB[c]][:, 256 + 64 * k:320 + 64 * k], T.nw[:, 128:256], T.dbc[:, 64 * d:64 * d + 64],
+                   False, False)
 
         def rem(c):
-            act([WB[c]], ["nn%d" % c], T.nn[:, 512 * c:512 * c + 512], T[WB[c]][:],
-                bias=QOFF + 0.5 / 4096 - 0.5, scale=1.0 / 4096)
-
-        def sub(c):
-            mm(["nn%d" % c, "idq"], PB[c], T[PB[c]][:], T.idq[:], T.nn[:, 512 * c:512 * c + 512], False, True)
+            for k in range(4):
+                u, d, o = k // 2, 2 * c + k % 2, 512 * c + 128 * k
+                act(["q0", "rb"], ["nn%d_%d" % (c, k)], T.nn[:, o:o + 128], T.q0[:, 128 * u:128 * u + 128],
+                    bias=T.rb[:, 8 * u + d:8 * u + d + 1], scale=1.0 / 4096)
+            if t == 1:
+                apart(PB[c], (0, 0, 1, 1), False)
+            mm(["nn%d_%d" % (c, k) for k in range(4)] + ["idq"], PB[c], T[PB[c]][:], T.idq[:], T.nn[:, 512 * c:512 * c + 512],
+               False, True)
 
         def out1(c):
-            act([PB[c]], ["u1%d" % c], T.u1[:, 256 * c:256 * c + 256], T[PB[c]][:, 0:256], bias=4096.0 * QOFF)
+            for k in range(2):
+                d = 2 * c + k
+                act([PB[c], "ob"], ["u1%d" % d], T.u1[:, 128 * d:128 * d + 128], T[PB[c]][:, 128 * k:128 * k + 128],
+                    bias=T.rb[:, 16 + d:17 + d])
 
-        for c in range(4):
-            const(c)
-            if t == 2:
-                apart(WB[c], True, False)
-                apart(PB[c], False, False)
         a, b, c, d = 0, 2, 1, 3
-        spread(a); side(a); full(a)
-        spread(b); side(b)
-        rem(a); sub(a); full(b)
-        spread(c); side(c)
-        out1(a); rem(b); sub(b); full(c)
-        spread(d); side(d)
-        out1(b); rem(c); sub(c); full(d)
-        rem(d); sub(d)
-        out1(c); out1(d)
+        for k in range(4):
+            const(k)
+            if t == 2:
+                apart(PB[k], (0, 0, 1, 1), False)
+        if t == 2:
+            sides()
+        offers()
+        spread(a); spread(b)
+        if t == 1:
+            sides()
+        biases()
+        spread(c)
+        rem(a); spread(d); rem(b); out1(a)
+        rem(c); out1(b); rem(d); out1(c); out1(d)
 
-    def back(c):
-        a, b = 256 * c, 256 * c + 256
-        u2 = T[PB[c]][:, 256:512]
-        return [lambda: tt(["u1%d" % c, PB[c]], ["mm%d" % c], T.mm[:, a:b], T.u1[:, a:b], u2, MUL),
-                lambda: ts(["mm%d" % c], ["kk%d" % c], T.kk[:, a:b], T.mm[:, a:b], 5, SHR, 8191, AND),
-                lambda: tt(["kk%d" % c, PB[c]], ["hh%d" % c], T.hh[:, a:b], T.kk[:, a:b], u2, ADD),
-                lambda: cp(["hh%d" % c], ["lst%d" % c], T.lst[:, a:b], T.hh[:, a:b])]
+    def back(d, e):
+        a, b, bank, k = 128 * d, 128 * e, PB[d // 2], str(d)
+        u2 = T[bank][:, 256 + a % 256:256 + a % 256 + b - a]
+        return [lambda: tt(["u1%d" % x for x in range(d, e)] + [bank], ["mm" + k], T.mm[:, a:b], T.u1[:, a:b], u2, MUL),
+                lambda: ts(["mm" + k], ["kk" + k], T.kk[:, a:b], T.mm[:, a:b], 5, SHR, 8191, AND),
+                lambda: tt(["kk" + k, bank], ["hh" + k], T.hh[:, a:b], T.kk[:, a:b], u2, ADD),
+                lambda: cp(["hh" + k], ["lst%d" % x for x in range(d, e)], T.lst[:, a:b], T.hh[:, a:b])]
 
     def first_lists(scatter):
-        steps = back(0)
-        steps[0]()
-        scatter(6)
-        for x in steps[1:]:
-            x()
-        scatter(7)
+        for k, step in enumerate(back(0, 1)):
+            step()
+            if k < 3:
+                scatter(1856 + 64 * k, 1920 + 64 * k)
 
     def gname(d):
         return lambda o: ["ga%d_%d" % (d, o // 256)]
@@ -529,47 +586,57 @@ def rank_program(g, core, T, topo):
         else:
             ts(r, w, out, src, bias, ADD)
 
-    def minus(bank, ref, h):
-        words(bank, lambda o: T[ref][:, o:o + 128], lambda o: [ref + "%d" % h if ref == "xp" else ref], h, "npk", True)
+    def minus(bank, ref, h, pk="npk", last=False):
+        words(bank, lambda o: T[ref][:, o:o + 128], lambda o: [ref + "%d" % h if ref == "xp" else ref], h, pk, True, last)
 
-    def compare(q, bank, d, h):
+    def compare(q, bank, d, h, deep=False):
         out, w = T.ne[:, 768 * d + h:768 * d + 768:2], ["ne%d_%d" % (d, h)]
-        if q == "S":
+        if deep:
+            tt([bank, "xl%d" % h], w, T.ne[:, 768 * d + h:768 * d + 384:2], T[bank][:, 0:192], T.xl[:, 192 * h:192 * h + 192],
+               OP.not_equal)
+        elif q == "S":
             act([bank], w, out, T[bank][:, 0:384], ACT.Abs)
         else:
             ts([bank], w, out, T[bank][:, 0:384], 0.0, OP.not_equal)
 
-    def misses(bank, d, masks):
+    def misses(bank, d, masks, n=6):
         for k, m in enumerate(masks):
             mm([m, "idb"], bank, T[bank][:, 0:128], T.idb[:], M[m], k == 0, False)
-        for w in range(6):
+        for w in range(n):
             o = 768 * d + 128 * w
             mm(["ne%d_0" % d, "ne%d_1" % d, "idb"], bank, T[bank][:, 0:128], T.ne[:, o:o + 128], T.idb[:],
-               w == 0 and not masks, w == 5)
+               w == 0 and not masks, w == n - 1)
 
     def main(t):
-        order, turns, summed = timetable()
+        order, turns, summed = timetable(t)
         co = 8 * (t - 1)
         for q, step in order:
             k = step[0]
             if k == "L":
-                for steps in zip(back(2), back(1), back(3)):
+                for steps in zip(back(1, 2), back(4, 6), back(2, 4), back(6, 8)):
                     for x in steps:
                         x()
                 continue
-            d, h = int(step[1]), int(step[2:] or 0)
-            bank = PB[summed.index(step[1]) % 4] if k in "sn" else WB[turns.index(step[1:]) % 4]
+            d, h, deep = int(step[1]), int(step[2:] or 0), step[1] in DEEP
+            bank = PB[summed.index(step[1]) % NS] if k in "sn" else (WB + PB[NS:])[turns.index(step[1:]) % NW]
             if k == "g":
-                look(q, d, 1024 * h, 1024 * h + 1024, lambda a, b: T.lst[:, 128 * d + a:128 * d + b], ["lst%d" % (d // 2)],
-                     T.dbc[:, 128 * d:128 * d + 1], DBC[d])
+                look(q, d, 1024 * h, 1024 * h + 1024, lambda a, b: T.lst[:, 128 * d + a:128 * d + b], ["lst%d" % d],
+                     T.dbc[:, 64 * d:64 * d + 1], DBC[d])
+            elif d == N:
+                if k == "m":
+                    minus(bank, "xp", h, "pkl", True)
+                elif k == "c":
+                    act([bank], ["xl%d" % h], T.xl[:, 192 * h:192 * h + 192], T[bank][:, 0:192])
             elif k == "m":
-                minus(bank, "xp", h)
+                minus(bank, "xp", h, "nph" if deep else "npk")
             elif k == "w":
-                words(bank, gsrc(d), gname(d), h, "pk", False)
+                if deep:
+                    words(bank, gsrc(d), gname(d), h, "pkh", False, False)
+                words(bank, gsrc(d), gname(d), h, "pkl" if deep else "pk", False, True)
             elif k == "c":
-                compare(q, bank, d, h)
+                compare(q, bank, d, h, deep)
             elif k == "s":
-                misses(bank, d, [] if t == 1 else ["mf1", "rj1"])
+                misses(bank, d, [] if t == 1 else ["mf1", "rj1"], 3 if deep else 6)
             else:
                 act([bank], ["fit%d" % d, "cnt%d" % (co + d)], T.fit[:, 128 * d:128 * d + 128], T[bank][:, 0:128],
                     ACT.Relu, bias=1.0, scale=-1.0, accum=T.cnt[:, co + d:co + d + 1])
@@ -586,14 +653,13 @@ def rank_program(g, core, T, topo):
         W = T["w_%d" % t]
         bs = T.base[:, 8 * t - 8:8 * t]
         for j in range(2):
-            mm(["nw%d" % j] + DBC, "q3", T.q3[:, 8 * j:8 * j + 8], T.nw[:, 128 * j:128 * j + 128], T.dbc[:, 0::128], j == 0, j == 1)
-        for j in range(2):
             mm(["asi", "idf"], "q0", T.q0[:, 128 * j:128 * j + 128], T.asi[:, 128 * j:128 * j + 128], T.idf[:], j == 0, j == 1)
         minus("q1", "xs", 0)
         minus("q2", "xs", 1)
         if t == 1:
             cp(["ew"], ["la"], T.la[:], T.ew[:, 2:34])
-            act(["xp0", "xp1", "la"], ["pai"], T.pai[:], T.xp[:].indirect(T.la[:]))
+            act(XB + ["lb"], ["pb1"], T.pai[:, 512:1024], T.xb[:].indirect(T.lb[:]), scale=-1.0)
+            act(["xp0", "xp1", "la"], ["pa1"], T.pai[:, 0:512], T.xp[:].indirect(T.la[:]))
             ts(["nrow"], ["base1"], bs, T.nrow[:, 0:8], -15.0, ADD, -1.0 / 128, MUL)
             ts(["cf"], ["ct12"], ct(12), cf(0), 4.0, OP.min, 8.0, MUL)
             fill(["wy1"], W[:, 24:32], 1.0)
@@ -609,8 +675,7 @@ def rank_program(g, core, T, topo):
             ts(lr, ["wy2"], W[:, 24:32], val, 2.0, MUL)
             tt(["b2a", "base1"], ["base2"], bs, T.ta[:, 0:8], T.base[:, 0:8], ADD)
             ts(["wd2a"], ["wd2"], W[:, 32:40], T.ct[:, 20:28], -1.0, ADD)
-        ts(DBC, ["wn%d" % t], W[:, 0:8], T.dbc[:, 0::128], -1.0, MUL)
-        ts(["q3"], ["wb%d" % t], W[:, 8:24], T.q3[:, 0:16], -32768.0, ADD)
+        ts(DBC, ["wn%d" % t], W[:, 0:8], T.dbc[:, 0::64], -1.0, MUL)
         mm(["b8", "base%d" % t], "p3", T.p3[:, 0:8], T.b8[:], bs, True, False)
 
     def idle1():
@@ -631,9 +696,11 @@ def rank_program(g, core, T, topo):
     def idle2():
         mm(["onef", "krow"], "p3", T.p3[:], T.onef[0:1, :], T.krow[0:1, :], True, False)
         ts(["nrow", "ct16"], ["oh"], T.oh[:], T.nrow[:, 0:16], ct(16), EQ, BIG, MUL)
+        for k, x in enumerate(("pa1", "pb1")):
+            mm([x, "idb"], "q3", T.q3[:], T.idb[:], T.pai[:, 512 * k:512 * k + 512], k == 0, k == 1)
+        act(["q3"], ["dall"], T.dall[:], T.q3[:])
         blocked(0, "mf1", 0)
         blocked(1, "fi1", 1)
-        tt(XB + ["lb", "pai"], ["dall"], T.dall[:], T.xb[:].indirect(T.lb[:]), T.pai[:], SUB)
 
     def choose(t):
         W, cl = T["w_%d" % t], T["cl%d" % t]
@@ -656,33 +723,33 @@ def rank_program(g, core, T, topo):
         ts(["c8", "kq%d" % t], ["fl%d" % t], fl, T.c8[:], T.kf[:, 1 + t:2 + t], ADD)
         for h in (1, 0):
             for j in range(2):
-                ts(["q0", w], ["s12%s%d" % ("ab"[j], h)], T.s12[:, 128 * h + 64 * j:128 * h + 64 * j + 64],
+                ts(["q0", w], ["s12%s%d" % ("ab"[j], 64 * h)], T.s12[:, 128 * h + 64 * j:128 * h + 64 * j + 64],
                    T.q0[:, 128 * j + 64 * h:128 * j + 64 * h + 64], col(1 + j), SUB)
         act(["fit%d" % d for d in range(8)] + ["fl%d" % t, w], [mf], M[mf], T.fit[:].indirect(fl), scale=col(3))
         shift([mf], [(M[mf], -SH, M["fi%d" % t], "fi%d" % t, "af%d" % t)])
-        for a, b in zip(slots(1, T.rl, "rl"), slots(0, T.rl, "rl")):
+        for a, b in zip(slots(64, 128, T.rl, "rl"), slots(0, 64, T.rl, "rl")):
             a()
             b()
         for q, h in (("S", 1), ("V", 0)):
-            for a in (1024 * h, 1024 * h + 512):
-                look(q, 0, a, a + 512, lambda a, b: T.rl[:, a:b], ["rl%d" % h], col(0), w)
-        for blocks in (range(4), range(4, 8)):
-            words("q2", gsrc(0), gname(0), 1, "pk", False, blocks)
-            words("q1", gsrc(0), gname(0), 0, "pk", False, blocks)
+            for a, n in ((1024 * h, 768), (1024 * h + 768, 256)):
+                look(q, 0, a, a + n, lambda a, b: T.rl[:, a:b], ["rl%d" % (64 * h)], col(0), w)
+        for blocks in (range(6), range(6, 8)):
+            words("q2", gsrc(0), gname(0), 1, "pk", False, True, blocks)
+            words("q1", gsrc(0), gname(0), 0, "pk", False, True, blocks)
         compare("S", "q2", 0, 1)
         compare("V", "q1", 0, 0)
         misses("p0", 0, [] if t == 1 else ["cs1"])
         act(["p0", w], [mr], T[mr][:], T.p0[:, 0:128], ACT.Relu, bias=col(3), scale=-float(t))
         if t == 1:
-            shift([mr], [(T[mr][:], SH, M["ri1"], "ri1", "ar1"), (T[mr][:], 2 * SH, M["rj1"], "rj1", "aj1")])
+            shift([mr], [(T[mr][:], SH, M["ri1"], "ri1", "ar1")])
+            shift([mr], [(T[mr][:], 2 * SH, M["rj1"], "rj1", "aj1")])
         else:
             send(mr, SH, "ri2", "ar2")
         ts(["km%d" % t], ["ko%d" % t], T.km[:, ko + 2:ko + 3], T.km[:, ko:ko + 1], 3, SHR)
         cp([w], ["yw%d" % t], T.ywo[:, t - 1:t], col(4))
         ts(["ko%d" % t], ["yx%d" % t], T.ywo[:, 1 + t:2 + t], T.km[:, ko + 2:ko + 3], -1.0, ADD)
 
-    put(4)
-    put(5)
+    put(1024, 1856)
     front(1)
     first_lists(put)
     main(1)
@@ -693,27 +760,26 @@ def rank_program(g, core, T, topo):
 
     for k, m in enumerate(("fi1", "ri1")):
         mm([m, "idb"], "p1", T.p1[:, 0:128], T.idb[:], M[m], k == 0, k == 1)
-    blocked(2, "rj1", 0)
-    blocked(3, "ri1", 1)
+    blocked(2, "ri1", 1)
+    blocked(3, "rj1", 0)
     for c in range(16):
         act(["p1", "oh"], ["in1_%d" % c], T.in1[:, 128 * c:128 * c + 128], T.p1[:, 0:128], scale=T.oh[:, c:c + 1])
     act(["p1"], ["cov"], T.cov[:], T.p1[:, 0:128])
 
-    def mark(j):
-        tt(["own%d" % (j // 4), XB[j // 2], "in1_%d" % (2 * j), "in1_%d" % (2 * j + 1)], TAB,
-           T.tab[:].indirect(T.own[:, 16 * j:16 * j + 16]), T.xb[:, 256 * j:256 * j + 256], T.in1[:, 256 * j:256 * j + 256], ADD)
+    def mark(a, b):
+        tt(["own%d" % x for x, y in SETS] + XB + ["in1_%d" % c for c in range(a // 128, (b + 127) // 128)], TAB,
+           T.tab[:].indirect(T.own[:, a // 16:b // 16]), T.xb[:, a:b], T.in1[:, a:b], ADD)
 
-    mark(0)
+    mark(0, 128)
     red(["p3"], ["kf"], T.kf[:, 0:1], T.p3[:], OP.min)
     o2 = S2 * rank
     ts(["kf"], ["kl"], T.kl[:, 0:1], T.kf[:, 0:1], 511.0, OP.min)
     ts(["kf"], ["la2b"], T.la2[:, o2 + 3:o2 + 4], T.kf[:, 0:1], 512.0, OP.is_lt)
-    ts(["dall", "kl"], ["la2a"], T.la2[:, o2 + 4:o2 + 20], T.dall[:].indirect(T.kl[:, 0:1]), -1.0, MUL)
+    cp(["dall", "kl"], ["la2a"], T.la2[:, o2 + 4:o2 + 20], T.dall[:].indirect(T.kl[:, 0:1]))
     gather_all(["la2a", "la2b"], "al2", T.la2[:, o2 + 3:o2 + 5], "la2")
     send("cov", -SH, "cs1", "acs")
 
-    for j in range(1, 6):
-        mark(j)
+    mark(128, 1856)
     front(2)
     first_lists(mark)
     main(2)

from concourse.bass import DstId, RemoteDMATransfer
from concourse.mybir import AluOpType, AxisListType, ActivationFunctionType

N, SH, NV, NP = 8, 3, 2048, 512
TW = 12288
BIG = float(2 ** 52)
EMPTY = 2 ** 23
S1, S2 = 32, 24
QOFF = 137

SCALAR = ("g00 g01 g10 c00 c80 c01 g20 c81 g11 g21 c10 c20 c11 c31 g30 c21 n4 n0 c30 g70 n1 n2 n3 c70 n5 n6 n7".split(),
          "g00 g01 c00 c01 g10 g11 c10 g20 g21 c11 n0 n4 c20 c21 g30 c31 c30 g70 n3 n1 n2 c70 n5 n6 n7".split())
VECTOR = ("L g40 g41 g50 c40 c41 g31 c50 g51 g60 g61 g71 c51 c60 c61 c71".split(),
          "L g40 g41 c40 g50 c41 g31 g51 g60 c50 g61 g71 c51 c60 c61 c71".split())
DEEP = "456"
COST = {"g": 1.4, "c": 0.33, "n": 0.13, "L": 3.0, "m": 0.22, "w": 0.22, "s": 0.38}
NW, NS = 5, 3
LAG, YIELD = 0.1, 0.3


def cost(x):
    if x[1:2] == "8":
        return {"m": COST["m"], "w": 0.0, "c": 0.5 * COST["c"]}[x[0]]
    return COST[x[0]] * ({"w": 2.0, "c": 0.5, "s": 0.6}.get(x[0], 1.0) if x != "L" and x[1] in DEEP else 1.0)


def timetable(t):
    end, order, free = {}, [], {"S": 0.0, "V": 0.0, "P": 0.0}
    left = {"S": list(SCALAR[t - 1]), "V": list(VECTOR[t - 1])}
    guess = {}
    for q in left:
        at = 0.0
        for x in left[q]:
            guess[x] = at
            at += cost(x)
    turns = sorted((x[1:] for x in guess if x[0] == "c"), key=lambda x: guess["c" + x])
    sums = sorted("01234567", key=lambda d: max(guess["c" + d + "0"], guess["c" + d + "1"]))
    left["P"] = ["m" + x for x in turns] + ["w" + x for x in turns] + ["s" + d for d in sums]

    def after(x):
        k, y = x[0], x[1:]
        if k == "g":
            return [] if y[0] == "0" else ["L"]
        if k == "m":
            n = turns.index(y)
            return ["c" + turns[n - NW]] if n >= NW else ["L"] if n >= 4 else []
        if k == "s":
            return ["c" + y + "0", "c" + y + "1"] + (["n" + sums[sums.index(y) - NS]] if sums.index(y) >= NS else [])
        if k == "c":
            return ["w" + y] + (["c8" + y[1]] if t == 1 and y[0] in DEEP else [])
        if k == "w":
            return ["m" + y] + (["g" + y] if y[0] != "8" else [])
        return ["s" + y] if k == "n" else []
    while any(left.values()):
        ready = []
        for q in left:
            for x in (left[q] if q == "P" else left[q][:1]):
                if all(y in end for y in after(x)):
                    at = max([free[q]] + [end[y] + (0.0 if q == "P" and y[0] == "m" else LAG) for y in after(x)])
                    ready.append((at + (YIELD if x[0] == "s" else 0.0), at, q, x))
        _, at, q, x = min(ready)
        left[q].remove(x)
        free[q] = end[x] = at + cost(x)
        order.append((q, x))
    return order, turns, sums


def _sb(n, dt):
    return ("sbuf", [128, n], dt)


B16, F32, I32, U16, F16 = "bfloat16", "float32", "int32", "uint16", "float16"
SCRATCH = {
    "tab": _sb(TW, B16), "xi": _sb(NV, I32), "xb": _sb(NV, B16), "ga": _sb(8 * NV, B16), "ne": _sb(8 * 768, B16),
    "xp": _sb(NV, B16), "xs": _sb(NV, B16), "dbc": _sb(512, B16), "dc": _sb(16, B16), "rb": _sb(24, F32),
    "zone": _sb(144, B16), "zw": _sb(288, B16),
    "pkl": _sb(24, B16), "pkh": _sb(24, B16), "nph": _sb(24, B16), "xl": _sb(384, F32),
    "npk": _sb(48, B16), "na": _sb(256, B16), "rr": _sb(256, B16), "ff": _sb(256, B16),
    "nn": _sb(2048, B16), "u1": _sb(1024, F32), "mm": _sb(1024, I32), "kk": _sb(1024, I32), "hh": _sb(1024, F32),
    "lst": _sb(1024, U16), "in1": _sb(NV, B16), "fit": _sb(1024, B16),
    "ew": _sb(36, I32), "pbi": _sb(32, I32), "es": _sb(2, F32), "ep": _sb(2, F32), "el": _sb(4, U16), "l0": _sb(4, U16),
    "wf": _sb(4, F32), "pcol": _sb(1, I32), "pf": _sb(1, F32), "ci": _sb(4, I32), "cf": _sb(4, F32), "ct": _sb(28, F32),
    "i3": _sb(1, I32), "nrow": _sb(144, B16), "rv1": _sb(128, B16), "krow": _sb(512, F32), "gs": _sb(8, B16),
    "wm": _sb(32, B16), "pk": _sb(48, B16), "idh": _sb(128, F16), "idq": _sb(128, B16), "idb": _sb(128, B16),
    "idf": _sb(128, F32), "nw": _sb(256, B16), "b8": _sb(128, B16), "bm": _sb(128, B16), "b1k": _sb(128, B16),
    "ones": _sb(128, B16), "onef": _sb(128, F32), "crow": _sb(256, B16), "oh": _sb(16, F32), "c8": _sb(8, F32),
    "s12": _sb(256, I32), "u12": _sb(256, I32), "m1": _sb(128, I32), "k1": _sb(128, I32), "h1": _sb(128, F32),
    "own": _sb(128, U16), "rl": _sb(128, U16), "la": _sb(32, U16), "lb": _sb(32, U16), "ao": _sb(256, F16),
    "ah": _sb(256, F16), "aso": _sb(256, F32), "asi": _sb(256, F32), "la1": _sb(8 * S1, F32), "la2": _sb(8 * S2, F32),
    "cl1": _sb(64, B16), "cl2": _sb(64, B16), "cnt": _sb(16, F32), "base": _sb(16, B16),
    "w_1": _sb(40, F32), "w_2": _sb(40, F32), "wo": _sb(32, F32), "km": _sb(8, I32), "wl": _sb(4, U16),
    "fl": _sb(16, U16), "mf2": _sb(128, B16), "mr1": _sb(128, B16), "mr2": _sb(128, B16), "fi2": _sb(128, B16),
    "ri2": _sb(128, B16), "cov": _sb(128, B16), "cs1": _sb(128, B16), "pt": _sb(128, I32), "pl": _sb(128, U16),
    "pai": _sb(1024, B16), "dall": _sb(512, B16), "em": _sb(1024, B16), "gm": _sb(2048, B16),
    "kf": _sb(4, F32), "kl": _sb(2, U16), "c1": _sb(128, F32), "ta": _sb(128, F32), "yo": _sb(128, F32), "ywo": _sb(4, F32),
}
WB = ("q0", "q1", "q2", "q3")
PB = ("p0", "p1", "p2", "p3")
BANKS = WB + PB
for _n in BANKS:
    SCRATCH[_n] = ("psum", [128, 512], F32)
SEMAPHORES = ["qv", "qs", "qp", "qg", "sent", "dx0", "dx1", "dx2", "dx3", "dw", "dpb", "dy", "dz", "dy2",
              "hx0", "hx1", "has", "aes", "ael", "aep", "al1", "aah", "axp0", "axp1", "axs", "aas", "ac1", "af1", "ar1",
              "aj1", "acs", "al2", "ac2", "af2", "ar2"]

OP = AluOpType
ACT = ActivationFunctionType
AX = AxisListType.X


def _count(mask):
    return bin(mask).count("1")


def _helper(r, cores, topo):
    c = cores[r]
    near = [cores[(r + k) % N] for k in (SH, -SH)]
    free = [h for h in topo.cores_of(c) if h not in cores and topo.die(h) != topo.die(c)
            and all(topo.may_write(h, d) for d in near)]
    return free[[x for x in cores if topo.chip(x) == topo.chip(c)].index(c)]


def _inner(r, cores, topo):
    return topo.mask(cores[r], _helper(r, cores, topo)) & ~topo.mask(cores[r], cores[(r + SH) % N])


def _handed(T):
    return [("hx1", T.xb[:, 1024:2048], SH, T.xp[:, 1024:2048], "xp1", "axp1"),
            ("has", T.aso[:], -SH, T.asi[:], "asi", "aas"),
            ("hx0", T.xb[:], -SH, T.xs[:], "xs", "axs")]


def helper_program(g, core, r, T, topo):
    cores, sent = list(T.cores), 0
    for sem, src, off, dst, _, there in _handed(T):
        to = cores[(r + off) % N]
        rid, pid, _ = topo.addr(to)
        g.wait_ge(T.sem[sem], _count(_inner(r, cores, topo)))
        g.remote_dma(dst, src, T.sem[there], T.sem.sent, pid, rid, topo.mask(core, to))
        sent += _count(topo.mask(core, to))
    g.wait_ge(T.sem.sent, sent)


def rank_program(g, core, T, topo):
    rank = T.rank_of(core)
    cores = list(T.cores)
    if rank is None:
        for r in range(N):
            if _helper(r, cores, topo) == core:
                helper_program(g, core, r, T, topo)
        return
    Q = {"v": g.vector, "s": g.scalar, "p": g.tensor, "g": g, "y": g.sync}
    cnt = {}
    waited = {}
    lastw, reads = {}, {}

    def need(q, toks):
        best = {}
        for s, v in toks:
            best[s] = max(best.get(s, 0), v)
        for s, v in best.items():
            if waited.get((q, s), 0) < v:
                Q[q].wait_ge(T.sem[s], v)
                waited[(q, s)] = v

    def deps(q, r, w):
        toks = []
        for x in r:
            if x in lastw:
                toks.append(lastw[x])
            if x in BANKS:
                toks += [t for t in reads.get(x, []) if t[0] != "q" + q]
        for x in w:
            toks += reads.get(x, []) + ([lastw[x]] if x in lastw else [])
        if q == "p":
            toks = [t for t in toks if t[0] != "qp"]
        need(q, toks)

    def done(tok, r, w):
        for x in r:
            reads.setdefault(x, []).append(tok)
        for x in w:
            lastw[x] = tok
            reads[x] = []

    def run(q, r, w, fn):
        deps(q, r, w)
        s = "q" + q
        cnt[s] = cnt.get(s, 0) + 1
        fn().then_inc(T.sem[s], 1)
        done((s, cnt[s]), r, w)

    def ts(r, w, out, in0, a, op0, b=None, op1=None):
        if op1 is None:
            run("v", r, w, lambda: g.vector.tensor_scalar(out, in0, a, None, op0))
        else:
            run("v", r, w, lambda: g.vector.tensor_scalar(out, in0, a, b, op0, op1))

    def tt(r, w, out, in0, in1, op):
        run("v", r, w, lambda: g.vector.tensor_tensor(out, in0, in1, op))

    def cp(r, w, out, in_):
        run("v", r, w, lambda: g.vector.tensor_copy(out, in_))

    def fill(w, out, c):
        run("v", [], w, lambda: g.vector.memset(out, c))

    def red(r, w, out, in_, op):
        run("v", r, w, lambda: g.vector.tensor_reduce(out, in_, AX, op))

    def act(r, w, out, in_, func=None, bias=0.0, scale=1.0, accum=None):
        f = ACT.Identity if func is None else func
        run("s", r, w, lambda: g.scalar.activation(out, in_, f, bias=bias, scale=scale, accum_out=accum))

    def mm(r, bank, out, lhsT, rhs, start, stop):
        run("p", r, [bank], lambda: g.tensor.matmul(out, lhsT, rhs, start, stop))

    def iota(w, out, pattern, base, mult, small=True):
        if small:
            run("g", [], w, lambda: g.iota(out, pattern, base, mult, allow_small_or_imprecise_dtypes=True))
        else:
            run("g", [], w, lambda: g.iota(out, pattern, base, mult))

    def dma(q, sem, r, w, out, in_):
        deps(q, r, w)
        cnt[sem] = cnt.get(sem, 0) + 16
        Q[q].dma_start(out, in_).then_inc(T.sem[sem], 16)
        done((sem, cnt[sem]), r, w)

    def plan(src_rank, dst_ranks):
        c = cores[src_rank]
        far = [d for d in dst_ranks if topo.chip(cores[d]) != topo.chip(c)]
        near = [d for d in dst_ranks if topo.chip(cores[d]) == topo.chip(c)]
        out, used = [], 0
        if far:
            m = topo.mask(c, cores[far[0]])
            for d in far[1:]:
                m &= topo.mask(c, cores[d])
            out.append((m, far))
            used = m
        if near:
            out.append((topo.mask(c, cores[near[0]]) & ~used, near))
        return out

    def dst_id(d):
        rid, pid, _ = topo.addr(cores[d])
        return DstId(rid=rid, pnc=pid)

    def gather_all(r, sem, src, landing):
        deps("g", r, [])
        trs = []
        for m, ds in plan(rank, [(rank + j) % N for j in range(1, N)]):
            trs.append(RemoteDMATransfer(dst_ids=[dst_id(d) for d in ds], dma_engine_mask=m, remote_sem=T.sem[sem],
                                         srcs=[src], dsts=[src for d in ds]))
            cnt["sent"] = cnt.get("sent", 0) + _count(m)
        g.remote_dma_fused(trs, local_sem=T.sem.sent)
        total = 0
        for s in range(N):
            if s != rank:
                total += sum(_count(m) for m, ds in plan(s, [(s + j) % N for j in range(1, N)]) if rank in ds)
        cnt[sem] = total
        lastw[landing] = (sem, total)

    def shift(r, items):
        deps("g", r, [])

        def masks(s):
            m = None
            for it in items:
                k = topo.mask(cores[s], cores[(s + it[1]) % N])
                m = k if m is None else m & k
            es = [e for e in topo.engines(cores[s], cores[(s + items[0][1]) % N]) if m >> e & 1]
            per = len(es) // len(items)
            return [sum(1 << e for e in es[j * per:(j + 1) * per]) for j in range(len(items))]
        mine = masks(rank)
        if len(items) == 1:
            src, off, dst, land, sem = items[0]
            rid, pid, _ = topo.addr(cores[(rank + off) % N])
            g.remote_dma(dst, src, T.sem[sem], T.sem.sent, pid, rid, mine[0])
        else:
            g.remote_dma_fused([RemoteDMATransfer(dst_ids=[dst_id((rank + it[1]) % N)], dma_engine_mask=m,
                                                  remote_sem=T.sem[it[4]], src=it[0], dst=it[2])
                                for it, m in zip(items, mine)], local_sem=T.sem.sent)
        for j, it in enumerate(items):
            cnt["sent"] = cnt.get("sent", 0) + _count(mine[j])
            cnt[it[4]] = _count(masks((rank - it[1]) % N)[j])
            lastw[it[3]] = (it[4], cnt[it[4]])

    def send(name, off, land, sem):
        shift([name], [(T[name][:], off, T[land][:], land, sem)])

    def hand(r, src, sem):
        deps("g", r, [])
        rid, pid, _ = topo.addr(_helper(rank, cores, topo))
        g.remote_dma(src, src, T.sem[sem], T.sem.sent, pid, rid, _inner(rank, cores, topo))
        cnt["sent"] = cnt.get("sent", 0) + _count(_inner(rank, cores, topo))

    for _, _, off, _, land, sem in _handed(T):
        cnt[sem] = _count(topo.mask(_helper((rank - off) % N, cores, topo), core))
        lastw[land] = (sem, cnt[sem])

    TAB = ["tab%d" % j for j in range(TW // 2048)]
    XB = ["xb%d" % j for j in range(4)]
    DBC = ["dbc%d" % d for d in range(8)]
    M = {"mf1": T.ff[:, 0:128], "fi1": T.ff[:, 128:256], "rj1": T.rr[:, 0:128], "ri1": T.rr[:, 128:256],
         "cs1": T.cs1[:], "mf2": T.mf2[:], "fi2": T.fi2[:]}
    AND, SHR = OP.bitwise_and, OP.arith_shift_right
    EQ, MUL, ADD, SUB, GE = OP.is_equal, OP.mult, OP.add, OP.subtract, OP.is_ge

    def cf(j):
        return T.cf[:, j:j + 1]

    def ct(j):
        return T.ct[:, j:j + 1]

    def wf(j):
        return T.wf[:, j:j + 1]

    def part(j):
        return T.tab[:, 2048 * j:2048 * j + 2048]

    def cast(j):
        cp(["xi%d" % j], [XB[j]], T.xb[:, 512 * j:512 * j + 512], T.xi[:, 512 * j:512 * j + 512])

    dma("s", "dw", [], ["ew"], T.ew[:, 0:1], T.w1[:])
    dma("y", "dw", [], ["ew1"], T.ew[:, 1:2], T.w2[:])
    dma("s", "dw", [], ["ew2"], T.ew[:, 2:34], T.pa[:])
    lastw["ew"] = lastw["ew2"]
    for j in range(4):
        dma("y", "dx%d" % j, [], ["xi%d" % j], T.xi[:, 512 * j:512 * j + 512], T.x[:, 512 * j:512 * j + 512])
    dma("s", "dpb", [], ["pbi"], T.pbi[:], T.pb[:])

    iota(["pcol"], T.pcol[:], [[0, 1]], 0, 1, small=False)
    iota(["pf"], T.pf[:], [[0, 1]], 0, 1)
    iota(["nrow"], T.nrow[:], [[1, 144]], 0, 0)
    iota(["rv1"], T.rv1[:], [[1, 8], [0, 16]], 0, 0)
    VF, GF, G0 = 3840, 2176, 448

    def blank(k, a, b):
        return lambda: fill(["tabv%d" % k], T.tab[:, a:b], float(EMPTY))
    iota([TAB[4]], T.tab[:, TW - GF:TW - GF + G0], [[0, G0]], EMPTY, 0)
    fill([TAB[0]], T.tab[:, 0:512], float(EMPTY))
    act([TAB[0]], [TAB[1]], T.tab[:, VF:VF + 512], T.tab[:, 0:512])
    blank(0, 512, 1536)()
    for k, a in enumerate(range(VF + 512, TW - GF, 1536)):
        b = min(a + 1536, TW - GF)
        act([TAB[0], "tabv0"], ["tabs%d" % k], T.tab[:, a:b], T.tab[:, 0:b - a])
    for j, (a, op, b) in enumerate([(15, AND, None), (4, SHR, None), (1, SHR, 7), (1, AND, None)]):
        ts(["pcol"], ["ci%d" % j], T.ci[:, j:j + 1], T.pcol[:], a, op, b, None if b is None else AND)
    fill(["ones"], T.ones[:], 1.0)
    cp(["ci%d" % j for j in range(4)], ["cf"], T.cf[:, 0:4], T.ci[:, 0:4])
    fill(["crow"], T.crow[0:1, :], 4096.0 * QOFF)
    ts(["cf"], ["ct4"], ct(4), cf(1), 16.0, MUL, 15.0, ADD)
    blank(1, 1536, 2560)()
    ts(["nrow", "ct4"], ["zone"], T.zone[:], T.nrow[:], ct(4), EQ)
    cp(["ew"], ["wf0"], T.wf[:, 0:2], T.ew[:, 0:2])
    cp(["ew"], ["l0"], T.l0[:], T.ew[:, 2:6])
    shift(["wf0", "l0"], [(T.wf[:, 0:2], -SH, T.es[:], "es", "aes"), (T.l0[:], -SH, T.el[:], "el", "ael")])
    shift(["wf0"], [(T.wf[:, 0:2], SH, T.ep[:], "ep", "aep")])
    iota([TAB[5]], T.tab[:, TW - GF + G0:TW], [[0, GF - G0]], EMPTY, 0)
    for j in range(2):
        ts(["zone", "wf0"], ["zw%d" % j], T.zw[:, 144 * j:144 * j + 144], T.zone[:], wf(j), MUL)
    blank(2, 2560, VF - 384)()
    cast(0)
    later = [
        lambda: ts(["cf"], ["i3"], T.i3[:], cf(0), -1.0, ADD, 1.0 / 3.0, MUL),
        lambda: ts(["nrow", "cf"], ["gs"], T.gs[:], T.nrow[:, 0:8], cf(1), EQ),
        lambda: cp(["pbi"], ["lb"], T.lb[:], T.pbi[:]),
        lambda: ts(["i3", "cf"], ["ct3"], ct(3), T.i3[:], -3.0, MUL, cf(0), ADD),
        lambda: ts(["nrow", "pf"], ["idb"], T.idb[:], T.nrow[:, 0:128], T.pf[:], EQ),
        lambda: ts(["i3", "cf"], ["ct2"], ct(2), T.i3[:], 8.0, MUL, cf(1), ADD),
        lambda: ts(["ct3"], ["ct6"], ct(6), ct(3), 1.0, GE, 255.0, MUL),
        lambda: ts(["ct3"], ["ct7"], ct(7), ct(3), 2.0, GE, 65280.0, MUL),
        blank(3, VF - 384, VF),
        lambda: ts(["ct6", "ct7"], ["ct10"], ct(10), ct(6), ct(7), ADD, 1.0, ADD),
        lambda: ts(["wf0"], ["wf2"], T.wf[:, 2:4], T.wf[:, 0:2], -1.0, MUL),
        lambda: ts(["nrow", "ct2", "ct10"], ["pk"], T.pk[:], T.nrow[:, 0:48], ct(2), EQ, ct(10), MUL),
        lambda: ts(["rv1", "cf"], ["bm"], T.bm[:], T.rv1[:], cf(1), EQ),
        lambda: ts(["nrow", "pf"], ["idh"], T.idh[:], T.nrow[:, 0:128], T.pf[:], EQ)]

    SETS = ((0, 32), (32, 64), (64, 128))

    def own_sums(k, bank, alone=True):
        a, b = SETS[k]
        for j in range(2):
            for r in range(16):
                o = 144 * j + 15 - r
                mm(XB[a // 32:b // 32] + ["zw%d" % j], bank, T[bank][:, (b - a) * j:(b - a) * (j + 1)], T.zw[:, o:o + 128],
                   T.xb[:, 16 * a + r:16 * b:16], alone and j == 0 and r == 0, alone and j == 1 and r == 15)

    def sums(bank, s, stop=True):
        for r in range(16):
            mm(XB + ["wm%d0" % s, "wm%d1" % s], bank, T[bank][:, r:256:16], T.xb[:, r::16], T.wm[:, 16 * s:16 * s + 16],
               r == 0, stop and r == 15)

    def words(bank, src, name, h, pk, first, last, blocks=range(8)):
        for b in blocks:
            o = 1024 * h + 128 * b
            mm(name(o) + [pk], bank, T[bank][:, b:8 * T[pk].shape[1]:8], src(o), T[pk][:], first and b == 0, last and b == 7)

    def slots(a, b, out, name):
        k = str(a)
        return [lambda: ts(["s12a" + k, "s12b" + k], ["u12" + k], T.u12[:, 2 * a:2 * b], T.s12[:, 2 * a:2 * b], 4095, AND),
                lambda: tt(["u12" + k], ["m1" + k], T.m1[:, a:b], T.u12[:, 2 * a:a + b], T.u12[:, a + b:2 * b], MUL),
                lambda: ts(["m1" + k], ["k1" + k], T.k1[:, a:b], T.m1[:, a:b], 5, SHR, 8191, AND),
                lambda: tt(["k1" + k, "u12" + k], ["h1" + k], T.h1[:, a:b], T.k1[:, a:b], T.u12[:, a + b:2 * b], ADD),
                lambda: cp(["h1" + k], [name + k], out[:, a:b], T.h1[:, a:b])]

    def own_slots(k):
        a, b = SETS[k]
        return [lambda: cp([PB[k]], ["s12a%d" % a, "s12b%d" % a], T.s12[:, 2 * a:2 * b], T[PB[k]][:, 0:2 * (b - a)])
                ] + slots(a, b, T.own, "own")

    def put(a, b):
        cp(["own%d" % x for x, y in SETS if 16 * x < b and a < 16 * y] + XB[a // 512:(b + 511) // 512],
           TAB + ["tab%s%d" % (q, k) for q in "vs" for k in range(4)], T.tab[:].indirect(T.own[:, a // 16:b // 16]), T.xb[:, a:b])

    def between(steps, scatter, a, b, n=64):
        cuts = [a] + [b - n * k for k in range(len(steps) - 1, -1, -1)]
        for k, step in enumerate(steps):
            scatter(cuts[k], cuts[k + 1])
            step()

    own_sums(0, "p0")
    for step in later[:8]:
        step()
    cast(1)
    own_sums(1, "p1")
    one, two = own_slots(0), own_slots(1)
    for step in (one[0], later[8], one[1], later[9], later[10], one[2], lambda: cast(2), one[3], later[11], later[12], one[4],
                 two[0], one[5], two[1], lambda: cast(3), two[2], lambda: put(0, 128), two[3], later[13],
                 lambda: put(128, 256), two[4], lambda: put(256, 384), two[5]):
        step()
    for j in range(2):
        act(["gs", "es"], ["wm0%d" % j], T.wm[:, 8 * j:8 * j + 8], T.gs[:], scale=T.es[:, j:j + 1])
    o1 = S1 * rank
    act(XB + ["lb"], ["la1a"], T.la1[:, o1 + 15:o1 + 31], T.xb[:].indirect(T.lb[:, 0:1]), scale=-1.0)
    act(XB + ["el", "la1a"], ["la1b"], T.la1[:, o1 + 16:o1 + 32], T.xb[:].indirect(T.el[:, 0:1]))
    hand(XB, T.xb[:, 1024:2048], "hx1")
    gather_all(["la1a", "la1b"], "al1", T.la1[:, o1 + 15:o1 + 17], "la1")
    act(["idb"], ["idq"], T.idq[:], T.idb[:], scale=-4096.0)
    sums("q0", 0)
    sums("q1", 0, False)
    act(["q0"], ["na"], T.na[:], T.q0[:, 0:256], bias=QOFF + 0.5 / 4096, scale=1.0 / 4096)
    mm(["na", "idq"], "q1", T.q1[:, 0:256], T.idq[:], T.na[:], False, True)
    own_sums(2, "p2")
    mm(["ones", "crow"], "p3", T.p3[:, 0:128], T.ones[0:1, :], T.crow[0:1, 0:128], True, False)
    own_sums(2, "p3", False)
    ts(["q1"], ["ao"], T.ao[:], T.q1[:, 0:256], 4096.0 * QOFF, ADD)
    send("ao", SH, "ah", "aah")
    shift(XB, [(T.xb[:, 0:1024], SH, T.xp[:, 0:1024], "xp0", "axp0")])
    hand(XB, T.xb[:, 0:1024], "hx0")
    for j in range(2):
        act(["gs", "ep"], ["wm1%d" % j], T.wm[:, 16 + 8 * j:24 + 8 * j], T.gs[:], scale=T.ep[:, j:j + 1])
    for j in range(2):
        act(["bm", "wf2"], ["nw%d" % j], T.nw[:, 128 * j:128 * j + 128], T.bm[:], scale=wf(2 + j))
    act(["pk"], ["npk"], T.npk[:], T.pk[:], scale=-1.0)
    for w in range(3):
        lo, hi, o = T.pk[:, 16 * w:16 * w + 8], T.pk[:, 16 * w + 8:16 * w + 16], slice(8 * w, 8 * w + 8)
        act(["pk"], ["pkl%d" % w], T.pkl[:, o], lo)
        act(["pk"], ["pkh%d" % w], T.pkh[:, o], hi, scale=2.0 ** 24)
        act(["pk"], ["nph%d" % w], T.nph[:, o], hi, scale=-2.0 ** 24)
    for x in ("pkl", "pkh", "nph"):
        lastw[x] = lastw["nph2"]
    act(["idb"], ["idf"], T.idf[:], T.idb[:])
    act(["bm"], ["b8"], T.b8[:], T.bm[:], scale=8.0)
    act(["bm"], ["b1k"], T.b1k[:], T.bm[:], scale=1024.0)
    act(["p2"], ["nn0_0"], T.nn[:, 0:128], T.p2[:, 0:128], bias=QOFF + 0.5 / 4096 - 0.5, scale=1.0 / 4096)
    mm(["nn0_0", "idq"], "p3", T.p3[:, 0:128], T.idq[:], T.nn[:, 0:128], False, True)
    act(["p3"], ["u10"], T.u1[:, 0:64], T.p3[:, 0:64])
    between([lambda: tt(["u10", "p3"], ["m164"], T.m1[:, 64:128], T.u1[:, 0:64], T.p3[:, 64:128], MUL),
             lambda: ts(["m164"], ["k164"], T.k1[:, 64:128], T.m1[:, 64:128], 5, SHR, 8191, AND),
             lambda: tt(["k164", "p3"], ["h164"], T.h1[:, 64:128], T.k1[:, 64:128], T.p3[:, 64:128], ADD),
             lambda: cp(["h164"], ["own64"], T.own[:, 64:128], T.h1[:, 64:128])], put, 384, 1024, 32)
    sums("q2", 1)
    act(["q2"], ["aso"], T.aso[:], T.q2[:, 0:256])
    hand(["aso"], T.aso[:], "has")
    iota(["krow"], T.krow[0:1, :], [[1, 512]], 0, 0)
    iota(["c8"], T.c8[:], [[16, 8]], 0, 1)

    def const(c):
        mm(["ones", "crow"], PB[c], T[PB[c]][:, 256:512], T.ones[0:1, :], T.crow[0:1, :], True, False)

    def apart(bank, order, first):
        for k, u in enumerate(order):
            mm(["ah", "idh"], bank, T[bank][:, 128 * k:128 * k + 128], T.ah[:, 128 * u:128 * u + 128], T.idh[:],
               first and k == 0, first and k == len(order) - 1)

    def front(t):
        if t == 1:
            k = S1 * (N - SH) + 16
            cols = [(T.dc[:, 0:SH], T.la1[:, k::S1]), (T.dc[:, SH:N], T.la1[:, 16:k:S1]), (T.dc[:, N:2 * N], T.la1[:, 15::S1])]
            src = ["la1", "la1a", "la1b"]
        else:
            cols, src = [(T.dc[:, 0:N], T.la2[:, 4::S2])], ["la2", "la2a"]

        def sides():
            apart("q0", (0, 1), True)

        def offers():
            for k, (out, in_) in enumerate(cols):
                act(src, ["dc%d" % k], out, in_)
            parts = range(3 - t)
            for u in range(2):
                for k in parts:
                    mm(["nw%d" % u, "dc0", "dc1", "dc2"], "q1", T.q1[:, 8 * u:8 * u + 8], T.nw[:, 128 * u:128 * u + 128],
                       T.dc[:, N * k:N * k + N], u == 0 and k == 0, u == 1 and k == parts[-1])

        def biases():
            act(["q1"], ["rb"], T.rb[:, 0:16], T.q1[:, 0:16], bias=QOFF + 0.5 / 4096 - 0.5, scale=1.0 / 4096)
            act(["q1"], ["ob"], T.rb[:, 16:24], T.q1[:, 0:8], bias=4096.0 * QOFF)
            act(["q1"], ["wb%d" % t], T["w_%d" % t][:, 8:24], T.q1[:, 0:16], bias=-32768.0)

        def spread(c):
            for d in (2 * c, 2 * c + 1):
                out = T.dbc[:, 64 * d:64 * d + 64]
                if t == 1:
                    a, b = S1 * ((d - SH) % N) + 16, S1 * d + 15
                    act(src + ["ones"], [DBC[d]], out, T.ones[:, 0:64], scale=T.la1[:, a:a + 1], bias=T.la1[:, b:b + 1])
                else:
                    a = S2 * d + 4
                    act(src + ["ones"], [DBC[d]], out, T.ones[:, 0:64], scale=T.la2[:, a:a + 1])
            for k in range(4):
                d = 2 * c + k // 2
                mm(["nw1", DBC[d]], PB[c], T[PB[c]][:, 256 + 64 * k:320 + 64 * k], T.nw[:, 128:256], T.dbc[:, 64 * d:64 * d + 64],
                   False, False)

        def rem(c):
            for k in range(4):
                u, d, o = k // 2, 2 * c + k % 2, 512 * c + 128 * k
                act(["q0", "rb"], ["nn%d_%d" % (c, k)], T.nn[:, o:o + 128], T.q0[:, 128 * u:128 * u + 128],
                    bias=T.rb[:, 8 * u + d:8 * u + d + 1], scale=1.0 / 4096)
            if t == 1:
                apart(PB[c], (0, 0, 1, 1), False)
            mm(["nn%d_%d" % (c, k) for k in range(4)] + ["idq"], PB[c], T[PB[c]][:], T.idq[:], T.nn[:, 512 * c:512 * c + 512],
               False, True)

        def out1(c):
            for k in range(2):
                d = 2 * c + k
                act([PB[c], "ob"], ["u1%d" % d], T.u1[:, 128 * d:128 * d + 128], T[PB[c]][:, 128 * k:128 * k + 128],
                    bias=T.rb[:, 16 + d:17 + d])

        a, b, c, d = 0, 2, 1, 3
        for k in range(4):
            const(k)
            if t == 2:
                apart(PB[k], (0, 0, 1, 1), False)
        if t == 2:
            sides()
        offers()
        spread(a); spread(b)
        if t == 1:
            sides()
        biases()
        spread(c)
        rem(a); spread(d); rem(b); out1(a)
        rem(c); out1(b); rem(d); out1(c); out1(d)

    def back(d, e):
        a, b, bank, k = 128 * d, 128 * e, PB[d // 2], str(d)
        u2 = T[bank][:, 256 + a % 256:256 + a % 256 + b - a]
        return [lambda: tt(["u1%d" % x for x in range(d, e)] + [bank], ["mm" + k], T.mm[:, a:b], T.u1[:, a:b], u2, MUL),
                lambda: ts(["mm" + k], ["kk" + k], T.kk[:, a:b], T.mm[:, a:b], 5, SHR, 8191, AND),
                lambda: tt(["kk" + k, bank], ["hh" + k], T.hh[:, a:b], T.kk[:, a:b], u2, ADD),
                lambda: cp(["hh" + k], ["lst%d" % x for x in range(d, e)], T.lst[:, a:b], T.hh[:, a:b])]

    def first_lists(scatter):
        for k, step in enumerate(back(0, 1)):
            step()
            if k < 3:
                scatter(1856 + 64 * k, 1920 + 64 * k)

    def gname(d):
        return lambda o: ["ga%d_%d" % (d, o // 256)]

    def gsrc(d):
        return lambda o: T.ga[:, NV * d + o:NV * d + o + 128]

    def look(q, d, a, b, lst, lname, bias, bname):
        out = T.ga[:, NV * d + a:NV * d + b]
        src = T.tab[:].indirect(lst(a // 16, b // 16))
        r, w = TAB + lname + [bname], ["ga%d_%d" % (d, k) for k in range(a // 256, b // 256)]
        if q == "S":
            act(r, w, out, src, bias=bias)
        else:
            ts(r, w, out, src, bias, ADD)

    def minus(bank, ref, h, pk="npk", last=False):
        words(bank, lambda o: T[ref][:, o:o + 128], lambda o: [ref + "%d" % h if ref == "xp" else ref], h, pk, True, last)

    def compare(q, bank, d, h, deep=False):
        out, w = T.ne[:, 768 * d + h:768 * d + 768:2], ["ne%d_%d" % (d, h)]
        if deep:
            tt([bank, "xl%d" % h], w, T.ne[:, 768 * d + h:768 * d + 384:2], T[bank][:, 0:192], T.xl[:, 192 * h:192 * h + 192],
               OP.not_equal)
        elif q == "S":
            act([bank], w, out, T[bank][:, 0:384], ACT.Abs)
        else:
            ts([bank], w, out, T[bank][:, 0:384], 0.0, OP.not_equal)

    def misses(bank, d, masks, n=6):
        for k, m in enumerate(masks):
            mm([m, "idb"], bank, T[bank][:, 0:128], T.idb[:], M[m], k == 0, False)
        for w in range(n):
            o = 768 * d + 128 * w
            mm(["ne%d_0" % d, "ne%d_1" % d, "idb"], bank, T[bank][:, 0:128], T.ne[:, o:o + 128], T.idb[:],
               w == 0 and not masks, w == n - 1)

    def main(t):
        order, turns, summed = timetable(t)
        co = 8 * (t - 1)
        for q, step in order:
            k = step[0]
            if k == "L":
                for steps in zip(back(1, 2), back(4, 6), back(2, 4), back(6, 8)):
                    for x in steps:
                        x()
                continue
            d, h, deep = int(step[1]), int(step[2:] or 0), step[1] in DEEP
            bank = PB[summed.index(step[1]) % NS] if k in "sn" else (WB + PB[NS:])[turns.index(step[1:]) % NW]
            if k == "g":
                look(q, d, 1024 * h, 1024 * h + 1024, lambda a, b: T.lst[:, 128 * d + a:128 * d + b], ["lst%d" % d],
                     T.dbc[:, 64 * d:64 * d + 1], DBC[d])
            elif d == N:
                if k == "m":
                    minus(bank, "xp", h, "pkl", True)
                elif k == "c":
                    act([bank], ["xl%d" % h], T.xl[:, 192 * h:192 * h + 192], T[bank][:, 0:192])
            elif k == "m":
                minus(bank, "xp", h, "nph" if deep else "npk")
            elif k == "w":
                if deep:
                    words(bank, gsrc(d), gname(d), h, "pkh", False, False)
                words(bank, gsrc(d), gname(d), h, "pkl" if deep else "pk", False, True)
            elif k == "c":
                compare(q, bank, d, h, deep)
            elif k == "s":
                misses(bank, d, [] if t == 1 else ["mf1", "rj1"], 3 if deep else 6)
            else:
                act([bank], ["fit%d" % d, "cnt%d" % (co + d)], T.fit[:, 128 * d:128 * d + 128], T[bank][:, 0:128],
                    ACT.Relu, bias=1.0, scale=-1.0, accum=T.cnt[:, co + d:co + d + 1])
        cl = T["cl%d" % t]
        o = 8 * rank
        names = ["cnt%d" % (co + d) for d in range(8)]
        if t == 1:
            cp(names, ["clo1"], cl[:, o:o + 8], T.cnt[:, 0:8])
        else:
            tt(names + ["la2", "la2b"], ["clo2"], cl[:, o:o + 8], T.cnt[:, 8:16], T.la2[:, 3::S2], MUL)
        gather_all(["clo%d" % t], "ac%d" % t, cl[:, o:o + 8], "cl%d" % t)

    def choices(t):
        W = T["w_%d" % t]
        bs = T.base[:, 8 * t - 8:8 * t]
        for j in range(2):
            mm(["asi", "idf"], "q0", T.q0[:, 128 * j:128 * j + 128], T.asi[:, 128 * j:128 * j + 128], T.idf[:], j == 0, j == 1)
        minus("q1", "xs", 0)
        minus("q2", "xs", 1)
        if t == 1:
            cp(["ew"], ["la"], T.la[:], T.ew[:, 2:34])
            act(XB + ["lb"], ["pb1"], T.pai[:, 512:1024], T.xb[:].indirect(T.lb[:]), scale=-1.0)
            act(["xp0", "xp1", "la"], ["pa1"], T.pai[:, 0:512], T.xp[:].indirect(T.la[:]))
            ts(["nrow"], ["base1"], bs, T.nrow[:, 0:8], -15.0, ADD, -1.0 / 128, MUL)
            ts(["cf"], ["ct12"], ct(12), cf(0), 4.0, OP.min, 8.0, MUL)
            fill(["wy1"], W[:, 24:32], 1.0)
            cp(["nrow"], ["wd1"], W[:, 32:40], T.nrow[:, 0:8])
            ts(["ct12"], ["ct14"], ct(14), ct(12), 7.0, ADD)
            ts(["cf"], ["ct15"], ct(15), cf(1), -16.0, MUL, 896.0, ADD)
            ts(["c8", "ct15"], ["c8"], T.c8[:], T.c8[:], ct(15), ADD)
        else:
            val = T.la2[:, 3::S2]
            lr = ["la2", "la2b"]
            ts(lr, ["b2a"], T.ta[:, 0:8], val, -1.0, ADD, 8.0 / 128, MUL)
            tt(lr + ["nrow"], ["wd2a"], T.ct[:, 20:28], val, T.nrow[:, 1:9], MUL)
            ts(lr, ["wy2"], W[:, 24:32], val, 2.0, MUL)
            tt(["b2a", "base1"], ["base2"], bs, T.ta[:, 0:8], T.base[:, 0:8], ADD)
            ts(["wd2a"], ["wd2"], W[:, 32:40], T.ct[:, 20:28], -1.0, ADD)
        ts(DBC, ["wn%d" % t], W[:, 0:8], T.dbc[:, 0::64], -1.0, MUL)
        mm(["b8", "base%d" % t], "p3", T.p3[:, 0:8], T.b8[:], bs, True, False)

    def idle1():
        ts(["cf"], ["ct16"], ct(16), cf(3), 8.0, MUL, cf(2), ADD)
        ts(["ew"], ["pt0"], T.pt[:, 0:32], T.ew[:, 2:34], 127, AND)
        ts(["pbi"], ["pt1"], T.pt[:, 32:64], T.pbi[:], 127, AND)
        ts(["ew"], ["pt2"], T.pt[:, 64:96], T.ew[:, 2:34], 7, SHR)
        ts(["pbi"], ["pt3"], T.pt[:, 96:128], T.pbi[:], 7, SHR)
        cp(["pt0", "pt1", "pt2", "pt3"], ["pl"], T.pl[:], T.pt[:])
        fill(["onef"], T.onef[0:1, :], 1.0)
        ts(["nrow", "pl", "ct16"], ["em"], T.em[:], T.nrow[:, 0:16].indirect(T.pl[:, 64:128]), ct(16), EQ)

    def blocked(j, src, side):
        tt([src, "pl", "em"], ["gm%d" % j], T.gm[:, 512 * j:512 * j + 512],
           M[src].indirect(T.pl[:, 32 * side:32 + 32 * side]), T.em[:, 512 * side:512 * side + 512], MUL)
        mm(["b1k", "gm%d" % j], "p3", T.p3[:], T.b1k[:], T.gm[:, 512 * j:512 * j + 512], False, j == 3)

    def idle2():
        mm(["onef", "krow"], "p3", T.p3[:], T.onef[0:1, :], T.krow[0:1, :], True, False)
        ts(["nrow", "ct16"], ["oh"], T.oh[:], T.nrow[:, 0:16], ct(16), EQ, BIG, MUL)
        for k, x in enumerate(("pa1", "pb1")):
            mm([x, "idb"], "q3", T.q3[:], T.idb[:], T.pai[:, 512 * k:512 * k + 512], k == 0, k == 1)
        act(["q3"], ["dall"], T.dall[:], T.q3[:])
        blocked(0, "mf1", 0)
        blocked(1, "fi1", 1)

    def choose(t):
        W, cl = T["w_%d" % t], T["cl%d" % t]
        wo = 16 * (t - 1)
        ko = 4 * (t - 1)
        for r in range(N):
            mm(["b8", "cl%d" % t, "clo%d" % t], "p3", T.p3[:, 0:8], T.b8[:], cl[:, 8 * r:8 * r + 8], False, r == N - 1)
        red(["p3"], ["km%d" % t], T.km[:, ko:ko + 1], T.p3[:, 0:8], OP.max)
        ts(["km%d" % t], ["kn%d" % t], T.km[:, ko + 1:ko + 2], T.km[:, ko:ko + 1], 7, AND)
        ts(["kn%d" % t, "ct14"], ["wl%d" % t], T.wl[:, 2 * t - 2:2 * t - 1], T.km[:, ko + 1:ko + 2], -1.0, MUL, ct(14), ADD)
        ts(["kn%d" % t], ["kq%d" % t], T.kf[:, 1 + t:2 + t], T.km[:, ko + 1:ko + 2], -128.0, MUL)
        cp(["wl%d" % t] + [x % t for x in ("wb%d", "wn%d", "wy%d", "wd%d")], ["wo%d" % t],
           T.wo[:, wo:wo + 16], W[:, 0:40].indirect(T.wl[:, 2 * t - 2:2 * t - 1]))
        w = "wo%d" % t
        mf, mr = "mf%d" % t, "mr%d" % t
        fl = T.fl[:, 8 * t - 8:8 * t]

        def col(j):
            return T.wo[:, wo + j:wo + j + 1]
        ts(["c8", "kq%d" % t], ["fl%d" % t], fl, T.c8[:], T.kf[:, 1 + t:2 + t], ADD)
        for h in (1, 0):
            for j in range(2):
                ts(["q0", w], ["s12%s%d" % ("ab"[j], 64 * h)], T.s12[:, 128 * h + 64 * j:128 * h + 64 * j + 64],
                   T.q0[:, 128 * j + 64 * h:128 * j + 64 * h + 64], col(1 + j), SUB)
        act(["fit%d" % d for d in range(8)] + ["fl%d" % t, w], [mf], M[mf], T.fit[:].indirect(fl), scale=col(3))
        shift([mf], [(M[mf], -SH, M["fi%d" % t], "fi%d" % t, "af%d" % t)])
        for a, b in zip(slots(64, 128, T.rl, "rl"), slots(0, 64, T.rl, "rl")):
            a()
            b()
        for q, h in (("S", 1), ("V", 0)):
            for a, n in ((1024 * h, 768), (1024 * h + 768, 256)):
                look(q, 0, a, a + n, lambda a, b: T.rl[:, a:b], ["rl%d" % (64 * h)], col(0), w)
        for blocks in (range(6), range(6, 8)):
            words("q2", gsrc(0), gname(0), 1, "pk", False, True, blocks)
            words("q1", gsrc(0), gname(0), 0, "pk", False, True, blocks)
        compare("S", "q2", 0, 1)
        compare("V", "q1", 0, 0)
        misses("p0", 0, [] if t == 1 else ["cs1"])
        act(["p0", w], [mr], T[mr][:], T.p0[:, 0:128], ACT.Relu, bias=col(3), scale=-float(t))
        if t == 1:
            shift([mr], [(T[mr][:], SH, M["ri1"], "ri1", "ar1")])
            shift([mr], [(T[mr][:], 2 * SH, M["rj1"], "rj1", "aj1")])
        else:
            send(mr, SH, "ri2", "ar2")
        ts(["km%d" % t], ["ko%d" % t], T.km[:, ko + 2:ko + 3], T.km[:, ko:ko + 1], 3, SHR)
        cp([w], ["yw%d" % t], T.ywo[:, t - 1:t], col(4))
        ts(["ko%d" % t], ["yx%d" % t], T.ywo[:, 1 + t:2 + t], T.km[:, ko + 2:ko + 3], -1.0, ADD)

    put(1024, 1856)
    front(1)
    first_lists(put)
    main(1)
    choices(1)
    idle1()
    choose(1)
    idle2()

    for k, m in enumerate(("fi1", "ri1")):
        mm([m, "idb"], "p1", T.p1[:, 0:128], T.idb[:], M[m], k == 0, k == 1)
    blocked(2, "ri1", 1)
    blocked(3, "rj1", 0)
    for c in range(16):
        act(["p1", "oh"], ["in1_%d" % c], T.in1[:, 128 * c:128 * c + 128], T.p1[:, 0:128], scale=T.oh[:, c:c + 1])
    act(["p1"], ["cov"], T.cov[:], T.p1[:, 0:128])

    def mark(a, b):
        tt(["own%d" % x for x, y in SETS] + XB + ["in1_%d" % c for c in range(a // 128, (b + 127) // 128)], TAB,
           T.tab[:].indirect(T.own[:, a // 16:b // 16]), T.xb[:, a:b], T.in1[:, a:b], ADD)

    mark(0, 128)
    red(["p3"], ["kf"], T.kf[:, 0:1], T.p3[:], OP.min)
    o2 = S2 * rank
    ts(["kf"], ["kl"], T.kl[:, 0:1], T.kf[:, 0:1], 511.0, OP.min)
    ts(["kf"], ["la2b"], T.la2[:, o2 + 3:o2 + 4], T.kf[:, 0:1], 512.0, OP.is_lt)
    cp(["dall", "kl"], ["la2a"], T.la2[:, o2 + 4:o2 + 20], T.dall[:].indirect(T.kl[:, 0:1]))
    gather_all(["la2a", "la2b"], "al2", T.la2[:, o2 + 3:o2 + 5], "la2")
    send("cov", -SH, "cs1", "acs")

    mark(128, 1856)
    front(2)
    first_lists(mark)
    main(2)
    choices(2)
    ts(["cov"], ["c1"], T.c1[:], T.cov[:], 1.0, OP.min)
    choose(2)
    dma("y", "dz", ["yw1", "yw2", "yx1", "yx2"], [], T.yw[:], T.ywo[0:128:16, :])
    tt(["fi2", "c1"], ["ta", "b2a"], T.ta[:], T.fi2[:], T.c1[:], OP.max)
    tt(["ta", "ri2"], ["yo"], T.yo[:], T.ta[:], T.ri2[:], OP.max)
    dma("y", "dy", ["yo"], [], T.yc[:, 0:1024], T.yo[0:128:2, :])
    dma("s", "dy2", ["yo"], [], T.yc[:, 1024:2048], T.yo[1:128:2, :])
    for s, v in cnt.items():
        if max([x for (q, n), x in waited.items() if n == s] + [0]) < v:
            need("y", [(s, v)])
